import numpy as np, ml_dtypes
CORES = [2,6,10,14,18,22,26,30]
N = 8
import mx_ref
BF = ml_dtypes.bfloat16
def gcols(t, e):
    v = np.concatenate([t.reshape(8, 16, -1, 4), np.zeros((8, 16, 1, 4), BF)], axis=2)
    return np.ascontiguousarray(np.stack([v[g][:, e[g]] for g in range(8)])).reshape(128, -1)
def tile(rs):
    return np.stack(rs, axis=2).reshape(128, -1).astype(BF)
def pick(q, e):
    c = np.concatenate([q[0].reshape(128, -1, 4), np.zeros((128, 1, 4), np.uint8)], axis=1); s = np.concatenate([q[1], np.ones((16, 1), np.uint8)], axis=1)
    return (np.ascontiguousarray(c[:, e].reshape(128, -1)), np.ascontiguousarray(s[:, e]))
def join(*qs):
    return (np.concatenate([q[0] for q in qs], axis=1), np.concatenate([q[1] for q in qs], axis=1))
def put(q, e, v):
    c, s = q[0].reshape(128, -1, 4).copy(), q[1].copy(); c[:, e] = v[0].reshape(128, -1, 4); s[:, e] = v[1]
    return (c.reshape(128, -1), s)
def pk(c, s):
    return (np.ascontiguousarray(c), mx_ref.live(s))
def emit(q):
    return q[0], q[1]
def packed(v, rng):
    q = [mx_ref.quantize(np.ascontiguousarray(v[r])) for r in range(N)]
    return np.stack([a for a, b in q]), np.stack([mx_ref.plane(b, rng) for a, b in q])
def values_of_codes():
    e, c = np.zeros((128, 128, 4), np.float32), np.zeros((128, 2, 4), np.uint8)
    e[np.arange(128), np.arange(128), 0] = 1
    c[:127, :, 0] = np.arange(256).reshape(2, 128).T[:127]
    return mx_ref.matmul(mx_ref.quantize(e.reshape(128, 512).astype(BF)), (c.reshape(128, 8), np.full((16, 2), 127, np.uint8))).T.reshape(-1).astype(np.float64)
CODE_VALUE, SCALE_VALUE = values_of_codes(), 2.0 ** (np.arange(256) - 127.0)
def decode(q):
    return (CODE_VALUE[q[0]].reshape(16, 8, -1, 4) * SCALE_VALUE[q[1]][:, None, :, None] + 0.0).reshape(128, -1).astype(np.float32)
def f(rng, *shape):
    return mx_ref.flush((rng.standard_normal(shape, dtype=np.float32) * np.exp2(rng.integers(-2, 3, shape[:-1] + (1,)))).astype(BF))
def wide(rng, *shape, cols=0):
    v = rng.standard_normal(shape, dtype=np.float32) * np.exp2(rng.integers(-12, 13, shape)).astype(np.float32)
    if cols: v *= np.repeat(np.exp2(rng.integers(-cols, cols + 1, shape[:-2] + (1, shape[-1] // 4))) * (rng.random(shape[:-2] + (1, shape[-1] // 4)) > 0.0625), 4, axis=-1).astype(np.float32)
    return mx_ref.flush(v.astype(BF))
C, K, LB = 256, 64, 7
def layer(w, g, t):
    return tile([mx_ref.matmul(pick(w, np.arange(128 * b, 128 * b + 128)), g) * np.float32(0.015625) + t[:, b::4] for b in range(4)])
def numbers_of(rng):
    return {"x": np.array(f(rng, N, 128, 4 * C)), "q": np.array(f(rng, N, 128, 4 * K)), "u": np.array(f(rng, N, 128, 512)), "z": np.array(f(rng, N, 128, 512)), "v": np.array(f(rng, N, 128, 512))}
def weights(rng, w):
    c, p = packed(w, rng)
    return {"wc": c, "ws": p}
def still(rng, k):
    w = np.zeros((N, 128, 4, 128, 4), np.float32)
    i = np.arange(128)
    for b in range(4): w[:, i, b, i, b] = k
    return weights(rng, w.reshape(N, 128, 2048).astype(BF))
def marked(rng, s, size):
    d = numbers_of(rng)
    c = size[:, None, None, None, None]
    m = rng.choice([-1.0, 0.0, 1.0], (N, 8, 8, C, 4))
    m[:, :, :4, :, 0] = 1.125 * s
    m[:, :, 4:, :, 0] = s
    m[..., 3] = 0
    d["x"].reshape(N, 8, 16, C, 4)[:, :, :8] = (m * c).astype(np.float32).astype(BF)
    h = rng.choice([1.0, 1.0, -1.0, 0.0], (N, 8, LB + 7, K))
    h[..., 0] = -1
    h[..., 1] = 1
    h[:, :, :LB, 2] = 1
    h[:, :, LB:, 2] = -1
    h[:, :, :LB, 3] = -1
    h[:, :, LB:, 3] = 1
    h[..., 4] = 0
    m = rng.choice([-1.0, 0.0, 1.0], (N, 8, 16, K, 4))
    m[:, :, :LB + 7, :, 3] = 1.125 * h
    m[..., 0][:, :, (np.arange(LB + 7) + 8) % 16] = h
    d["q"] = (m * c).astype(np.float32).astype(BF).reshape(N, 128, 4 * K)
    u, z = d["u"].reshape(N, 8, 16, 128, 4), d["z"].reshape(N, 8, 16, 128, 4)
    u[:, :, :, ::16] = 0
    z[:, :, :, np.arange(128) % 16 < LB + 7] = 0
    i = np.arange(N)
    plus, minus = (1.125 * size).astype(np.float32).astype(BF), (-1.25 * size).astype(np.float32).astype(BF)
    for g in range(8):
        u[i, g, i % 4, 16 * g, 0] = plus
        u[i, g, 4 + i % 4, 16 * g, 0] = minus
        for e in range(LB + 7):
            z[i, g, e, 16 * g + e, 3] = plus
            z[i, g, (e + 8) % 16, 16 * g + e, 0] = minus
    return d
def setup_inputs(rng):
    return {**numbers_of(rng), **weights(rng, f(rng, N, 128, 2048))}
def setup_inputs_near(rng):
    size = np.where(rng.permutation(N) < N // 2, 2.0 ** -30, 1.0)
    s = rng.choice([1.0, 1.0, -1.0, 0.0], (N, 8, 4, C))
    a, i = (1 << LB) - 1, np.arange(N)
    s[..., a] = -1
    s[i, :, i % 4, a] = 1
    s[..., a + 126] = -1
    s[..., a + 127] = 1
    return {**marked(rng, s, size), **still(rng, 64)}
def setup_inputs_flat(rng):
    s = np.zeros((N, 8, 4, C))
    for r in range(N):
        for i in range(4):
            k = rng.permutation(8) % 6
            for g in range(8):
                a = s[r, g, i]
                if k[g] == 5: a[:] = rng.choice([1.0, -1.0, 0.0], C)
                elif k[g] != 2:
                    a[:] = 1.0 if k[g] in (0, 4) else -1.0
                    if k[g] > 2: a[int(rng.integers(C))] *= -1.0
    d = marked(rng, s, np.ones(N))
    d["x"][int(rng.integers(N))] = 0
    return {**d, **still(rng, 64)}
def setup_inputs_huge(rng):
    d = numbers_of(rng)
    h = (np.arange(N) + int(rng.integers(4))) % 4
    c = rng.choice([-1.0, 1.0], (N, 8, C))
    c[:, :, 0] = 1
    c[:, :, 1] = -1
    c[h == 0] = c[h == 0][:, :1]
    c[h > 1] = 1
    x = 2.0 ** 30 * (0.65 + 0.1 * rng.random((N, 8, 16, C, 4))) * c[:, :, None, :, None]
    k = rng.choice([-1.0, 1.0], (N, 128, K, 4))
    k[:, :, ::2] = rng.choice([-1.0, 1.0], (N, 1, K // 2, 1))
    q = 2.0 ** 29 * (0.75 + 0.25 * rng.random((N, 128, K, 4))) * k
    s = rng.choice([-1.0, 1.0], (N, 8))
    s[h == 0] = -np.roll(s, -1, axis=0)[h == 0]
    s = np.maximum(np.eye(8), (h == 0)[:, None, None]) * s[:, None, :]
    u = d["u"].reshape(N, 8, 16, 128, 4)
    u[:, :, :, ::16] = (2.0 ** 30 * (0.9 + 0.1 * rng.random((N, 8, 16, 8, 4))) * s[:, :, None, :, None] + 0.0).astype(np.float32).astype(BF)
    z = 2.0 ** 30 * (0.75 + 0.25 * rng.random((N, 128, 128, 4))) * rng.choice([-1.0, 1.0], (N, 1, 128, 1))
    d["x"] = x.astype(np.float32).astype(BF).reshape(N, 128, 4 * C)
    d["q"] = q.astype(np.float32).astype(BF).reshape(N, 128, 4 * K)
    d["z"] = z.astype(np.float32).astype(BF).reshape(N, 128, 512)
    return {**d, **still(rng, 1)}
def setup_inputs_spread(rng):
    d = setup_inputs(rng)
    d["x"] = wide(rng, N, 128, 4 * C, cols=6)
    d["q"] = wide(rng, N, 128, 4 * K, cols=6)
    return d
def check_inputs(d):
    b = []
    for k in ("x", "q", "u", "z", "v"):
        a = np.abs(d[k].astype(np.float32))
        if not (np.isfinite(a).all() and ((a == 0) | (a >= 2.0 ** -30) & (a <= 2.0 ** 30)).all()): b.append("a value of " + k)
    return b
def reference(x, q, u, z, v, wc, ws):
    qu = [mx_ref.quantize(u[r]) for r in range(N)]
    lay = [pk(wc[r], ws[r]) for r in range(N)]
    y, ol = np.zeros((N, 128, K), np.float32), np.zeros((N, 8, K), np.float32)
    oc, osc = np.zeros((N, 128, 4 * K), np.uint8), np.zeros((N, 16, K), np.uint8)
    weight = (1 << np.arange(7))[:, None]
    for r in range(N):
        t, at, key = x[r], np.tile(np.arange(C), (8, 1)), np.zeros((8, C), np.int64)
        level, path = [], []
        for l in range(3):
            h = (r + l) % N
            if l:
                g = mx_ref.quantize(gcols(t, o))
                t = layer(lay[h], g, decode(g))
                at = np.take_along_axis(np.argsort(o, axis=1), at, axis=1)
            bit = mx_ref.matmul(qu[h], mx_ref.quantize(t))[::16] > 0
            o = np.argsort(bit, axis=1, kind="stable")
            key = 2 * key + np.take_along_axis(bit, at, axis=1)
            level.append(t)
            path.append(at)
        e = mx_ref.matmul(mx_ref.quantize(z[r]), mx_ref.quantize(q[r])).reshape(8, 16, K) > 0
        lo = np.sum(e[:, :LB] * weight[:LB], axis=1)
        k = np.sum(e[:, LB:LB + 7] * weight, axis=1)
        i = np.argsort(key[np.arange(8)[:, None, None], lo[:, :, None] + np.arange(128)], axis=2, kind="stable")
        a = lo + np.take_along_axis(i, k[:, :, None], axis=2)[:, :, 0]
        part = [gcols(level[l], np.take_along_axis(path[l], a, axis=1)) for l in range(3)]
        first = ((decode(mx_ref.quantize(part[2])) + decode(mx_ref.quantize(part[1]))) * np.float32(0.5)).astype(BF)
        both = ((decode(mx_ref.quantize(first)) + part[0].astype(np.float32)) * np.float32(0.5)).astype(BF)
        last = mx_ref.quantize(layer(lay[r], mx_ref.quantize(both), q[r].astype(np.float32)))
        y[r] = mx_ref.matmul(mx_ref.quantize(v[r]), last)
        ol[r] = a
        oc[r], osc[r] = emit(last)
    return {"y": y, "ol": ol, "oc": oc, "osc": osc}

@@ -1,0 +1,429 @@
+from concourse.mybir import dt, AluOpType, ActivationFunctionType
+
+X4, U8, BF, F32, U16 = "float8_e4m3fn_x4", "uint8", "bfloat16", "float32", "uint16"
+SCRATCH = {"ps": ("psum", [128, 4096], F32)}
+for _n, _w in (("u", 128), ("ur", 128), ("t0", 256), ("t1", 256), ("t2", 256), ("f0", 256), ("f1", 256),
+               ("l1", 256), ("l2", 256), ("w", 512), ("e64", 512), ("e05", 512), ("z", 128), ("qd", 128),
+               ("v", 128), ("b1", 128), ("lb", 192), ("b", 128), ("xx", 128)):
+    SCRATCH[_n + "_q"] = ("sbuf", [128, _w], X4)
+    SCRATCH[_n + "_s"] = ("sbuf", [128, _w], U8)
+for _n, _w in (("ub", 512), ("zb", 512), ("vb", 512), ("t0", 1024), ("t1", 1024), ("t2", 1024), ("tp0", 1024),
+               ("tp1", 1024), ("f0", 1024), ("f1", 1024), ("e64", 2048), ("e05", 2048), ("c64", 128), ("idn", 128),
+               ("qd", 512), ("q64", 256), ("b1p", 1024), ("b1", 512), ("x2", 1024), ("a0h", 256),
+               ("bt", 512), ("xp", 256), ("xt", 512), ("zt", 512),
+               ("ones", 256), ("tmod", 256), ("hold", 256), ("diag", 128), ("k16", 128), ("k32", 128), ("kh", 160),
+               ("jrow", 256), ("bit", 256), ("rr", 272), ("hi", 256), ("he", 256), ("ob0", 288), ("ob1", 288),
+               ("ot", 544), ("eb", 96), ("ebt", 160), ("esc", 160), ("gm", 128), ("s16", 128), ("s32", 128),
+               ("orig", 256), ("arr", 512), ("cmp", 1536), ("cs", 768), ("junk", 512), ("pos", 8), ("nd", 8)):
+    SCRATCH[_n] = ("sbuf", [128, _w], BF)
+for _n, _w in (("j16", 16), ("jw", 16), ("crow", 96), ("ccol", 96), ("d0", 32), ("d1", 32), ("pp", 32), ("lk", 16),
+               ("stf", 16), ("g0", 32), ("g1", 32), ("gg", 32), ("zc", 4), ("h0", 8), ("h1", 8),
+               ("pre", 12), ("acc", 4), ("km", 8), ("kml", 8), ("arow", 64), ("ysb", 64)):
+    SCRATCH[_n] = ("sbuf", [128, _w], F32)
+for _n, _w in (("urep", 8), ("sel", 8), ("esel", 8), ("pw", 16), ("ow0", 16), ("ow1", 16), ("st0", 16), ("so0", 16),
+               ("so1", 16), ("st1", 16), ("st2", 16), ("o1l", 16), ("o4", 64), ("j2", 8), ("j2l", 8)):
+    SCRATCH[_n] = ("sbuf", [128, _w], U16)
+SEMAPHORES = ["cv", "cs", "ct", "cg", "sent", "out",
+              "ld_u", "ld_xa", "ld_xb", "ld_q", "ld_z", "ld_wc", "ld_ws", "ld_v",
+              "a1", "s1", "b1", "a2", "s2", "b2", "km", "st1", "st2", "o1", "j2", "bq", "bs"]
+A = AluOpType
+ACT = ActivationFunctionType
+
+
+def rank_program(g, core, T, topo):
+    rank = T.rank_of(core)
+    if rank is None:
+        return
+    cores = list(T.cores)
+    n = len(cores)
+    nxt, prv = cores[(rank + 1) % n], cores[(rank - 1) % n]
+    back2, fwd2 = cores[(rank - 2) % n], cores[(rank + 2) % n]
+    V, S, P = g.vector, g.scalar, g.tensor
+    queues = {"v": V, "s": S, "t": P, "g": g, "y": g.sync}
+    counter = {"v": "cv", "s": "cs", "t": "ct", "g": "cg"}
+    seen = {k: {} for k in queues}
+    total = {}
+    writer, readers = {}, {}
+
+    def need(q, tok):
+        sem, val, clock = tok[0], tok[1], tok[2]
+        if seen[q].get(sem, 0) >= val:
+            return
+        queues[q].wait_ge(T.sem[sem], val)
+        seen[q][sem] = val
+        for k in clock:
+            if seen[q].get(k, 0) < clock[k]:
+                seen[q][k] = clock[k]
+
+    def before(q, r, w):
+        toks = [writer[k] for k in list(r) + list(w) if k in writer]
+        for k in w:
+            toks += readers.get(k, [])
+        for k in r:
+            if k.startswith("bank"):
+                toks += [t for t in readers.get(k, []) if t[3] != q]
+        for t in sorted(toks, key=lambda t: -t[1]):
+            need(q, t)
+
+    def after(tok, r, w):
+        for k in r:
+            readers.setdefault(k, []).append(tok)
+        for k in w:
+            writer[k] = tok
+            readers[k] = []
+
+    def op(q, call, r=(), w=(), sem=None):
+        before(q, r, w)
+        name, inc = (counter[q], 1) if sem is None else (sem, 16)
+        call().then_inc(T.sem[name], inc)
+        total[name] = total.get(name, 0) + inc
+        after((name, total[name], dict(seen[q]), q), r, w)
+
+    def arrives(sem, src, key):
+        total[sem] = len(topo.engines(src, core))
+        writer[key] = (sem, total[sem], {}, "r")
+
+    def send(dst, out, src, sem, r):
+        before("g", r, ())
+        rid, pid, _ = topo.addr(dst)
+        g.remote_dma(out, src, T.sem[sem], T.sem.sent, pid, rid, topo.mask(core, dst))
+        total["sent"] = total.get("sent", 0) + len(topo.engines(core, dst))
+
+    def ts(out, in0, s1, s2, o0, o1, r, w):
+        if o1 is None:
+            op("v", lambda: V.tensor_scalar(out, in0, s1, None, o0), r, w)
+        else:
+            op("v", lambda: V.tensor_scalar(out, in0, s1, s2, o0, o1), r, w)
+
+    def tt(out, a, b, o, r, w):
+        op("v", lambda: V.tensor_tensor(out, a, b, o), r, w)
+
+    def cp(out, a, r, w):
+        op("v", lambda: V.tensor_copy(out, a), r, w)
+
+    def scan(out, a, b, init, o0, o1, r, w):
+        op("v", lambda: V.tensor_tensor_scan(out, a, b, init, o0, o1), r, w)
+
+    def turn(out, a, r, w):
+        op("v", lambda: V.transpose(out, a), r, w)
+
+    def fill(ap, c, w):
+        op("v", lambda: V.memset(ap, c), (), w)
+
+    def act(out, a, r, w, scale=1.0):
+        if scale == 1.0:
+            op("s", lambda: S.activation(out, a, ACT.Copy), r, w)
+        else:
+            op("s", lambda: S.activation(out, a, ACT.Copy, scale=scale), r, w)
+
+    def quant(name, a, b, src, r, w):
+        op("v", lambda: V.quantize_mx(T[name + "_q"][:, a:b], T[name + "_s"][:, a:b], src), r, w)
+
+    def bank(k, m):
+        return T.ps[:, 512 * k:512 * k + m]
+
+    def mm(k, terms, r):
+        before("t", r, ["bank%d" % k])
+        for i, (ln, la, rn, ra, rb) in enumerate(terms):
+            ins = P.matmul_mx(bank(k, rb - ra), T[ln + "_q"][:, la:la + 128], T[ln + "_s"][:, la:la + 128],
+                              T[rn + "_q"][:, ra:rb], T[rn + "_s"][:, ra:rb], i == 0, i == len(terms) - 1)
+        ins.then_inc(T.sem.ct, 1)
+        total["ct"] = total.get("ct", 0) + 1
+        after(("ct", total["ct"], dict(seen["t"]), "t"), r, ["bank%d" % k])
+
+    def iota(out, pattern, base, w):
+        op("g", lambda: g.iota(out, pattern, base, 0, allow_small_or_imprecise_dtypes=True), (), w)
+
+    u8 = lambda v: v.bitcast(dt.uint8)
+    u32 = lambda v: v.bitcast(dt.uint32)
+
+    for lv in (1, 2):
+        for s, k in (("a", "lqa"), ("s", "ls"), ("b", "lqb")):
+            arrives("%s%d" % (s, lv), prv, "%s%d" % (k, lv))
+    for s, k in (("km", "kml"), ("st1", "st1"), ("st2", "st2")):
+        arrives(s, prv, k)
+    arrives("o1", nxt, "o1l")
+    for s in ("j2", "bq", "bs"):
+        arrives(s, fwd2, "in_" + s)
+
+    op("y", lambda: g.sync.dma_start(T.qd[:, 0:256], T.q[:]), (), ["qb"], "ld_q")
+    op("s", lambda: S.dma_start(T.zb[:], T.z[:]), (), ["zb"], "ld_z")
+    op("y", lambda: g.sync.dma_start(T.ub[:], T.u[:]), (), ["ub"], "ld_u")
+    op("s", lambda: S.dma_start(T.t0[:, 0:512], T.x[:, 0:512]), (), ["t0a"], "ld_xa")
+    op("y", lambda: g.sync.dma_start(T.t0[:, 512:1024], T.x[:, 512:1024]), (), ["t0b"], "ld_xb")
+    op("y", lambda: g.sync.dma_start(u8(T.w_q[:]), T.wc[:]), (), ["wq"], "ld_wc")
+    op("y", lambda: g.sync.dma_start(T.w_s[:], T.ws[:]), (), ["ws"], "ld_ws")
+    op("y", lambda: g.sync.dma_start(T.vb[:], T.v[:]), (), ["vb"], "ld_v")
+
+    fill(T.crow[:, 64:96], 0.0, ["crow3", "crow4"])
+    fill(T.c64[:], 64.0, ["c64"])
+    iota(T.j16[:], [[16, 16]], 0, ["j16"])
+    iota(T.crow[:, 0:32], [[0, 2], [1, 16]], 0, ["crow0"])
+    iota(T.crow[:, 32:48], [[32, 8], [-256, 2]], 288, ["crow1"])
+    iota(T.crow[:, 48:64], [[32, 8], [288, 2]], 16, ["crow2"])
+    iota(T.crow[:, 64:72], [[7, 2], [32, 2], [-64, 2]], 102, ["crow3"])
+    iota(T.crow[:, 80:88], [[7, 2], [32, 2], [96, 2]], 22, ["crow4"])
+    iota(T.tmod[:], [[0, 16], [1, 16]], 0, ["tmod"])
+    op("g", lambda: g.affine_select(T.idn[:], T.c64[:], [[-1, 128]], A.is_equal, 0.0, 0, 1), ["c64"], ["idn"])
+    iota(T.jrow[:], [[1, 256]], 0, ["jrow"])
+    fill(T.zt[:], 0.0, ["zt"])
+    for b in range(4):
+        act(T.e64[:, 512 * b:512 * b + 512], T.zt[:], ["zt"], ["e64_%d" % b])
+    fill(T.qd[:, 256:512], 0.0, ["qdz"])
+    fill(T.kh[:], 0.5, ["kh"])
+    fill(T.eb[:], 0.0, ["eb"])
+    fill(T.ones[:], 1.0, ["ones"])
+    fill(T.kh[:, 0:160:16], 0.0, ["kh"])
+    fill(T.rr[:, 0:1], 0.0, ["rr0"])
+    fill(T.kh[:, 7:160:16], 0.0, ["kh"])
+    cp(T.urep[:], T.j16[:, 0:8], ["j16"], ["urep"])
+    fill(T.d0[:], 0.0, ["d0"])
+    fill(T.ob0[:], 0.0, ["ob0"])
+    fill(T.ob1[:], 0.0, ["ob1"])
+    for name in ("b1", "bt", "xt"):
+        fill(T[name][:, 256:512], 0.0, [name + "z"])
+    turn(T.ccol[:], T.crow[:], ["crow%d" % i for i in range(5)], ["ccol"])
+    quant("lb", 64, 192, T.zt[:], ["zt"], ["lbz"])
+    pm = T.ccol[:, 0:1]
+    cp(T.esel[:, 0:1], T.ccol[:, 64:65], ["ccol"], ["esel"])
+    cp(T.sel[:, 0:1], T.ccol[:, 32:33], ["ccol"], ["sel"])
+    ts(T.jw[:], T.j16[:], pm, None, A.add, None, ["j16", "ccol"], ["jw"])
+
+    quant("qd", 0, 128, T.qd[:], ["qb", "qdz"], ["qdq"])
+    quant("z", 0, 128, T.zb[:], ["zb"], ["zq"])
+    mm(1, [("z", 0, "qd", 0, 128)], ["zq", "qdq"])
+    ts(T.hold[:], T.tmod[:], pm, 512.0, A.is_equal, A.mult, ["tmod", "ccol"], ["hold"])
+    ts(T.eb[:, 16:80], bank(1, 64), 0.0, None, A.is_gt, None, ["bank1"], ["eb"])
+    turn(T.ebt[:, 0:96], T.eb[:, 0:96], ["eb"], ["ebta"])
+    turn(T.ebt[:, 96:160], T.eb[:, 16:80], ["eb"], ["ebtb"])
+    quant("u", 0, 128, T.ub[:], ["ub"], ["uq"])
+    act(T.ur_s[:], T.u_s[:].indirect(T.urep[:]), ["uq", "urep"], ["urs"])
+    scan(T.esc[:], T.kh[:], T.ebt[:], 0.0, A.mult, A.add, ["kh", "ebta", "ebtb"], ["esc"])
+    cp(u32(T.ur_q[:]), u32(T.u_q[:]).indirect(T.urep[:]), ["uq", "urep"], ["urq"])
+    ts(T.lk[:], T.esc[:].indirect(T.esel[:, 0:1]), 64.0, None, A.mult, None, ["esc", "esel"], ["lk"])
+    lo, kk = T.lk[:, 0:4], T.lk[:, 4:8]
+    E64 = ["e64_%d" % b for b in range(4)]
+    for b in range(4):
+        act(T.e64[:, 512 * b + b:512 * b + 512:4], T.idn[:], ["idn"], ["e64_%d" % b])
+
+    def scores(lv, h):
+        mm(4 * h, [("ur", 0, "t%d" % lv, 128 * h, 128 * h + 128)], ["urq", "urs", "tq%d%d" % (lv, h)])
+
+    def bits(h):
+        a = 128 * h
+        ts(T.bit[:, a:a + 128], bank(4 * h, 128), 0.0, None, A.is_gt, None, ["bank%d" % (4 * h)], ["bit%d" % h])
+        scan(T.rr[:, 1 + a:129 + a], T.ones[:, 0:128], T.bit[:, a:a + 128], T.rr[:, a:a + 1], A.mult, A.add,
+             ["ones", "bit%d" % h, "rr0", "rra"] if h else ["ones", "bit0", "rr0"], ["rrb" if h else "rra"])
+
+    RR = ["rr0", "rra", "rrb"]
+    n1 = T.rr[:, 256:257]
+
+    def order_and_send(lv, spare):
+        ob, ow, tp, f = T["ob%d" % lv], T["ow%d" % lv], T["tp%d" % lv], T["f%d" % lv]
+        obk, owk = "ob%d" % lv, "ow%d" % lv
+
+        def gap():
+            if spare:
+                spare.pop(0)()
+
+        scan(T.hi[:], T.hold[:], T.rr[:, 1:257], 0.0, A.add, A.min, ["hold"] + RR, ["hi"])
+        scan(T.he[:], T.hold[:], T.rr[:, 0:256], 0.0, A.add, A.min, ["hold"] + RR, ["he"])
+        inc, exc = T.hi[:, 15:256:16], T.he[:, 15:256:16]
+        tt(T.d1[:, 1:32:2], T.jw[:], inc, A.subtract, ["jw", "hi"], ["d1b"])
+        ts(T.d1[:, 0:32:2], exc, n1, 256.0, A.subtract, A.add, ["he", "rrb"], ["d1a"])
+        tt(T.d0[:, 1:32:2], inc, exc, A.subtract, ["hi", "he"], ["d0"])
+        gap()
+        scan(T.pp[:], T.d0[:], T.d1[:], 0.0, A.mult, A.max, ["d0", "d1a", "d1b"], ["pp"])
+        gap()
+        cp(T.pw[:], T.pp[:, 1:32:2], ["pp"], ["pw"])
+        gap()
+        cp(ob[:, 16:272].indirect(T.pw[:]), T.jrow[:], ["pw", "jrow"], [obk])
+        gap()
+        turn(T.ot[:, 0:288], ob[:, 0:288], [obk], ["ota"])
+        turn(T.ot[:, 288:544], ob[:, 16:272], [obk], ["otb"])
+        gap()
+        cp(ow[:], T.ot[:].indirect(T.sel[:, 0:1]), ["ota", "otb", "sel"], [owk])
+        gap()
+        fq, fs, lq, ls = T["f%d_q" % lv], T["f%d_s" % lv], T["l%d_q" % (lv + 1)], T["l%d_s" % (lv + 1)]
+        for h in range(2):
+            for b in (2, 3, 0, 1):
+                (cp if b < 2 else act)(f[:, 512 * h + b:512 * h + 512:4],
+                                       tp[:, 256 * b:256 * b + 256].indirect(ow[:, 8 * h:8 * h + 8]),
+                                       [owk, "tp%d%d" % (lv, b)], ["f%d%d%d" % (lv, h, b)])
+            quant("f%d" % lv, 128 * h, 128 * h + 128, f[:, 512 * h:512 * h + 512],
+                  ["f%d%d%d" % (lv, h, b) for b in range(4)], ["fq%d%d" % (lv, h)])
+        send(nxt, u8(lq[:, 0:128]), u8(fq[:, 0:128]), "a%d" % (lv + 1), ["fq%d0" % lv])
+        send(nxt, ls[:], fs[:], "s%d" % (lv + 1), ["fq%d0" % lv, "fq%d1" % lv])
+        send(nxt, u8(lq[:, 128:256]), u8(fq[:, 128:256]), "b%d" % (lv + 1), ["fq%d1" % lv])
+        while spare:
+            gap()
+
+    def zeros_total():
+        ts(T.zc[:, 0:1], n1, -1.0, 256.0, A.mult, A.add, ["rrb"], ["zc"])
+
+    def keep_rest():
+        cp(T.g1[:, 24:32:2], T.stf[:, 12:16], ["stf"], ["g13"])
+
+    def picked(lst, key):
+        tt(T.gm[:], T.rr[:, 0:257].indirect(lst[:, 0:8]), T.diag[:], A.mult, RR + [key, "diag"], ["gm"])
+
+    def counts():
+        scan(T.s32[:], T.k32[:], T.gm[:], 0.0, A.mult, A.add, ["k32", "gm"], ["s32"])
+        scan(T.s16[:], T.k16[:], T.gm[:], 0.0, A.mult, A.add, ["k16", "gm"], ["s16"])
+
+    def step(lst, key, out, okey, first):
+        picked(lst, key)
+        counts()
+        ab, a, b, m = T.s16[:, 15:128:16], T.s16[:, 15:128:32], T.s16[:, 31:128:32], T.s32[:, 31:128:32]
+        lk, kap = T.stf[:, 8:12], T.stf[:, 12:16]
+        for i, view in enumerate((T.g0[:, 1:16:4], T.g0[:, 3:16:4], T.g0[:, 17:24:2], T.g0[:, 25:32:2])):
+            tt(view, m, T.pre[:, 0:4] if first else kap, A.is_ge, ["s32", "stf", "pre0", "g0z"], ["g0%d" % i])
+        if not first:
+            tt(T.pre[:, 8:12], b, kap, A.subtract, ["stf", "s16"], ["pre2"])
+        tt(T.g1[:, 1:16:2], T.stf[:, 0:8], ab, A.subtract, ["stf", "s16"], ["g10"])
+        tt(T.g1[:, 17:24:2], lk, a, A.subtract, ["stf", "s16"], ["g11"])
+        tt(T.g1[:, 25:32:2], kap, m, A.subtract, ["stf", "s32"], ["g12"])
+        ts(T.g1[:, 0:16:2], ab, T.zc[:, 0:1], None, A.add, None, ["zc", "s16"], ["g14"])
+        ts(T.g1[:, 16:24:2], b if first else T.pre[:, 8:12], T.zc[:, 0:1], None, A.add, None,
+           ["zc", "s16", "pre2"], ["g15"])
+        scan(T.gg[:], T.g0[:], T.g1[:], 0.0, A.mult, A.max,
+             ["g0%d" % i for i in range(4)] + ["g1%d" % i for i in range(6)], ["gg"])
+        cp(out[:], T.gg[:, 1:32:2], ["gg"], [okey])
+
+    def layer(lv):
+        t, ln = T["t%d" % lv], "l%d" % lv
+        for h in range(2):
+            for b in (2, 0, 3, 1):
+                mm(4 * h + b, [("w", 128 * b, ln, 128 * h, 128 * h + 128), ("e64", 128 * b, ln, 128 * h, 128 * h + 128)],
+                   ["wq", "ws", "e64q", "ls%d" % lv, "lq%s%d" % ("ab"[h], lv)])
+        for h in range(2):
+            for b in (2, 0, 3, 1):
+                view, k = t[:, 512 * h + b:512 * h + 512:4], 4 * h + b
+                if b < 2:
+                    ts(view, bank(k, 128), 0.015625, None, A.mult, None, ["bank%d" % k], ["t%d%d%d" % (lv, h, b)])
+                else:
+                    act(view, bank(k, 128), ["bank%d" % k], ["t%d%d%d" % (lv, h, b)], 0.015625)
+            quant("t%d" % lv, 128 * h, 128 * h + 128, t[:, 512 * h:512 * h + 512],
+                  ["t%d%d%d" % (lv, h, b) for b in range(4)], ["tq%d%d" % (lv, h)])
+            scores(lv, h)
+
+    quant("t0", 0, 128, T.t0[:, 0:512], ["t0a"], ["tq00"])
+    scores(0, 0)
+    ts(T.km[:, 0:4], kk, -128.0, None, A.add, None, ["lk"], ["kma"])
+    ts(T.km[:, 4:8], kk, -1.0, None, A.mult, None, ["lk"], ["km"])
+    send(nxt, T.kml[:], T.km[:], "km", ["km", "kma"])
+    bits(0)
+    quant("t0", 128, 256, T.t0[:, 512:1024], ["t0b"], ["tq01"])
+    scores(0, 1)
+    for b in range(4):
+        act(T.tp0[:, 256 * b:256 * b + 256], T.t0[:, b:1024:4], ["t0a", "t0b"], ["tp0%d" % b])
+    bits(1)
+    order_and_send(0, [
+        lambda: ts(T.k32[:], T.tmod[:, 0:128], 1.0, None, A.min, None, ["tmod"], ["k32"]),
+        lambda: ts(T.diag[:], T.tmod[:, 0:128], pm, None, A.is_equal, None, ["tmod", "ccol"], ["diag"]),
+        lambda: ts(T.k16[:], T.tmod[:, 0:128], 1.0, None, A.min, None, ["tmod"], ["k16"]),
+        lambda: fill(T.k32[:, 16:128:32], -1.0, ["k32"]),
+        lambda: fill(T.g0[:], 0.0, ["g0z"]),
+        zeros_total])
+
+    quant("e64", 0, 512, T.e64[:], E64, ["e64q"])
+    act(T.q64[:], T.qd[:, 0:256], ["qb"], ["q64"], 64.0)
+    act(T.e05[:], T.e64[:], E64, ["e05"], 0.0078125)
+    cp(T.st0[:, 0:8:2], lo, ["lk"], ["st0a"])
+    ts(T.st0[:, 1:8:2], lo, 128.0, None, A.add, None, ["lk"], ["st0"])
+    cp(T.stf[:, 0:8:2], lo, ["lk"], ["stfa"])
+    ts(T.stf[:, 1:8:2], lo, 128.0, None, A.add, None, ["lk"], ["stfb"])
+    ts(T.stf[:, 8:12], lo, 128.0, None, A.add, None, ["lk"], ["stfc"])
+    fill(T.stf[:, 12:16], 128.0, ["stf"])
+    ts(T.pre[:, 0:4], kk, -1.0, 128.0, A.mult, A.add, ["lk"], ["pre0"])
+    keep_rest()
+    step(T.st0, "st0", T.so0, "so0", True)
+    send(nxt, T.st1[:], T.so0[:], "st1", ["so0"])
+
+    layer(1)
+    for b in range(4):
+        act(T.tp1[:, 256 * b:256 * b + 256], T.t1[:, b:1024:4], ["t10%d" % b, "t11%d" % b], ["tp1%d" % b])
+    bits(0)
+    bits(1)
+    order_and_send(1, [
+        zeros_total,
+        lambda: fill(T.h0[:], 0.0, ["h0"]),
+        lambda: cp(T.stf[:], T.st1[:], ["st1"], ["stf"]),
+        lambda: tt(T.stf[:, 8:16], T.stf[:, 8:16], T.kml[:], A.add, ["stf", "kml"], ["stf"]),
+        keep_rest])
+    step(T.st1, "st1", T.so1, "so1", False)
+    send(nxt, T.st2[:], T.so1[:], "st2", ["so1"])
+    send(prv, T.o1l[:], T.ow1[:], "o1", ["ow1"])
+    quant("e05", 0, 512, T.e05[:], ["e05"], ["e05q"])
+    quant("v", 0, 128, T.vb[:], ["vb"], ["vq"])
+
+    layer(2)
+    mixed = (1, 2, 3, 5)
+    for b in range(4):
+        mm(mixed[b], [("e64", 128 * b, "t2", 0, 256), ("e64", 128 * b, "l2", 0, 256)],
+           ["e64q", "tq20", "tq21", "ls2", "lqa2", "lqb2"])
+    for b in range(4):
+        act(T.b1p[:, 256 * b:256 * b + 256], bank(mixed[b], 256), ["bank%d" % mixed[b]], ["b1p%d" % b], 0.0078125)
+    bits(0)
+    bits(1)
+    scan(T.arr[:, 0:256], T.ones[:], T.bit[:], 0.0, A.add, A.subtract, ["ones", "bit0", "bit1"], ["arra"])
+    picked(T.st2, "st2")
+    cp(T.stf[:, 8:16], T.st2[:, 8:16], ["st2"], ["stf"])
+    counts()
+    ts(T.zc[:], T.stf[:, 12:16], n1, -256.0, A.add, A.add, ["stf", "rrb"], ["zc"])
+    tt(T.h0[:, 1:8:2], T.s32[:, 31:128:32], T.stf[:, 12:16], A.is_ge, ["s32", "stf"], ["h0"])
+    tt(T.h1[:, 1:8:2], T.stf[:, 8:12], T.s16[:, 15:128:32], A.subtract, ["stf", "s16"], ["h1a"])
+    tt(T.h1[:, 0:8:2], T.s16[:, 31:128:32], T.zc[:], A.subtract, ["zc", "s16"], ["h1b"])
+    ts(T.arr[:, 256:512], T.rr[:, 1:257], n1, 256.0, A.subtract, A.add, RR, ["arrb"])
+    scan(T.pos[:], T.h0[:], T.h1[:], 0.0, A.mult, A.max, ["h0", "h1a", "h1b"], ["pos"])
+    ts(T.nd[:, 0:4], T.h0[:, 1:8:2], -256.0, None, A.mult, None, ["h0"], ["nda"])
+    ts(T.acc[:, 1:2], T.pos[:, 7:8], 0.5, None, A.add, None, ["pos"], ["posh"])
+    op("s", lambda: S.activation(T.junk[:], T.arr[:], ACT.Sign, bias=T.acc[:, 1:2], scale=-1.0,
+                                 accum_out=T.acc[:, 0:1]), ["arra", "arrb", "posh"], ["acc"])
+    for c in range(3):
+        ts(T.cmp[:, 512 * c:512 * c + 512], T.arr[:], T.pos[:, 2 * c + 1:2 * c + 2], None, A.is_le, None,
+           ["arra", "arrb", "pos"], ["cmp%d" % c])
+    ts(T.nd[:, 4:8], T.h0[:, 1:8:2], -256.0, 256.0, A.mult, A.add, ["h0"], ["ndb"])
+    for c in range(3):
+        scan(T.cs[:, 256 * c:256 * c + 256], T.cmp[:, 512 * c:512 * c + 256], T.cmp[:, 512 * c + 256:512 * c + 512],
+             T.nd[:, c:c + 1], A.add, A.add, ["cmp%d" % c, "nda"], ["cs%d" % c])
+    ts(T.j2[:, 3:4], T.acc[:, 0:1], 0.5, T.nd[:, 7:8], A.mult, A.add, ["acc", "ndb"], ["j2a"])
+    cp(T.j2[:, 0:3], T.cs[:, 255:768:256], ["cs0", "cs1", "cs2"], ["j2"])
+    send(back2, T.j2l[:, 0:4], T.j2[:, 0:4], "j2", ["j2", "j2a"])
+    for b in (2, 3, 0, 1):
+        (cp if b < 2 else act)(T.b1[:, b:256:4], T.b1p[:, 256 * b:256 * b + 256].indirect(T.j2[:, 0:4]),
+                               ["j2", "j2a", "b1p%d" % b], ["b1%d" % b])
+    quant("b1", 0, 128, T.b1[:], ["b1z"] + ["b1%d" % b for b in range(4)], ["b1q"])
+    send(back2, u8(T.lb_q[:, 0:64]), u8(T.b1_q[:, 0:64]), "bq", ["b1q"])
+    send(back2, T.lb_s[:, 0:64], T.b1_s[:, 0:64], "bs", ["b1q"])
+
+    F0 = ["f0%d%d" % (h, b) for h in range(2) for b in range(4)]
+    for t in (2, 3, 0, 1):
+        ts(T.o4[:, 16 * t:16 * t + 16], T.o1l[:], 4.0, float(t), A.mult, A.add, ["o1l"], ["o4%d" % t])
+    act(T.x2[:, 512:1024], T.f0[:].indirect(T.o4[:, 32:64]), F0 + ["o42", "o43"], ["x2b"], 0.5)
+    ts(T.x2[:, 0:512], T.f0[:].indirect(T.o4[:, 0:32]), 0.5, None, A.mult, None, F0 + ["o40", "o41"], ["x2a"])
+    act(T.orig[:], T.ob0[:, 16:272].indirect(T.o1l[:]), ["ob0", "o1l"], ["orig"])
+    for b in (2, 3, 0, 1):
+        (cp if b < 2 else act)(T.a0h[:, 64 * b:64 * b + 64], T.x2[:, 256 * b:256 * b + 256].indirect(T.j2l[:, 0:4]),
+                               ["in_j2", "x2" + "ab"[b // 2]], ["a0h%d" % b])
+    act(T.arow[:], T.orig[:].indirect(T.j2l[:, 0:4]), ["in_j2", "orig"], ["arow"])
+    op("y", lambda: g.sync.dma_start(T.ol[:], T.arow[0:128:16, :]), ["arow"], (), "out")
+    for b in range(4):
+        mm(b, [("e05", 128 * b, "lb", 0, 128)], ["e05q", "lbz", "in_bq", "in_bs"])
+    for b in range(4):
+        tt(T.bt[:, b:256:4], bank(b, 64), T.a0h[:, 64 * b:64 * b + 64], A.add, ["bank%d" % b, "a0h%d" % b], ["bt%d" % b])
+    quant("b", 0, 128, T.bt[:], ["btz"] + ["bt%d" % b for b in range(4)], ["bq"])
+    for b in range(4):
+        mm(4 + b, [("w", 128 * b, "b", 0, 128)], ["wq", "ws", "bq"])
+    for b in range(4):
+        tt(T.xp[:, b:256:4], bank(4 + b, 64), T.q64[:, b:256:4], A.add, ["bank%d" % (4 + b), "q64"], ["xp%d" % b])
+    ts(T.xt[:, 0:256], T.xp[:], 0.015625, None, A.mult, None, ["xp%d" % b for b in range(4)], ["xt"])
+    quant("xx", 0, 128, T.xt[:], ["xt", "xtz"], ["xq"])
+    mm(0, [("v", 0, "xx", 0, 128)], ["vq", "xq"])
+    op("y", lambda: g.sync.dma_start(T.oc[:], u8(T.xx_q[:, 0:64])), ["xq"], (), "out")
+    for k in range(4):
+        op("s", lambda: S.dma_start(T.osc[4 * k:4 * k + 4, :], T.xx_s[32 * k:32 * k + 4, 0:64]), ["xq"], (), "out")
+    cp(T.ysb[:], bank(0, 64), ["bank0"], ["ysb"])
+    op("y", lambda: g.sync.dma_start(T.y[:], T.ysb[:]), ["ysb"], (), "out")
+    for sem in ("cg", "sent", "ct", "cs", "cv", "out"):
+        g.wait_ge(T.sem[sem], total[sem])

@@ -11,14 +11,14 @@ for _n, _w in (("ub", 512), ("zb", 512), ("vb", 512), ("t0", 1024), ("t1", 1024)
                ("tp1", 1024), ("f0", 1024), ("f1", 1024), ("e64", 2048), ("e05", 2048), ("c64", 128), ("idn", 128),
                ("qd", 512), ("q64", 256), ("b1p", 1024), ("b1", 512), ("x2", 1024), ("a0h", 256),
                ("bt", 512), ("xp", 256), ("xt", 512), ("zt", 512),
-               ("ones", 256), ("tmod", 256), ("hold", 256), ("diag", 128), ("k16", 128), ("k32", 128), ("kh", 160),
+               ("ones", 128), ("tmod", 128), ("hold", 128), ("diag", 128), ("k16", 128), ("k32", 128), ("kh", 160),
                ("jrow", 256), ("bit", 256), ("rr", 272), ("hi", 256), ("he", 256), ("ob0", 288), ("ob1", 288),
                ("ot", 544), ("eb", 96), ("ebt", 160), ("esc", 160), ("gm", 128), ("s16", 128), ("s32", 128),
                ("orig", 256), ("arr", 512), ("cmp", 1536), ("cs", 768), ("junk", 512), ("pos", 8), ("nd", 8)):
     SCRATCH[_n] = ("sbuf", [128, _w], BF)
 for _n, _w in (("j16", 16), ("jw", 16), ("crow", 96), ("ccol", 96), ("d0", 32), ("d1", 32), ("pp", 32), ("lk", 16),
                ("stf", 16), ("g0", 32), ("g1", 32), ("gg", 32), ("zc", 4), ("h0", 8), ("h1", 8),
-               ("pre", 12), ("acc", 4), ("km", 8), ("kml", 8), ("arow", 64), ("ysb", 64)):
+               ("pre", 12), ("acc", 4), ("km", 4), ("kml", 4), ("arow", 64), ("ysb", 64)):
     SCRATCH[_n] = ("sbuf", [128, _w], F32)
 for _n, _w in (("urep", 8), ("sel", 8), ("esel", 8), ("pw", 16), ("ow0", 16), ("ow1", 16), ("st0", 16), ("so0", 16),
                ("so1", 16), ("st1", 16), ("st2", 16), ("o1l", 16), ("o4", 64), ("j2", 8), ("j2l", 8)):
@@ -146,12 +146,12 @@ def rank_program(g, core, T, topo):
     for s in ("j2", "bq", "bs"):
         arrives(s, fwd2, "in_" + s)
 
-    op("y", lambda: g.sync.dma_start(T.qd[:, 0:256], T.q[:]), (), ["qb"], "ld_q")
-    op("s", lambda: S.dma_start(T.zb[:], T.z[:]), (), ["zb"], "ld_z")
     op("y", lambda: g.sync.dma_start(T.ub[:], T.u[:]), (), ["ub"], "ld_u")
     op("s", lambda: S.dma_start(T.t0[:, 0:512], T.x[:, 0:512]), (), ["t0a"], "ld_xa")
     op("y", lambda: g.sync.dma_start(T.t0[:, 512:1024], T.x[:, 512:1024]), (), ["t0b"], "ld_xb")
-    op("y", lambda: g.sync.dma_start(u8(T.w_q[:]), T.wc[:]), (), ["wq"], "ld_wc")
+    op("y", lambda: g.sync.dma_start(T.qd[:, 0:256], T.q[:]), (), ["qb"], "ld_q")
+    op("y", lambda: g.sync.dma_start(T.zb[:], T.z[:]), (), ["zb"], "ld_z")
+    op("y", lambda: g.sync.dma_start(u8(T.w_q[:]), T.wc[:]), ["t0b"], ["wq"], "ld_wc")
     op("y", lambda: g.sync.dma_start(T.w_s[:], T.ws[:]), (), ["ws"], "ld_ws")
     op("y", lambda: g.sync.dma_start(T.vb[:], T.v[:]), (), ["vb"], "ld_v")
 
@@ -163,11 +163,11 @@ def rank_program(g, core, T, topo):
     iota(T.crow[:, 48:64], [[32, 8], [288, 2]], 16, ["crow2"])
     iota(T.crow[:, 64:72], [[7, 2], [32, 2], [-64, 2]], 102, ["crow3"])
     iota(T.crow[:, 80:88], [[7, 2], [32, 2], [96, 2]], 22, ["crow4"])
-    iota(T.tmod[:], [[0, 16], [1, 16]], 0, ["tmod"])
-    op("g", lambda: g.affine_select(T.idn[:], T.c64[:], [[-1, 128]], A.is_equal, 0.0, 0, 1), ["c64"], ["idn"])
+    iota(T.tmod[:], [[0, 8], [1, 16]], 0, ["tmod"])
     iota(T.jrow[:], [[1, 256]], 0, ["jrow"])
+    op("g", lambda: g.affine_select(T.idn[:], T.c64[:], [[-1, 128]], A.is_equal, 0.0, 0, 1), ["c64"], ["idn"])
     fill(T.zt[:], 0.0, ["zt"])
-    for b in range(4):
+    for b in range(3):
         act(T.e64[:, 512 * b:512 * b + 512], T.zt[:], ["zt"], ["e64_%d" % b])
     fill(T.qd[:, 256:512], 0.0, ["qdz"])
     fill(T.kh[:], 0.5, ["kh"])
@@ -179,41 +179,43 @@ def rank_program(g, core, T, topo):
     cp(T.urep[:], T.j16[:, 0:8], ["j16"], ["urep"])
     fill(T.d0[:], 0.0, ["d0"])
     fill(T.ob0[:], 0.0, ["ob0"])
-    fill(T.ob1[:], 0.0, ["ob1"])
-    for name in ("b1", "bt", "xt"):
-        fill(T[name][:, 256:512], 0.0, [name + "z"])
+    fill(T.e64[:, 1536:2048], 0.0, ["e64_3"])
     turn(T.ccol[:], T.crow[:], ["crow%d" % i for i in range(5)], ["ccol"])
-    quant("lb", 64, 192, T.zt[:], ["zt"], ["lbz"])
+    fill(T.ob1[:], 0.0, ["ob1"])
     pm = T.ccol[:, 0:1]
     cp(T.esel[:, 0:1], T.ccol[:, 64:65], ["ccol"], ["esel"])
     cp(T.sel[:, 0:1], T.ccol[:, 32:33], ["ccol"], ["sel"])
     ts(T.jw[:], T.j16[:], pm, None, A.add, None, ["j16", "ccol"], ["jw"])
-
-    quant("qd", 0, 128, T.qd[:], ["qb", "qdz"], ["qdq"])
-    quant("z", 0, 128, T.zb[:], ["zb"], ["zq"])
-    mm(1, [("z", 0, "qd", 0, 128)], ["zq", "qdq"])
     ts(T.hold[:], T.tmod[:], pm, 512.0, A.is_equal, A.mult, ["tmod", "ccol"], ["hold"])
-    ts(T.eb[:, 16:80], bank(1, 64), 0.0, None, A.is_gt, None, ["bank1"], ["eb"])
-    turn(T.ebt[:, 0:96], T.eb[:, 0:96], ["eb"], ["ebta"])
-    turn(T.ebt[:, 96:160], T.eb[:, 16:80], ["eb"], ["ebtb"])
+
     quant("u", 0, 128, T.ub[:], ["ub"], ["uq"])
     act(T.ur_s[:], T.u_s[:].indirect(T.urep[:]), ["uq", "urep"], ["urs"])
-    scan(T.esc[:], T.kh[:], T.ebt[:], 0.0, A.mult, A.add, ["kh", "ebta", "ebtb"], ["esc"])
     cp(u32(T.ur_q[:]), u32(T.u_q[:]).indirect(T.urep[:]), ["uq", "urep"], ["urq"])
-    ts(T.lk[:], T.esc[:].indirect(T.esel[:, 0:1]), 64.0, None, A.mult, None, ["esc", "esel"], ["lk"])
     lo, kk = T.lk[:, 0:4], T.lk[:, 4:8]
     E64 = ["e64_%d" % b for b in range(4)]
-    for b in range(4):
-        act(T.e64[:, 512 * b + b:512 * b + 512:4], T.idn[:], ["idn"], ["e64_%d" % b])
 
     def scores(lv, h):
         mm(4 * h, [("ur", 0, "t%d" % lv, 128 * h, 128 * h + 128)], ["urq", "urs", "tq%d%d" % (lv, h)])
 
-    def bits(h):
+    def bits(h, first=None, second=None):
         a = 128 * h
         ts(T.bit[:, a:a + 128], bank(4 * h, 128), 0.0, None, A.is_gt, None, ["bank%d" % (4 * h)], ["bit%d" % h])
-        scan(T.rr[:, 1 + a:129 + a], T.ones[:, 0:128], T.bit[:, a:a + 128], T.rr[:, a:a + 1], A.mult, A.add,
+        if first:
+            first()
+        scan(T.rr[:, 1 + a:129 + a], T.ones[:], T.bit[:, a:a + 128], T.rr[:, a:a + 1], A.mult, A.add,
              ["ones", "bit%d" % h, "rr0", "rra"] if h else ["ones", "bit0", "rr0"], ["rrb" if h else "rra"])
+        if second:
+            second()
+
+    def held(name, h):
+        a = 128 * h + (1 if name == "hi" else 0)
+        scan(T[name][:, 128 * h:128 * h + 128], T.hold[:], T.rr[:, a:a + 128], 0.0, A.add, A.min,
+             ["hold", "rr0", "rra"] + (["rrb"] if h else []), [name + str(h)])
+
+    def zeros_to(h):
+        a = 128 * h
+        scan(T.arr[:, a:a + 128], T.ones[:], T.bit[:, a:a + 128], T.arr[:, 127:128] if h else 0.0,
+             A.add, A.subtract, ["ones", "bit%d" % h] + (["arr0"] if h else []), ["arra" if h else "arr0"])
 
     RR = ["rr0", "rra", "rrb"]
     n1 = T.rr[:, 256:257]
@@ -226,12 +228,13 @@ def rank_program(g, core, T, topo):
             if spare:
                 spare.pop(0)()
 
-        scan(T.hi[:], T.hold[:], T.rr[:, 1:257], 0.0, A.add, A.min, ["hold"] + RR, ["hi"])
-        scan(T.he[:], T.hold[:], T.rr[:, 0:256], 0.0, A.add, A.min, ["hold"] + RR, ["he"])
+        held("hi", 1)
+        held("he", 1)
+        gap()
         inc, exc = T.hi[:, 15:256:16], T.he[:, 15:256:16]
-        tt(T.d1[:, 1:32:2], T.jw[:], inc, A.subtract, ["jw", "hi"], ["d1b"])
-        ts(T.d1[:, 0:32:2], exc, n1, 256.0, A.subtract, A.add, ["he", "rrb"], ["d1a"])
-        tt(T.d0[:, 1:32:2], inc, exc, A.subtract, ["hi", "he"], ["d0"])
+        tt(T.d1[:, 1:32:2], T.jw[:], inc, A.subtract, ["jw", "hi0", "hi1"], ["d1b"])
+        ts(T.d1[:, 0:32:2], exc, n1, 256.0, A.subtract, A.add, ["he0", "he1", "rrb"], ["d1a"])
+        tt(T.d0[:, 1:32:2], inc, exc, A.subtract, ["hi0", "hi1", "he0", "he1"], ["d0"])
         gap()
         scan(T.pp[:], T.d0[:], T.d1[:], 0.0, A.mult, A.max, ["d0", "d1a", "d1b"], ["pp"])
         gap()
@@ -307,28 +310,46 @@ def rank_program(g, core, T, topo):
                   ["t%d%d%d" % (lv, h, b) for b in range(4)], ["tq%d%d" % (lv, h)])
             scores(lv, h)
 
+    def query_scores():
+        quant("z", 0, 128, T.zb[:], ["zb"], ["zq"])
+        mm(1, [("z", 0, "qd", 0, 128)], ["zq", "qdq"])
+
+    def query_turns():
+        turn(T.ebt[:, 0:96], T.eb[:, 0:96], ["eb"], ["ebta"])
+        turn(T.ebt[:, 96:160], T.eb[:, 16:80], ["eb"], ["ebtb"])
+
+    def query_numbers():
+        scan(T.esc[:], T.kh[:], T.ebt[:], 0.0, A.mult, A.add, ["kh", "ebta", "ebtb"], ["esc"])
+        fill(T.g0[:], 0.0, ["g0z"])
+        ts(T.lk[:], T.esc[:].indirect(T.esel[:, 0:1]), 64.0, None, A.mult, None, ["esc", "esel"], ["lk"])
+        send(nxt, T.kml[:], kk, "km", ["lk"])
+
     quant("t0", 0, 128, T.t0[:, 0:512], ["t0a"], ["tq00"])
     scores(0, 0)
-    ts(T.km[:, 0:4], kk, -128.0, None, A.add, None, ["lk"], ["kma"])
-    ts(T.km[:, 4:8], kk, -1.0, None, A.mult, None, ["lk"], ["km"])
-    send(nxt, T.kml[:], T.km[:], "km", ["km", "kma"])
     bits(0)
     quant("t0", 128, 256, T.t0[:, 512:1024], ["t0b"], ["tq01"])
     scores(0, 1)
     for b in range(4):
         act(T.tp0[:, 256 * b:256 * b + 256], T.t0[:, b:1024:4], ["t0a", "t0b"], ["tp0%d" % b])
-    bits(1)
+    for b in range(4):
+        act(T.e64[:, 512 * b + b:512 * b + 512:4], T.idn[:], ["idn"], ["e64_%d" % b])
+    held("hi", 0)
+    held("he", 0)
+    bits(1, lambda: quant("qd", 0, 128, T.qd[:], ["qb", "qdz"], ["qdq"]), query_scores)
     order_and_send(0, [
-        lambda: ts(T.k32[:], T.tmod[:, 0:128], 1.0, None, A.min, None, ["tmod"], ["k32"]),
-        lambda: ts(T.diag[:], T.tmod[:, 0:128], pm, None, A.is_equal, None, ["tmod", "ccol"], ["diag"]),
-        lambda: ts(T.k16[:], T.tmod[:, 0:128], 1.0, None, A.min, None, ["tmod"], ["k16"]),
-        lambda: fill(T.k32[:, 16:128:32], -1.0, ["k32"]),
-        lambda: fill(T.g0[:], 0.0, ["g0z"]),
-        zeros_total])
+        lambda: None,
+        lambda: ts(T.eb[:, 16:80], bank(1, 64), 0.0, None, A.is_gt, None, ["bank1"], ["eb"]),
+        query_turns,
+        query_numbers,
+        lambda: ts(T.k32[:], T.tmod[:], 1.0, None, A.min, None, ["tmod"], ["k32"]),
+        lambda: ts(T.diag[:], T.tmod[:], pm, None, A.is_equal, None, ["tmod", "ccol"], ["diag"]),
+        lambda: ts(T.k16[:], T.tmod[:], 1.0, None, A.min, None, ["tmod"], ["k16"])])
 
     quant("e64", 0, 512, T.e64[:], E64, ["e64q"])
     act(T.q64[:], T.qd[:, 0:256], ["qb"], ["q64"], 64.0)
     act(T.e05[:], T.e64[:], E64, ["e05"], 0.0078125)
+    fill(T.k32[:, 16:128:32], -1.0, ["k32"])
+    zeros_total()
     cp(T.st0[:, 0:8:2], lo, ["lk"], ["st0a"])
     ts(T.st0[:, 1:8:2], lo, 128.0, None, A.add, None, ["lk"], ["st0"])
     cp(T.stf[:, 0:8:2], lo, ["lk"], ["stfa"])
@@ -344,18 +365,22 @@ def rank_program(g, core, T, topo):
     for b in range(4):
         act(T.tp1[:, 256 * b:256 * b + 256], T.t1[:, b:1024:4], ["t10%d" % b, "t11%d" % b], ["tp1%d" % b])
     bits(0)
-    bits(1)
+    bits(1, lambda: held("hi", 0), lambda: held("he", 0))
     order_and_send(1, [
+        lambda: None,
         zeros_total,
-        lambda: fill(T.h0[:], 0.0, ["h0"]),
+        lambda: ts(T.km[:], T.kml[:], -128.0, None, A.add, None, ["kml"], ["km"]),
         lambda: cp(T.stf[:], T.st1[:], ["st1"], ["stf"]),
-        lambda: tt(T.stf[:, 8:16], T.stf[:, 8:16], T.kml[:], A.add, ["stf", "kml"], ["stf"]),
+        lambda: tt(T.stf[:, 12:16], T.stf[:, 12:16], T.kml[:], A.subtract, ["stf", "kml"], ["stf"]),
+        lambda: tt(T.stf[:, 8:12], T.stf[:, 8:12], T.km[:], A.add, ["stf", "km"], ["stf"]),
         keep_rest])
     step(T.st1, "st1", T.so1, "so1", False)
     send(nxt, T.st2[:], T.so1[:], "st2", ["so1"])
     send(prv, T.o1l[:], T.ow1[:], "o1", ["ow1"])
+    for name in ("b1", "bt", "xt"):
+        act(T[name][:, 256:512], T.zt[:, 0:256], ["zt"], [name + "z"])
+    fill(T.h0[:], 0.0, ["h0"])
     quant("e05", 0, 512, T.e05[:], ["e05"], ["e05q"])
-    quant("v", 0, 128, T.vb[:], ["vb"], ["vq"])
 
     layer(2)
     mixed = (1, 2, 3, 5)
@@ -365,8 +390,7 @@ def rank_program(g, core, T, topo):
     for b in range(4):
         act(T.b1p[:, 256 * b:256 * b + 256], bank(mixed[b], 256), ["bank%d" % mixed[b]], ["b1p%d" % b], 0.0078125)
     bits(0)
-    bits(1)
-    scan(T.arr[:, 0:256], T.ones[:], T.bit[:], 0.0, A.add, A.subtract, ["ones", "bit0", "bit1"], ["arra"])
+    bits(1, lambda: zeros_to(0), lambda: zeros_to(1))
     picked(T.st2, "st2")
     cp(T.stf[:, 8:16], T.st2[:, 8:16], ["st2"], ["stf"])
     counts()
@@ -403,6 +427,8 @@ def rank_program(g, core, T, topo):
     act(T.x2[:, 512:1024], T.f0[:].indirect(T.o4[:, 32:64]), F0 + ["o42", "o43"], ["x2b"], 0.5)
     ts(T.x2[:, 0:512], T.f0[:].indirect(T.o4[:, 0:32]), 0.5, None, A.mult, None, F0 + ["o40", "o41"], ["x2a"])
     act(T.orig[:], T.ob0[:, 16:272].indirect(T.o1l[:]), ["ob0", "o1l"], ["orig"])
+    quant("lb", 64, 192, T.zt[:], ["zt"], ["lbz"])
+    quant("v", 0, 128, T.vb[:], ["vb"], ["vq"])
     for b in (2, 3, 0, 1):
         (cp if b < 2 else act)(T.a0h[:, 64 * b:64 * b + 64], T.x2[:, 256 * b:256 * b + 256].indirect(T.j2l[:, 0:4]),
                                ["in_j2", "x2" + "ab"[b // 2]], ["a0h%d" % b])

@@ -4,28 +4,28 @@ X4, U8, BF, F32, U16 = "float8_e4m3fn_x4", "uint8", "bfloat16", "float32", "uint
 SCRATCH = {"ps": ("psum", [128, 4096], F32)}
 for _n, _w in (("u", 128), ("ur", 128), ("t0", 256), ("t1", 256), ("t2", 256), ("f0", 256), ("f1", 256),
                ("l1", 256), ("l2", 256), ("w", 512), ("e64", 512), ("e05", 512), ("z", 128), ("qd", 128),
-               ("v", 128), ("b1", 128), ("lb", 192), ("b", 128), ("xx", 128)):
+               ("v", 128), ("lb", 192), ("b", 128), ("xx", 128)):
     SCRATCH[_n + "_q"] = ("sbuf", [128, _w], X4)
     SCRATCH[_n + "_s"] = ("sbuf", [128, _w], U8)
-for _n, _w in (("ub", 512), ("zb", 512), ("vb", 512), ("t0", 1024), ("t1", 1024), ("t2", 1024), ("tp0", 1024),
-               ("tp1", 1024), ("f0", 1024), ("f1", 1024), ("e64", 2048), ("e05", 2048), ("c64", 128), ("idn", 128),
-               ("qd", 512), ("q64", 256), ("b1p", 1024), ("b1", 512), ("x2", 1024), ("a0h", 256),
-               ("bt", 512), ("xp", 256), ("xt", 512), ("zt", 512),
-               ("ones", 128), ("tmod", 128), ("hold", 128), ("diag", 128), ("k16", 128), ("k32", 128), ("kh", 160),
-               ("jrow", 256), ("bit", 256), ("rr", 272), ("hi", 256), ("he", 256), ("ob0", 288), ("ob1", 288),
+for _n, _w in (("ub", 512), ("zb", 512), ("vb", 512), ("t0", 1280), ("t1", 1280), ("t2", 1280), ("tp0", 1024),
+               ("tp1", 1024), ("f0", 1024), ("f1", 1280), ("fp", 1024), ("e64", 520), ("e05", 520), ("c64", 160),
+               ("idn", 128), ("q64", 256), ("b1p", 1024), ("x2", 1024), ("a0h", 256), ("xp", 256),
+               ("ones", 128), ("kb", 896), ("k16", 128), ("k32", 128), ("kh", 160),
+               ("jrow", 256), ("bit", 256), ("rr", 272), ("hi", 256), ("he", 256),
                ("ot", 544), ("eb", 96), ("ebt", 160), ("esc", 160), ("gm", 128), ("s16", 128), ("s32", 128),
-               ("orig", 256), ("arr", 512), ("cmp", 1536), ("cs", 768), ("junk", 512), ("pos", 8), ("nd", 8)):
+               ("orig", 256), ("arr", 512), ("cmp", 1536), ("cs", 1024), ("junk", 512), ("pos", 8), ("nd", 8),
+               ("pm", 32)):
     SCRATCH[_n] = ("sbuf", [128, _w], BF)
-for _n, _w in (("j16", 16), ("jw", 16), ("crow", 96), ("ccol", 96), ("d0", 32), ("d1", 32), ("pp", 32), ("lk", 16),
-               ("stf", 16), ("g0", 32), ("g1", 32), ("gg", 32), ("zc", 4), ("h0", 8), ("h1", 8),
-               ("pre", 12), ("acc", 4), ("km", 4), ("kml", 4), ("arow", 64), ("ysb", 64)):
+for _n, _w in (("j16", 16), ("jw", 16), ("crow", 64), ("ccol", 64), ("d0", 32), ("d1", 32), ("pp", 32), ("lk", 16),
+               ("stf", 12), ("kap", 4), ("g0", 24), ("g1", 24), ("gg", 24), ("zc", 4), ("h0", 8), ("h1", 8),
+               ("acc", 4), ("kml", 4), ("arow", 64), ("ysb", 64)):
     SCRATCH[_n] = ("sbuf", [128, _w], F32)
-for _n, _w in (("urep", 8), ("sel", 8), ("esel", 8), ("pw", 16), ("ow0", 16), ("ow1", 16), ("st0", 16), ("so0", 16),
-               ("so1", 16), ("st1", 16), ("st2", 16), ("o1l", 16), ("o4", 64), ("j2", 8), ("j2l", 8)):
+for _n, _w in (("urep", 8), ("sel", 8), ("esel", 8), ("pw", 16), ("ow0", 16), ("ow1", 16), ("st0", 8), ("so0", 16),
+               ("so1", 16), ("st1", 16), ("st2", 16), ("o1l", 16), ("j2", 8), ("j2l", 8)):
     SCRATCH[_n] = ("sbuf", [128, _w], U16)
 SEMAPHORES = ["cv", "cs", "ct", "cg", "sent", "out",
               "ld_u", "ld_xa", "ld_xb", "ld_q", "ld_z", "ld_wc", "ld_ws", "ld_v",
-              "a1", "s1", "b1", "a2", "s2", "b2", "km", "st1", "st2", "o1", "j2", "bq", "bs"]
+              "a1", "b1", "a2", "b2", "km", "st1", "st2", "o1", "j2", "bq"]
 A = AluOpType
 ACT = ActivationFunctionType
 
@@ -79,8 +79,8 @@ def rank_program(g, core, T, topo):
         total[name] = total.get(name, 0) + inc
         after((name, total[name], dict(seen[q]), q), r, w)
 
-    def arrives(sem, src, key):
-        total[sem] = len(topo.engines(src, core))
+    def arrives(sem, src, key, writes=1):
+        total[sem] = writes * len(topo.engines(src, core))
         writer[key] = (sem, total[sem], {}, "r")
 
     def send(dst, out, src, sem, r):
@@ -110,17 +110,22 @@ def rank_program(g, core, T, topo):
     def fill(ap, c, w):
         op("v", lambda: V.memset(ap, c), (), w)
 
-    def act(out, a, r, w, scale=1.0):
-        if scale == 1.0:
+    def act(out, a, r, w, scale=1.0, bias=None):
+        if bias is not None:
+            op("s", lambda: S.activation(out, a, ACT.Identity, bias=bias, scale=scale), r, w)
+        elif scale == 1.0:
             op("s", lambda: S.activation(out, a, ACT.Copy), r, w)
         else:
             op("s", lambda: S.activation(out, a, ACT.Copy, scale=scale), r, w)
 
+    def sfill(ap, m, c, w):
+        act(ap, T.c64[:, 0:m], ["c64"], w, c / 64.0)
+
     def quant(name, a, b, src, r, w):
         op("v", lambda: V.quantize_mx(T[name + "_q"][:, a:b], T[name + "_s"][:, a:b], src), r, w)
 
-    def bank(k, m):
-        return T.ps[:, 512 * k:512 * k + m]
+    def bank(k, m, a=0):
+        return T.ps[:, 512 * k + a:512 * k + a + m]
 
     def mm(k, terms, r):
         before("t", r, ["bank%d" % k])
@@ -138,61 +143,57 @@ def rank_program(g, core, T, topo):
     u32 = lambda v: v.bitcast(dt.uint32)
 
     for lv in (1, 2):
-        for s, k in (("a", "lqa"), ("s", "ls"), ("b", "lqb")):
-            arrives("%s%d" % (s, lv), prv, "%s%d" % (k, lv))
+        arrives("a%d" % lv, prv, "lqa%d" % lv, 2)
+        arrives("b%d" % lv, prv, "lqb%d" % lv, 2 if topo.chip(prv) == topo.chip(core) else 1)
     for s, k in (("km", "kml"), ("st1", "st1"), ("st2", "st2")):
         arrives(s, prv, k)
     arrives("o1", nxt, "o1l")
-    for s in ("j2", "bq", "bs"):
-        arrives(s, fwd2, "in_" + s)
+    arrives("j2", fwd2, "in_j2")
+    arrives("bq", fwd2, "in_bq", 2)
 
+    qb = T.t0[:, 1024:1280]
     op("y", lambda: g.sync.dma_start(T.ub[:], T.u[:]), (), ["ub"], "ld_u")
     op("s", lambda: S.dma_start(T.t0[:, 0:512], T.x[:, 0:512]), (), ["t0a"], "ld_xa")
     op("y", lambda: g.sync.dma_start(T.t0[:, 512:1024], T.x[:, 512:1024]), (), ["t0b"], "ld_xb")
-    op("y", lambda: g.sync.dma_start(T.qd[:, 0:256], T.q[:]), (), ["qb"], "ld_q")
+    op("y", lambda: g.sync.dma_start(qb, T.q[:]), (), ["qb"], "ld_q")
     op("y", lambda: g.sync.dma_start(T.zb[:], T.z[:]), (), ["zb"], "ld_z")
     op("y", lambda: g.sync.dma_start(u8(T.w_q[:]), T.wc[:]), ["t0b"], ["wq"], "ld_wc")
     op("y", lambda: g.sync.dma_start(T.w_s[:], T.ws[:]), (), ["ws"], "ld_ws")
     op("y", lambda: g.sync.dma_start(T.vb[:], T.v[:]), (), ["vb"], "ld_v")
 
-    fill(T.crow[:, 64:96], 0.0, ["crow3", "crow4"])
+    tmod, hold, diag = T.kb[:, 0:128], T.kb[:, 384:512], T.kb[:, 768:896]
+    obase = (128, 512)
     fill(T.c64[:], 64.0, ["c64"])
+    fill(T.crow[:, 32:64], 0.0, ["crow3", "crow4"])
+    fill(T.e64[:], 0.0, ["e64"])
     iota(T.j16[:], [[16, 16]], 0, ["j16"])
-    iota(T.crow[:, 0:32], [[0, 2], [1, 16]], 0, ["crow0"])
-    iota(T.crow[:, 32:48], [[32, 8], [-256, 2]], 288, ["crow1"])
-    iota(T.crow[:, 48:64], [[32, 8], [288, 2]], 16, ["crow2"])
-    iota(T.crow[:, 64:72], [[7, 2], [32, 2], [-64, 2]], 102, ["crow3"])
-    iota(T.crow[:, 80:88], [[7, 2], [32, 2], [96, 2]], 22, ["crow4"])
-    iota(T.tmod[:], [[0, 8], [1, 16]], 0, ["tmod"])
+    iota(tmod, [[0, 8], [1, 16]], 0, ["tmod"])
+    iota(T.crow[:, 0:16], [[32, 8], [-256, 2]], 288, ["crow1"])
+    iota(T.crow[:, 16:32], [[32, 8], [288, 2]], 16, ["crow2"])
+    iota(T.crow[:, 32:40], [[7, 2], [32, 2], [-64, 2]], 102, ["crow3"])
+    iota(T.crow[:, 48:56], [[7, 2], [32, 2], [96, 2]], 22, ["crow4"])
     iota(T.jrow[:], [[1, 256]], 0, ["jrow"])
-    op("g", lambda: g.affine_select(T.idn[:], T.c64[:], [[-1, 128]], A.is_equal, 0.0, 0, 1), ["c64"], ["idn"])
-    fill(T.zt[:], 0.0, ["zt"])
-    for b in range(3):
-        act(T.e64[:, 512 * b:512 * b + 512], T.zt[:], ["zt"], ["e64_%d" % b])
-    fill(T.qd[:, 256:512], 0.0, ["qdz"])
-    fill(T.kh[:], 0.5, ["kh"])
-    fill(T.eb[:], 0.0, ["eb"])
-    fill(T.ones[:], 1.0, ["ones"])
-    fill(T.kh[:, 0:160:16], 0.0, ["kh"])
-    fill(T.rr[:, 0:1], 0.0, ["rr0"])
-    fill(T.kh[:, 7:160:16], 0.0, ["kh"])
+    op("g", lambda: g.affine_select(T.idn[:], T.c64[:, 0:128], [[-1, 128]], A.is_equal, 0.0, 0, 1), ["c64"], ["idn"])
+    sfill(T.kh[:], 160, 0.5, ["kh"])
+    sfill(T.ones[:], 128, 1.0, ["ones"])
+    sfill(T.kh[:, 0:160:16], 10, 0.0, ["kh"])
+    sfill(T.rr[:, 0:1], 1, 0.0, ["rr0"])
+    sfill(T.kh[:, 7:160:16], 10, 0.0, ["kh"])
+    sfill(T.d0[:], 32, 0.0, ["d0"])
+    sfill(T.eb[:], 96, 0.0, ["eb"])
+
+    def unit(name, b):
+        quant(name, 128 * b, 128 * b + 128, T[name][:, 3 - b:515 - b], [name], ["%sq%d" % (name, b)])
+
+    pm = T.pm[:, 0:1]
     cp(T.urep[:], T.j16[:, 0:8], ["j16"], ["urep"])
-    fill(T.d0[:], 0.0, ["d0"])
-    fill(T.ob0[:], 0.0, ["ob0"])
-    fill(T.e64[:, 1536:2048], 0.0, ["e64_3"])
-    turn(T.ccol[:], T.crow[:], ["crow%d" % i for i in range(5)], ["ccol"])
-    fill(T.ob1[:], 0.0, ["ob1"])
-    pm = T.ccol[:, 0:1]
-    cp(T.esel[:, 0:1], T.ccol[:, 64:65], ["ccol"], ["esel"])
-    cp(T.sel[:, 0:1], T.ccol[:, 32:33], ["ccol"], ["sel"])
-    ts(T.jw[:], T.j16[:], pm, None, A.add, None, ["j16", "ccol"], ["jw"])
-    ts(T.hold[:], T.tmod[:], pm, 512.0, A.is_equal, A.mult, ["tmod", "ccol"], ["hold"])
+    turn(T.pm[:], T.kb[:, 0:32], ["tmod"], ["pm"])
+    ts(hold, tmod, pm, 512.0, A.is_equal, A.mult, ["tmod", "pm"], ["hold"])
+    ts(T.jw[:], T.j16[:], pm, None, A.add, None, ["j16", "pm"], ["jw"])
 
     quant("u", 0, 128, T.ub[:], ["ub"], ["uq"])
     act(T.ur_s[:], T.u_s[:].indirect(T.urep[:]), ["uq", "urep"], ["urs"])
     cp(u32(T.ur_q[:]), u32(T.u_q[:]).indirect(T.urep[:]), ["uq", "urep"], ["urq"])
-    lo, kk = T.lk[:, 0:4], T.lk[:, 4:8]
-    E64 = ["e64_%d" % b for b in range(4)]
 
     def scores(lv, h):
         mm(4 * h, [("ur", 0, "t%d" % lv, 128 * h, 128 * h + 128)], ["urq", "urs", "tq%d%d" % (lv, h)])
@@ -209,7 +210,7 @@ def rank_program(g, core, T, topo):
 
     def held(name, h):
         a = 128 * h + (1 if name == "hi" else 0)
-        scan(T[name][:, 128 * h:128 * h + 128], T.hold[:], T.rr[:, a:a + 128], 0.0, A.add, A.min,
+        scan(T[name][:, 128 * h:128 * h + 128], hold, T.rr[:, a:a + 128], 0.0, A.add, A.min,
              ["hold", "rr0", "rra"] + (["rrb"] if h else []), [name + str(h)])
 
     def zeros_to(h):
@@ -220,9 +221,10 @@ def rank_program(g, core, T, topo):
     RR = ["rr0", "rra", "rrb"]
     n1 = T.rr[:, 256:257]
 
-    def order_and_send(lv, spare):
-        ob, ow, tp, f = T["ob%d" % lv], T["ow%d" % lv], T["tp%d" % lv], T["f%d" % lv]
+    def order_and_send(lv, spare, parts=1):
+        o, ow, tp, f = obase[lv], T["ow%d" % lv], T["tp%d" % lv], T["f%d" % lv]
         obk, owk = "ob%d" % lv, "ow%d" % lv
+        pads = (["tmod", "hold"], ["hold", "diag"])[lv]
 
         def gap():
             if spare:
@@ -232,73 +234,85 @@ def rank_program(g, core, T, topo):
         held("he", 1)
         gap()
         inc, exc = T.hi[:, 15:256:16], T.he[:, 15:256:16]
-        tt(T.d1[:, 1:32:2], T.jw[:], inc, A.subtract, ["jw", "hi0", "hi1"], ["d1b"])
         ts(T.d1[:, 0:32:2], exc, n1, 256.0, A.subtract, A.add, ["he0", "he1", "rrb"], ["d1a"])
+        tt(T.d1[:, 1:32:2], T.jw[:], inc, A.subtract, ["jw", "hi0", "hi1"], ["d1b"])
         tt(T.d0[:, 1:32:2], inc, exc, A.subtract, ["hi0", "hi1", "he0", "he1"], ["d0"])
         gap()
         scan(T.pp[:], T.d0[:], T.d1[:], 0.0, A.mult, A.max, ["d0", "d1a", "d1b"], ["pp"])
         gap()
         cp(T.pw[:], T.pp[:, 1:32:2], ["pp"], ["pw"])
         gap()
-        cp(ob[:, 16:272].indirect(T.pw[:]), T.jrow[:], ["pw", "jrow"], [obk])
-        gap()
-        turn(T.ot[:, 0:288], ob[:, 0:288], [obk], ["ota"])
-        turn(T.ot[:, 288:544], ob[:, 16:272], [obk], ["otb"])
+        m = 16 // parts
+        for k in range(parts):
+            cp(T.kb[:, o:o + 256].indirect(T.pw[:, m * k:m * k + m]), T.jrow[:, 16 * m * k:16 * m * (k + 1)],
+               ["pw", "jrow"], [obk])
+            gap()
+        turn(T.ot[:, 0:288], T.kb[:, o - 16:o + 272], [obk] + pads, ["ota"])
+        turn(T.ot[:, 288:544], T.kb[:, o:o + 256], [obk], ["otb"])
         gap()
         cp(ow[:], T.ot[:].indirect(T.sel[:, 0:1]), ["ota", "otb", "sel"], [owk])
         gap()
         fq, fs, lq, ls = T["f%d_q" % lv], T["f%d_s" % lv], T["l%d_q" % (lv + 1)], T["l%d_s" % (lv + 1)]
-        for h in range(2):
-            for b in (2, 3, 0, 1):
-                (cp if b < 2 else act)(f[:, 512 * h + b:512 * h + 512:4],
-                                       tp[:, 256 * b:256 * b + 256].indirect(ow[:, 8 * h:8 * h + 8]),
-                                       [owk, "tp%d%d" % (lv, b)], ["f%d%d%d" % (lv, h, b)])
-            quant("f%d" % lv, 128 * h, 128 * h + 128, f[:, 512 * h:512 * h + 512],
+
+        def gather(h, b):
+            (cp if b < 2 else act)(f[:, 512 * h + b:512 * h + 512:4],
+                                   tp[:, 256 * b:256 * b + 256].indirect(ow[:, 8 * h:8 * h + 8]),
+                                   [owk, "tp%d%d" % (lv, b)], ["f%d%d%d" % (lv, h, b)])
+
+        def pack(h):
+            a, sem = 128 * h, "%s%d" % ("ab"[h], lv + 1)
+            quant("f%d" % lv, a, a + 128, f[:, 4 * a:4 * a + 512],
                   ["f%d%d%d" % (lv, h, b) for b in range(4)], ["fq%d%d" % (lv, h)])
-        send(nxt, u8(lq[:, 0:128]), u8(fq[:, 0:128]), "a%d" % (lv + 1), ["fq%d0" % lv])
-        send(nxt, ls[:], fs[:], "s%d" % (lv + 1), ["fq%d0" % lv, "fq%d1" % lv])
-        send(nxt, u8(lq[:, 128:256]), u8(fq[:, 128:256]), "b%d" % (lv + 1), ["fq%d1" % lv])
+            near = topo.chip(core) == topo.chip(nxt)
+            if h and not near:
+                send(nxt, ls[:], fs[:], "a%d" % (lv + 1), ["fq%d0" % lv, "fq%d1" % lv])
+            send(nxt, u8(lq[:, a:a + 128]), u8(fq[:, a:a + 128]), sem, ["fq%d%d" % (lv, h)])
+            if near:
+                send(nxt, ls[:, a:a + 128], fs[:, a:a + 128], sem, ["fq%d%d" % (lv, h)])
+
+        for h, b in ((0, 2), (0, 3), (1, 2), (1, 3), (0, 0), (0, 1), (1, 0)):
+            gather(h, b)
+        pack(0)
+        gather(1, 1)
+        pack(1)
         while spare:
             gap()
 
-    def zeros_total():
-        ts(T.zc[:, 0:1], n1, -1.0, 256.0, A.mult, A.add, ["rrb"], ["zc"])
-
-    def keep_rest():
-        cp(T.g1[:, 24:32:2], T.stf[:, 12:16], ["stf"], ["g13"])
-
     def picked(lst, key):
-        tt(T.gm[:], T.rr[:, 0:257].indirect(lst[:, 0:8]), T.diag[:], A.mult, RR + [key, "diag"], ["gm"])
+        tt(T.gm[:], T.rr[:, 0:257].indirect(lst[:, 0:8]), diag, A.mult, RR + [key, "diag"], ["gm"])
 
     def counts():
         scan(T.s32[:], T.k32[:], T.gm[:], 0.0, A.mult, A.add, ["k32", "gm"], ["s32"])
         scan(T.s16[:], T.k16[:], T.gm[:], 0.0, A.mult, A.add, ["k16", "gm"], ["s16"])
 
+    ab, before_l, before_r, ones_in = T.s16[:, 15:128:16], T.s16[:, 15:128:32], T.s16[:, 31:128:32], T.s32[:, 31:128:32]
+
     def step(lst, key, out, okey, first):
         picked(lst, key)
-        counts()
-        ab, a, b, m = T.s16[:, 15:128:16], T.s16[:, 15:128:32], T.s16[:, 31:128:32], T.s32[:, 31:128:32]
-        lk, kap = T.stf[:, 8:12], T.stf[:, 12:16]
-        for i, view in enumerate((T.g0[:, 1:16:4], T.g0[:, 3:16:4], T.g0[:, 17:24:2], T.g0[:, 25:32:2])):
-            tt(view, m, T.pre[:, 0:4] if first else kap, A.is_ge, ["s32", "stf", "pre0", "g0z"], ["g0%d" % i])
         if not first:
-            tt(T.pre[:, 8:12], b, kap, A.subtract, ["stf", "s16"], ["pre2"])
-        tt(T.g1[:, 1:16:2], T.stf[:, 0:8], ab, A.subtract, ["stf", "s16"], ["g10"])
-        tt(T.g1[:, 17:24:2], lk, a, A.subtract, ["stf", "s16"], ["g11"])
-        tt(T.g1[:, 25:32:2], kap, m, A.subtract, ["stf", "s32"], ["g12"])
-        ts(T.g1[:, 0:16:2], ab, T.zc[:, 0:1], None, A.add, None, ["zc", "s16"], ["g14"])
-        ts(T.g1[:, 16:24:2], b if first else T.pre[:, 8:12], T.zc[:, 0:1], None, A.add, None,
-           ["zc", "s16", "pre2"], ["g15"])
+            ts(T.zc[:], T.kap[:], n1, -256.0, A.add, A.add, ["kap", "rrb"], ["zc"])
+        counts()
+        rest = T.lk[:, 4:8] if first else T.kap[:]
+        place = T.stf[:, 1:8:2] if first else T.stf[:, 8:12]
+        for i, view in enumerate((T.g0[:, 1:16:4], T.g0[:, 3:16:4], T.g0[:, 17:24:2])):
+            tt(view, ones_in, rest, A.is_ge, ["s32", "kap", "lk", "g0z"], ["g0%d" % i])
+        tt(T.g1[:, 1:16:2], T.stf[:, 0:8], ab, A.subtract, ["stf", "stfr", "s16"], ["g10"])
+        tt(T.g1[:, 17:24:2], place, before_l, A.subtract, ["stf", "stfr", "s16"], ["g11"])
+        ts(T.g1[:, 0:16:2], ab, n1, 256.0, A.subtract, A.add, ["rrb", "s16"], ["g12"])
+        if first:
+            ts(T.g1[:, 16:24:2], before_r, n1, 256.0, A.subtract, A.add, ["rrb", "s16"], ["g13"])
+        else:
+            tt(T.g1[:, 16:24:2], before_r, T.zc[:], A.subtract, ["zc", "s16"], ["g13"])
         scan(T.gg[:], T.g0[:], T.g1[:], 0.0, A.mult, A.max,
-             ["g0%d" % i for i in range(4)] + ["g1%d" % i for i in range(6)], ["gg"])
-        cp(out[:], T.gg[:, 1:32:2], ["gg"], [okey])
+             ["g0%d" % i for i in range(3)] + ["g1%d" % i for i in range(4)], ["gg"])
+        cp(out[:, 0:12], T.gg[:, 1:24:2], ["gg"], [okey])
 
     def layer(lv):
         t, ln = T["t%d" % lv], "l%d" % lv
         for h in range(2):
             for b in (2, 0, 3, 1):
                 mm(4 * h + b, [("w", 128 * b, ln, 128 * h, 128 * h + 128), ("e64", 128 * b, ln, 128 * h, 128 * h + 128)],
-                   ["wq", "ws", "e64q", "ls%d" % lv, "lq%s%d" % ("ab"[h], lv)])
+                   ["wq", "ws", "e64q%d" % b, "lq%s%d" % ("ab"[h], lv)])
         for h in range(2):
             for b in (2, 0, 3, 1):
                 view, k = t[:, 512 * h + b:512 * h + 512:4], 4 * h + b
@@ -314,142 +328,145 @@ def rank_program(g, core, T, topo):
         quant("z", 0, 128, T.zb[:], ["zb"], ["zq"])
         mm(1, [("z", 0, "qd", 0, 128)], ["zq", "qdq"])
 
-    def query_turns():
+    def query_numbers():
         turn(T.ebt[:, 0:96], T.eb[:, 0:96], ["eb"], ["ebta"])
         turn(T.ebt[:, 96:160], T.eb[:, 16:80], ["eb"], ["ebtb"])
-
-    def query_numbers():
         scan(T.esc[:], T.kh[:], T.ebt[:], 0.0, A.mult, A.add, ["kh", "ebta", "ebtb"], ["esc"])
-        fill(T.g0[:], 0.0, ["g0z"])
-        ts(T.lk[:], T.esc[:].indirect(T.esel[:, 0:1]), 64.0, None, A.mult, None, ["esc", "esel"], ["lk"])
-        send(nxt, T.kml[:], kk, "km", ["lk"])
+        act(T.lk[:], T.esc[:].indirect(T.esel[:, 0:1]), ["esc", "esel"], ["lk"], -64.0, 128.0)
+        send(nxt, T.kml[:], T.lk[:, 4:8], "km", ["lk"])
+        act(T.stf[:, 0:8:2], T.lk[:, 0:4], ["lk"], ["stf"], -1.0, 128.0)
+        act(T.stf[:, 1:8:2], T.lk[:, 0:4], ["lk"], ["stfr"], -1.0, 256.0)
 
-    quant("t0", 0, 128, T.t0[:, 0:512], ["t0a"], ["tq00"])
-    scores(0, 0)
-    bits(0)
-    quant("t0", 128, 256, T.t0[:, 512:1024], ["t0b"], ["tq01"])
-    scores(0, 1)
+    for h in range(2):
+        quant("t0", 128 * h, 128 * h + 128, T.t0[:, 512 * h:512 * h + 512], ["t0" + "ab"[h]], ["tq0%d" % h])
+        scores(0, h)
     for b in range(4):
         act(T.tp0[:, 256 * b:256 * b + 256], T.t0[:, b:1024:4], ["t0a", "t0b"], ["tp0%d" % b])
-    for b in range(4):
-        act(T.e64[:, 512 * b + b:512 * b + 512:4], T.idn[:], ["idn"], ["e64_%d" % b])
-    held("hi", 0)
-    held("he", 0)
-    bits(1, lambda: quant("qd", 0, 128, T.qd[:], ["qb", "qdz"], ["qdq"]), query_scores)
-    order_and_send(0, [
-        lambda: None,
-        lambda: ts(T.eb[:, 16:80], bank(1, 64), 0.0, None, A.is_gt, None, ["bank1"], ["eb"]),
-        query_turns,
-        query_numbers,
-        lambda: ts(T.k32[:], T.tmod[:], 1.0, None, A.min, None, ["tmod"], ["k32"]),
-        lambda: ts(T.diag[:], T.tmod[:], pm, None, A.is_equal, None, ["tmod", "ccol"], ["diag"]),
-        lambda: ts(T.k16[:], T.tmod[:], 1.0, None, A.min, None, ["tmod"], ["k16"])])
+    act(T.e64[:, 3:515:4], T.idn[:], ["idn"], ["e64"])
 
-    quant("e64", 0, 512, T.e64[:], E64, ["e64q"])
-    act(T.q64[:], T.qd[:, 0:256], ["qb"], ["q64"], 64.0)
-    act(T.e05[:], T.e64[:], E64, ["e05"], 0.0078125)
-    fill(T.k32[:, 16:128:32], -1.0, ["k32"])
-    zeros_total()
-    cp(T.st0[:, 0:8:2], lo, ["lk"], ["st0a"])
-    ts(T.st0[:, 1:8:2], lo, 128.0, None, A.add, None, ["lk"], ["st0"])
-    cp(T.stf[:, 0:8:2], lo, ["lk"], ["stfa"])
-    ts(T.stf[:, 1:8:2], lo, 128.0, None, A.add, None, ["lk"], ["stfb"])
-    ts(T.stf[:, 8:12], lo, 128.0, None, A.add, None, ["lk"], ["stfc"])
-    fill(T.stf[:, 12:16], 128.0, ["stf"])
-    ts(T.pre[:, 0:4], kk, -1.0, 128.0, A.mult, A.add, ["lk"], ["pre0"])
-    keep_rest()
+    def later_constants():
+        act(diag, hold, ["hold"], ["diag"], 1.0 / 512)
+        for name in ("k16", "k32"):
+            op("s", lambda: S.activation(T[name][:], tmod, ACT.Sign), ["tmod"], [name])
+        sfill(T.g0[:], 24, 0.0, ["g0z"])
+        sfill(T.k32[:, 16:128:32], 4, -1.0, ["k32"])
+        cp(T.sel[:, 0:1], T.ccol[:, 0:1], ["ccol"], ["sel"])
+
+    turn(T.ccol[:], T.crow[:], ["crow%d" % i for i in range(1, 5)], ["ccol"])
+    bits(0, lambda: cp(T.esel[:, 0:1], T.ccol[:, 32:33], ["ccol"], ["esel"]),
+         lambda: quant("qd", 0, 128, T.t0[:, 768:1280], ["qb", "t0b"], ["qdq"]))
+    bits(1, lambda: held("hi", 0), lambda: held("he", 0))
+    order_and_send(0, [
+        query_scores,
+        lambda: None,
+        lambda: ts(T.eb[:, 16:80], bank(1, 64, 64), 0.0, None, A.is_gt, None, ["bank1"], ["eb"]),
+        query_numbers,
+        later_constants])
+
+    F0 = ["f0%d%d" % (h, b) for h in range(2) for b in range(4)]
+    act(T.e05[:], T.e64[:], ["e64"], ["e05"], 0.0078125)
+    sfill(T.h0[:], 8, 0.0, ["h0"])
+    for b in range(2):
+        act(T.fp[:, 256 * b:256 * b + 256], T.f0[:, b:1024:4], F0, ["fp%d" % b], 0.5)
+    for b in (2, 0, 3, 1):
+        unit("e64", b)
+    cp(T.st0[:], T.stf[:, 0:8], ["stf", "stfr"], ["st0"])
     step(T.st0, "st0", T.so0, "so0", True)
-    send(nxt, T.st1[:], T.so0[:], "st1", ["so0"])
+    send(nxt, T.st1[:, 0:12], T.so0[:, 0:12], "st1", ["so0"])
 
     layer(1)
     for b in range(4):
         act(T.tp1[:, 256 * b:256 * b + 256], T.t1[:, b:1024:4], ["t10%d" % b, "t11%d" % b], ["tp1%d" % b])
     bits(0)
     bits(1, lambda: held("hi", 0), lambda: held("he", 0))
-    order_and_send(1, [
-        lambda: None,
-        zeros_total,
-        lambda: ts(T.km[:], T.kml[:], -128.0, None, A.add, None, ["kml"], ["km"]),
-        lambda: cp(T.stf[:], T.st1[:], ["st1"], ["stf"]),
-        lambda: tt(T.stf[:, 12:16], T.stf[:, 12:16], T.kml[:], A.subtract, ["stf", "kml"], ["stf"]),
-        lambda: tt(T.stf[:, 8:12], T.stf[:, 8:12], T.km[:], A.add, ["stf", "km"], ["stf"]),
-        keep_rest])
-    step(T.st1, "st1", T.so1, "so1", False)
-    send(nxt, T.st2[:], T.so1[:], "st2", ["so1"])
+    order_and_send(1, [])
     send(prv, T.o1l[:], T.ow1[:], "o1", ["ow1"])
-    for name in ("b1", "bt", "xt"):
-        act(T[name][:, 256:512], T.zt[:, 0:256], ["zt"], [name + "z"])
-    fill(T.h0[:], 0.0, ["h0"])
-    quant("e05", 0, 512, T.e05[:], ["e05"], ["e05q"])
+    for b in range(2, 4):
+        act(T.fp[:, 256 * b:256 * b + 256], T.f0[:, b:1024:4], F0, ["fp%d" % b], 0.5)
+    act(T.q64[:], qb, ["qb"], ["q64"], 64.0)
+    cp(T.stf[:], T.st1[:, 0:12], ["st1"], ["stf", "stfr"])
+    unit("e05", 0)
+    tt(T.stf[:, 8:12], T.stf[:, 8:12], T.kml[:], A.subtract, ["stf", "kml"], ["stf"])
+    unit("e05", 1)
+    tt(T.kap[:], T.stf[:, 1:8:2], T.stf[:, 8:12], A.subtract, ["stf"], ["kap"])
+    step(T.st1, "st1", T.so1, "so1", False)
+    send(nxt, T.st2[:, 0:12], T.so1[:, 0:12], "st2", ["so1"])
 
     layer(2)
     mixed = (1, 2, 3, 5)
     for b in range(4):
         mm(mixed[b], [("e64", 128 * b, "t2", 0, 256), ("e64", 128 * b, "l2", 0, 256)],
-           ["e64q", "tq20", "tq21", "ls2", "lqa2", "lqb2"])
-    for b in range(4):
+           ["e64q%d" % b, "tq20", "tq21", "lqa2", "lqb2"])
+
+    def mean(b):
         act(T.b1p[:, 256 * b:256 * b + 256], bank(mixed[b], 256), ["bank%d" % mixed[b]], ["b1p%d" % b], 0.0078125)
-    bits(0)
-    bits(1, lambda: zeros_to(0), lambda: zeros_to(1))
+
+    for b in range(3):
+        mean(b)
+    bits(0, None, lambda: zeros_to(0))
+    bits(1, lambda: ts(T.stf[:], T.st2[:, 0:12], 1.0, None, A.add, None, ["st2"], ["stf", "stfr"]),
+         lambda: tt(T.kap[:], T.stf[:, 1:8:2], T.stf[:, 8:12], A.subtract, ["stf"], ["kap"]))
     picked(T.st2, "st2")
-    cp(T.stf[:, 8:16], T.st2[:, 8:16], ["st2"], ["stf"])
+    ts(T.zc[:], T.kap[:], n1, -257.0, A.add, A.add, ["kap", "rrb"], ["zc"])
     counts()
-    ts(T.zc[:], T.stf[:, 12:16], n1, -256.0, A.add, A.add, ["stf", "rrb"], ["zc"])
-    tt(T.h0[:, 1:8:2], T.s32[:, 31:128:32], T.stf[:, 12:16], A.is_ge, ["s32", "stf"], ["h0"])
-    tt(T.h1[:, 1:8:2], T.stf[:, 8:12], T.s16[:, 15:128:32], A.subtract, ["stf", "s16"], ["h1a"])
-    tt(T.h1[:, 0:8:2], T.s16[:, 31:128:32], T.zc[:], A.subtract, ["zc", "s16"], ["h1b"])
+    zeros_to(1)
+    tt(T.h0[:, 1:8:2], ones_in, T.kap[:], A.is_ge, ["s32", "kap"], ["h0"])
+    tt(T.h1[:, 1:8:2], T.stf[:, 8:12], before_l, A.subtract, ["stf", "s16"], ["h1a"])
+    tt(T.h1[:, 0:8:2], before_r, T.zc[:], A.subtract, ["zc", "s16"], ["h1b"])
     ts(T.arr[:, 256:512], T.rr[:, 1:257], n1, 256.0, A.subtract, A.add, RR, ["arrb"])
     scan(T.pos[:], T.h0[:], T.h1[:], 0.0, A.mult, A.max, ["h0", "h1a", "h1b"], ["pos"])
     ts(T.nd[:, 0:4], T.h0[:, 1:8:2], -256.0, None, A.mult, None, ["h0"], ["nda"])
-    ts(T.acc[:, 1:2], T.pos[:, 7:8], 0.5, None, A.add, None, ["pos"], ["posh"])
-    op("s", lambda: S.activation(T.junk[:], T.arr[:], ACT.Sign, bias=T.acc[:, 1:2], scale=-1.0,
-                                 accum_out=T.acc[:, 0:1]), ["arra", "arrb", "posh"], ["acc"])
+    act(T.nd[:, 7:8], T.h0[:, 7:8], ["h0"], ["ndb"], -256.0, 256.0)
+    op("s", lambda: S.activation(T.junk[:], T.arr[:], ACT.Sign, bias=T.pos[:, 7:8], scale=-1.0009765625,
+                                 accum_out=T.acc[:, 0:1]), ["arra", "arrb", "pos"], ["acc"])
+    act(T.cs[:, 1023:1024], T.acc[:, 0:1], ["acc", "ndb"], ["cs3"], 0.5, T.nd[:, 7:8])
+    mean(3)
     for c in range(3):
-        ts(T.cmp[:, 512 * c:512 * c + 512], T.arr[:], T.pos[:, 2 * c + 1:2 * c + 2], None, A.is_le, None,
+        ts(T.cmp[:, 512 * c:512 * c + 512], T.arr[:], T.pos[:, 2 * c + 1:2 * c + 2], None, A.is_lt, None,
            ["arra", "arrb", "pos"], ["cmp%d" % c])
-    ts(T.nd[:, 4:8], T.h0[:, 1:8:2], -256.0, 256.0, A.mult, A.add, ["h0"], ["ndb"])
     for c in range(3):
         scan(T.cs[:, 256 * c:256 * c + 256], T.cmp[:, 512 * c:512 * c + 256], T.cmp[:, 512 * c + 256:512 * c + 512],
              T.nd[:, c:c + 1], A.add, A.add, ["cmp%d" % c, "nda"], ["cs%d" % c])
-    ts(T.j2[:, 3:4], T.acc[:, 0:1], 0.5, T.nd[:, 7:8], A.mult, A.add, ["acc", "ndb"], ["j2a"])
-    cp(T.j2[:, 0:3], T.cs[:, 255:768:256], ["cs0", "cs1", "cs2"], ["j2"])
-    send(back2, T.j2l[:, 0:4], T.j2[:, 0:4], "j2", ["j2", "j2a"])
+    cp(T.j2[:, 0:4], T.cs[:, 255:1024:256], ["cs0", "cs1", "cs2", "cs3"], ["j2"])
+    send(back2, T.j2l[:, 0:4], T.j2[:, 0:4], "j2", ["j2"])
     for b in (2, 3, 0, 1):
-        (cp if b < 2 else act)(T.b1[:, b:256:4], T.b1p[:, 256 * b:256 * b + 256].indirect(T.j2[:, 0:4]),
-                               ["j2", "j2a", "b1p%d" % b], ["b1%d" % b])
-    quant("b1", 0, 128, T.b1[:], ["b1z"] + ["b1%d" % b for b in range(4)], ["b1q"])
-    send(back2, u8(T.lb_q[:, 0:64]), u8(T.b1_q[:, 0:64]), "bq", ["b1q"])
-    send(back2, T.lb_s[:, 0:64], T.b1_s[:, 0:64], "bs", ["b1q"])
+        (cp if b < 2 else act)(T.t2[:, 1024 + b:1280:4], T.b1p[:, 256 * b:256 * b + 256].indirect(T.j2[:, 0:4]),
+                               ["j2", "b1p%d" % b], ["b1%d" % b])
+    quant("lb", 64, 192, T.t2[:, 768:1280], ["tq21"] + ["b1%d" % b for b in range(4)], ["b1q"])
+    send(back2, u8(T.lb_q[:, 0:64]), u8(T.lb_q[:, 128:192]), "bq", ["b1q"])
+    send(back2, T.lb_s[:, 0:64], T.lb_s[:, 128:192], "bq", ["b1q"])
 
-    F0 = ["f0%d%d" % (h, b) for h in range(2) for b in range(4)]
-    for t in (2, 3, 0, 1):
-        ts(T.o4[:, 16 * t:16 * t + 16], T.o1l[:], 4.0, float(t), A.mult, A.add, ["o1l"], ["o4%d" % t])
-    act(T.x2[:, 512:1024], T.f0[:].indirect(T.o4[:, 32:64]), F0 + ["o42", "o43"], ["x2b"], 0.5)
-    ts(T.x2[:, 0:512], T.f0[:].indirect(T.o4[:, 0:32]), 0.5, None, A.mult, None, F0 + ["o40", "o41"], ["x2a"])
-    act(T.orig[:], T.ob0[:, 16:272].indirect(T.o1l[:]), ["ob0", "o1l"], ["orig"])
-    quant("lb", 64, 192, T.zt[:], ["zt"], ["lbz"])
+    unit("e05", 2)
+    unit("e05", 3)
+    for b in (2, 3, 0, 1):
+        (cp if b < 2 else act)(T.x2[:, 256 * b:256 * b + 256], T.fp[:, 256 * b:256 * b + 256].indirect(T.o1l[:]),
+                               ["o1l", "fp%d" % b], ["x2%d" % b])
+    act(T.orig[:], T.kb[:, obase[0]:obase[0] + 256].indirect(T.o1l[:]), ["ob0", "o1l"], ["orig"])
     quant("v", 0, 128, T.vb[:], ["vb"], ["vq"])
     for b in (2, 3, 0, 1):
         (cp if b < 2 else act)(T.a0h[:, 64 * b:64 * b + 64], T.x2[:, 256 * b:256 * b + 256].indirect(T.j2l[:, 0:4]),
-                               ["in_j2", "x2" + "ab"[b // 2]], ["a0h%d" % b])
+                               ["in_j2", "x2%d" % b], ["a0h%d" % b])
     act(T.arow[:], T.orig[:].indirect(T.j2l[:, 0:4]), ["in_j2", "orig"], ["arow"])
     op("y", lambda: g.sync.dma_start(T.ol[:], T.arow[0:128:16, :]), ["arow"], (), "out")
     for b in range(4):
-        mm(b, [("e05", 128 * b, "lb", 0, 128)], ["e05q", "lbz", "in_bq", "in_bs"])
+        mm(b, [("e05", 128 * b, "lb", 0, 128)], ["e05q%d" % b, "b1q", "in_bq"])
     for b in range(4):
-        tt(T.bt[:, b:256:4], bank(b, 64), T.a0h[:, 64 * b:64 * b + 64], A.add, ["bank%d" % b, "a0h%d" % b], ["bt%d" % b])
-    quant("b", 0, 128, T.bt[:], ["btz"] + ["bt%d" % b for b in range(4)], ["bq"])
-    for b in range(4):
+        tt(T.t1[:, 1024 + b:1280:4], bank(b, 64), T.a0h[:, 64 * b:64 * b + 64], A.add,
+           ["bank%d" % b, "a0h%d" % b], ["bt%d" % b])
+    quant("b", 0, 128, T.t1[:, 768:1280], ["tq11"] + ["bt%d" % b for b in range(4)], ["bq"])
+    for b in (0, 2, 1, 3):
         mm(4 + b, [("w", 128 * b, "b", 0, 128)], ["wq", "ws", "bq"])
-    for b in range(4):
-        tt(T.xp[:, b:256:4], bank(4 + b, 64), T.q64[:, b:256:4], A.add, ["bank%d" % (4 + b), "q64"], ["xp%d" % b])
-    ts(T.xt[:, 0:256], T.xp[:], 0.015625, None, A.mult, None, ["xp%d" % b for b in range(4)], ["xt"])
-    quant("xx", 0, 128, T.xt[:], ["xt", "xtz"], ["xq"])
+    for b in (0, 2, 1, 3):
+        tt(T.xp[:, b:256:4], bank(4 + b, 64, 64), T.q64[:, b:256:4], A.add, ["bank%d" % (4 + b), "q64"], ["xp%d" % b])
+    for b in range(2):
+        ts(T.f1[:, 1024 + b:1280:2], T.xp[:, b:256:2], 0.015625, None, A.mult, None,
+           ["xp%d" % b, "xp%d" % (b + 2)], ["xt%d" % b])
+    quant("xx", 0, 128, T.f1[:, 768:1280], ["fq11", "xt0", "xt1"], ["xq"])
     mm(0, [("v", 0, "xx", 0, 128)], ["vq", "xq"])
-    op("y", lambda: g.sync.dma_start(T.oc[:], u8(T.xx_q[:, 0:64])), ["xq"], (), "out")
+    op("y", lambda: g.sync.dma_start(T.oc[:], u8(T.xx_q[:, 64:128])), ["xq"], (), "out")
     for k in range(4):
-        op("s", lambda: S.dma_start(T.osc[4 * k:4 * k + 4, :], T.xx_s[32 * k:32 * k + 4, 0:64]), ["xq"], (), "out")
-    cp(T.ysb[:], bank(0, 64), ["bank0"], ["ysb"])
+        op("s", lambda: S.dma_start(T.osc[4 * k:4 * k + 4, :], T.xx_s[32 * k:32 * k + 4, 64:128]), ["xq"], (), "out")
+    cp(T.ysb[:], bank(0, 64, 64), ["bank0"], ["ysb"])
     op("y", lambda: g.sync.dma_start(T.y[:], T.ysb[:]), ["ysb"], (), "out")
     for sem in ("cg", "sent", "ct", "cs", "cv", "out"):
         g.wait_ge(T.sem[sem], total[sem])

@@ -8,26 +8,27 @@ for _n, _w in (("u", 128), ("ur", 128), ("t0", 256), ("t1", 256), ("t2", 256), (
     SCRATCH[_n + "_q"] = ("sbuf", [128, _w], X4)
     SCRATCH[_n + "_s"] = ("sbuf", [128, _w], U8)
 for _n, _w in (("ub", 512), ("zb", 512), ("vb", 512), ("t0", 1280), ("t1", 1280), ("t2", 1280), ("tp0", 1024),
-               ("tp1", 1024), ("f0", 1024), ("f1", 1280), ("fp", 1024), ("e64", 520), ("e05", 520), ("c64", 160),
-               ("idn", 128), ("q64", 256), ("b1p", 1024), ("x2", 1024), ("a0h", 256), ("xp", 256),
+               ("tp1", 1024), ("f0", 1024), ("f1", 1280), ("e64", 520), ("e05", 520), ("c64", 160),
+               ("idn", 128), ("q64", 256), ("b1p", 1024), ("a0h", 256), ("xp", 256),
                ("ones", 128), ("kb", 896), ("k16", 128), ("k32", 128), ("kh", 160),
-               ("jrow", 256), ("bit", 256), ("rr", 272), ("hi", 256), ("he", 256),
+               ("jrow", 256), ("bit", 256), ("rr", 272), ("zr", 272), ("own", 256), ("mown", 128), ("h3", 800), ("b3", 800),
                ("ot", 544), ("eb", 96), ("ebt", 160), ("esc", 160), ("gm", 128), ("s16", 128), ("s32", 128),
-               ("orig", 256), ("arr", 512), ("cmp", 1536), ("cs", 1024), ("junk", 512), ("pos", 8), ("nd", 8),
-               ("pm", 32)):
+               ("orig", 256), ("arr", 512), ("cmp", 768), ("cs", 1024), ("junk", 256), ("pos", 16), ("nd", 8),
+               ("pm", 32), ("hb", 272), ("hz", 272), ("yo", 256), ("zt", 256)):
     SCRATCH[_n] = ("sbuf", [128, _w], BF)
-for _n, _w in (("j16", 16), ("jw", 16), ("crow", 64), ("ccol", 64), ("d0", 32), ("d1", 32), ("pp", 32), ("lk", 16),
-               ("stf", 12), ("kap", 4), ("g0", 24), ("g1", 24), ("gg", 24), ("zc", 4), ("h0", 8), ("h1", 8),
+for _n, _w in (("j16", 16), ("crow", 64), ("ccol", 64), ("jm", 16), ("pp", 48), ("lk", 16),
+               ("stf", 12), ("kap", 4), ("g0", 24), ("g1", 24), ("gg", 24), ("zc", 4), ("h0", 12), ("h1", 12),
                ("acc", 4), ("kml", 4), ("arow", 64), ("ysb", 64)):
     SCRATCH[_n] = ("sbuf", [128, _w], F32)
 for _n, _w in (("urep", 8), ("sel", 8), ("esel", 8), ("pw", 16), ("ow0", 16), ("ow1", 16), ("st0", 8), ("so0", 16),
-               ("so1", 16), ("st1", 16), ("st2", 16), ("o1l", 16), ("j2", 8), ("j2l", 8)):
+               ("so1", 16), ("st1", 16), ("st2", 16), ("o1l", 16), ("j2", 8), ("j2l", 8), ("j0", 8)):
     SCRATCH[_n] = ("sbuf", [128, _w], U16)
 SEMAPHORES = ["cv", "cs", "ct", "cg", "sent", "out",
               "ld_u", "ld_xa", "ld_xb", "ld_q", "ld_z", "ld_wc", "ld_ws", "ld_v",
               "a1", "b1", "a2", "b2", "km", "st1", "st2", "o1", "j2", "bq"]
 A = AluOpType
 ACT = ActivationFunctionType
+UNIT = 1.0 / 512
 
 
 def rank_program(g, core, T, topo):
@@ -118,8 +119,8 @@ def rank_program(g, core, T, topo):
         else:
             op("s", lambda: S.activation(out, a, ACT.Copy, scale=scale), r, w)
 
-    def sfill(ap, m, c, w):
-        act(ap, T.c64[:, 0:m], ["c64"], w, c / 64.0)
+    def sfill(ap, m, c, w, r=()):
+        act(ap, T.c64[:, 0:m], ["c64"] + list(r), w, c / 64.0)
 
     def quant(name, a, b, src, r, w):
         op("v", lambda: V.quantize_mx(T[name + "_q"][:, a:b], T[name + "_s"][:, a:b], src), r, w)
@@ -127,11 +128,14 @@ def rank_program(g, core, T, topo):
     def bank(k, m, a=0):
         return T.ps[:, 512 * k + a:512 * k + a + m]
 
-    def mm(k, terms, r):
-        before("t", r, ["bank%d" % k])
+    def mm(k, terms, r, start=True, stop=True):
+        before("t", r, ["bank%d" % k] if start else [])
         for i, (ln, la, rn, ra, rb) in enumerate(terms):
             ins = P.matmul_mx(bank(k, rb - ra), T[ln + "_q"][:, la:la + 128], T[ln + "_s"][:, la:la + 128],
-                              T[rn + "_q"][:, ra:rb], T[rn + "_s"][:, ra:rb], i == 0, i == len(terms) - 1)
+                              T[rn + "_q"][:, ra:rb], T[rn + "_s"][:, ra:rb],
+                              start and i == 0, stop and i == len(terms) - 1)
+        if not stop:
+            return
         ins.then_inc(T.sem.ct, 1)
         total["ct"] = total.get("ct", 0) + 1
         after(("ct", total["ct"], dict(seen["t"]), "t"), r, ["bank%d" % k])
@@ -153,7 +157,7 @@ def rank_program(g, core, T, topo):
 
     qb = T.t0[:, 1024:1280]
     op("y", lambda: g.sync.dma_start(T.ub[:], T.u[:]), (), ["ub"], "ld_u")
-    op("s", lambda: S.dma_start(T.t0[:, 0:512], T.x[:, 0:512]), (), ["t0a"], "ld_xa")
+    op("y", lambda: g.sync.dma_start(T.t0[:, 0:512], T.x[:, 0:512]), (), ["t0a"], "ld_xa")
     op("y", lambda: g.sync.dma_start(T.t0[:, 512:1024], T.x[:, 512:1024]), (), ["t0b"], "ld_xb")
     op("y", lambda: g.sync.dma_start(qb, T.q[:]), (), ["qb"], "ld_q")
     op("y", lambda: g.sync.dma_start(T.zb[:], T.z[:]), (), ["zb"], "ld_z")
@@ -176,11 +180,12 @@ def rank_program(g, core, T, topo):
     op("g", lambda: g.affine_select(T.idn[:], T.c64[:, 0:128], [[-1, 128]], A.is_equal, 0.0, 0, 1), ["c64"], ["idn"])
     sfill(T.kh[:], 160, 0.5, ["kh"])
     sfill(T.ones[:], 128, 1.0, ["ones"])
-    sfill(T.kh[:, 0:160:16], 10, 0.0, ["kh"])
-    sfill(T.rr[:, 0:1], 1, 0.0, ["rr0"])
-    sfill(T.kh[:, 7:160:16], 10, 0.0, ["kh"])
-    sfill(T.d0[:], 32, 0.0, ["d0"])
-    sfill(T.eb[:], 96, 0.0, ["eb"])
+    sfill(T.kh[:, 0:160:16], 10, 0.0, ["kh0"], ["kh"])
+    sfill(T.kh[:, 7:160:16], 10, 0.0, ["kh7"], ["kh"])
+    sfill(T.zr[:, 0:1], 1, -128.0, ["zr0"])
+    sfill(T.b3[:, 45:800:48], 16, 0.0, ["b30"])
+    sfill(T.b3[:, 61:800:48], 16, -2.0, ["b31"])
+    op("s", lambda: S.activation(T.k16[:], tmod, ACT.Sign), ["tmod"], ["k16"])
 
     def unit(name, b):
         quant(name, 128 * b, 128 * b + 128, T[name][:, 3 - b:515 - b], [name], ["%sq%d" % (name, b)])
@@ -189,64 +194,70 @@ def rank_program(g, core, T, topo):
     cp(T.urep[:], T.j16[:, 0:8], ["j16"], ["urep"])
     turn(T.pm[:], T.kb[:, 0:32], ["tmod"], ["pm"])
     ts(hold, tmod, pm, 512.0, A.is_equal, A.mult, ["tmod", "pm"], ["hold"])
-    ts(T.jw[:], T.j16[:], pm, None, A.add, None, ["j16", "pm"], ["jw"])
+    ts(T.jm[:], T.j16[:], pm, -128.0, A.add, A.add, ["j16", "pm"], ["jm"])
+    act(T.mown[:], hold, ["hold"], ["mown"], -2.0 ** 71, 2.0 ** 80)
 
     quant("u", 0, 128, T.ub[:], ["ub"], ["uq"])
+    turn(T.ccol[:], T.crow[:], ["crow%d" % i for i in range(1, 5)], ["ccol"])
     act(T.ur_s[:], T.u_s[:].indirect(T.urep[:]), ["uq", "urep"], ["urs"])
     cp(u32(T.ur_q[:]), u32(T.u_q[:]).indirect(T.urep[:]), ["uq", "urep"], ["urq"])
+    sfill(T.eb[:], 96, 0.0, ["eb"])
+    sfill(T.rr[:, 0:1], 1, 0.0, ["rr0"])
 
     def scores(lv, h):
         mm(4 * h, [("ur", 0, "t%d" % lv, 128 * h, 128 * h + 128)], ["urq", "urs", "tq%d%d" % (lv, h)])
 
-    def bits(h, first=None, second=None):
+    def bits(h):
+        ts(T.bit[:, 128 * h:128 * h + 128], bank(4 * h, 128), 0.0, None, A.is_gt, None,
+           ["bank%d" % (4 * h)], ["bit%d" % h])
+
+    def own_bits(h):
+        tt(T.own[:, 128 * h:128 * h + 128], bank(4 * h, 128), T.mown[:], A.is_gt,
+           ["bank%d" % (4 * h), "mown"], ["own%d" % h])
+
+    def ones_to(h):
         a = 128 * h
-        ts(T.bit[:, a:a + 128], bank(4 * h, 128), 0.0, None, A.is_gt, None, ["bank%d" % (4 * h)], ["bit%d" % h])
-        if first:
-            first()
         scan(T.rr[:, 1 + a:129 + a], T.ones[:], T.bit[:, a:a + 128], T.rr[:, a:a + 1], A.mult, A.add,
              ["ones", "bit%d" % h, "rr0", "rra"] if h else ["ones", "bit0", "rr0"], ["rrb" if h else "rra"])
-        if second:
-            second()
-
-    def held(name, h):
-        a = 128 * h + (1 if name == "hi" else 0)
-        scan(T[name][:, 128 * h:128 * h + 128], hold, T.rr[:, a:a + 128], 0.0, A.add, A.min,
-             ["hold", "rr0", "rra"] + (["rrb"] if h else []), [name + str(h)])
 
     def zeros_to(h):
         a = 128 * h
-        scan(T.arr[:, a:a + 128], T.ones[:], T.bit[:, a:a + 128], T.arr[:, 127:128] if h else 0.0,
-             A.add, A.subtract, ["ones", "bit%d" % h] + (["arr0"] if h else []), ["arra" if h else "arr0"])
+        scan(T.zr[:, 1 + a:129 + a], T.ones[:], T.bit[:, a:a + 128], T.zr[:, a:a + 1], A.add, A.subtract,
+             ["ones", "bit%d" % h, "zr0", "zra"] if h else ["ones", "bit0", "zr0"], ["zrb" if h else "zra"])
+
+    def held(h, s):
+        scan(T.h3[:, 384 * h + s:384 * h + s + 384:3], hold, T.zr[:, 128 * h:128 * h + 128], 0.0, A.add, A.min,
+             ["hold", "zr0", "zra"] + (["zrb"] if h else []), ["h3%d%d" % (h, s)])
+
+    def held_bits(h):
+        scan(T.b3[:, 384 * h + 32:384 * h + 416:3], T.k16[:], T.own[:, 128 * h:128 * h + 128], 0.0, A.mult, A.add,
+             ["k16", "own%d" % h], ["b3%d2" % h])
+
+    def all_zeros():
+        act(T.h3[:, 61:800:48], T.jm[:], ["jm", "zrb"], ["jz"], 1.0, T.zr[:, 256:257])
 
     RR = ["rr0", "rra", "rrb"]
     n1 = T.rr[:, 256:257]
 
-    def order_and_send(lv, spare, parts=1):
+    def order_and_send(lv, spare):
         o, ow, tp, f = obase[lv], T["ow%d" % lv], T["tp%d" % lv], T["f%d" % lv]
         obk, owk = "ob%d" % lv, "ow%d" % lv
         pads = (["tmod", "hold"], ["hold", "diag"])[lv]
 
         def gap():
-            if spare:
-                spare.pop(0)()
+            for call in spare.pop(0):
+                call()
 
-        held("hi", 1)
-        held("he", 1)
+        held(1, 0)
+        held(1, 32)
         gap()
-        inc, exc = T.hi[:, 15:256:16], T.he[:, 15:256:16]
-        ts(T.d1[:, 0:32:2], exc, n1, 256.0, A.subtract, A.add, ["he0", "he1", "rrb"], ["d1a"])
-        tt(T.d1[:, 1:32:2], T.jw[:], inc, A.subtract, ["jw", "hi0", "hi1"], ["d1b"])
-        tt(T.d0[:, 1:32:2], inc, exc, A.subtract, ["hi0", "hi1", "he0", "he1"], ["d0"])
+        scan(T.pp[:], T.b3[:, 45:800:16], T.h3[:, 45:800:16], 0.0, A.mult, A.add,
+             ["b30", "b31", "b302", "b312", "jz", "h300", "h3032", "h310", "h3132"], ["pp"])
         gap()
-        scan(T.pp[:], T.d0[:], T.d1[:], 0.0, A.mult, A.max, ["d0", "d1a", "d1b"], ["pp"])
+        ts(T.pw[:], T.pp[:, 2:48:3], 128.0, None, A.add, None, ["pp"], ["pw"])
         gap()
-        cp(T.pw[:], T.pp[:, 1:32:2], ["pp"], ["pw"])
+        cp(T.kb[:, o:o + 256].indirect(T.pw[:]), T.jrow[:], ["pw", "jrow"], [obk])
         gap()
-        m = 16 // parts
-        for k in range(parts):
-            cp(T.kb[:, o:o + 256].indirect(T.pw[:, m * k:m * k + m]), T.jrow[:, 16 * m * k:16 * m * (k + 1)],
-               ["pw", "jrow"], [obk])
-            gap()
         turn(T.ot[:, 0:288], T.kb[:, o - 16:o + 272], [obk] + pads, ["ota"])
         turn(T.ot[:, 288:544], T.kb[:, o:o + 256], [obk], ["otb"])
         gap()
@@ -275,8 +286,6 @@ def rank_program(g, core, T, topo):
         pack(0)
         gather(1, 1)
         pack(1)
-        while spare:
-            gap()
 
     def picked(lst, key):
         tt(T.gm[:], T.rr[:, 0:257].indirect(lst[:, 0:8]), diag, A.mult, RR + [key, "diag"], ["gm"])
@@ -287,27 +296,26 @@ def rank_program(g, core, T, topo):
 
     ab, before_l, before_r, ones_in = T.s16[:, 15:128:16], T.s16[:, 15:128:32], T.s16[:, 31:128:32], T.s32[:, 31:128:32]
 
-    def step(lst, key, out, okey, first):
-        picked(lst, key)
-        if not first:
-            ts(T.zc[:], T.kap[:], n1, -256.0, A.add, A.add, ["kap", "rrb"], ["zc"])
-        counts()
+    def step(out, okey, first):
         rest = T.lk[:, 4:8] if first else T.kap[:]
         place = T.stf[:, 1:8:2] if first else T.stf[:, 8:12]
-        for i, view in enumerate((T.g0[:, 1:16:4], T.g0[:, 3:16:4], T.g0[:, 17:24:2])):
-            tt(view, ones_in, rest, A.is_ge, ["s32", "kap", "lk", "g0z"], ["g0%d" % i])
-        tt(T.g1[:, 1:16:2], T.stf[:, 0:8], ab, A.subtract, ["stf", "stfr", "s16"], ["g10"])
-        tt(T.g1[:, 17:24:2], place, before_l, A.subtract, ["stf", "stfr", "s16"], ["g11"])
-        ts(T.g1[:, 0:16:2], ab, n1, 256.0, A.subtract, A.add, ["rrb", "s16"], ["g12"])
+        act(T.g1[:, 0:16:2], ab, ["zc", "s16"], ["g12"], 1.0, T.zc[:, 0:1])
         if first:
-            ts(T.g1[:, 16:24:2], before_r, n1, 256.0, A.subtract, A.add, ["rrb", "s16"], ["g13"])
-        else:
-            tt(T.g1[:, 16:24:2], before_r, T.zc[:], A.subtract, ["zc", "s16"], ["g13"])
-        scan(T.gg[:], T.g0[:], T.g1[:], 0.0, A.mult, A.max,
-             ["g0%d" % i for i in range(3)] + ["g1%d" % i for i in range(4)], ["gg"])
-        cp(out[:, 0:12], T.gg[:, 1:24:2], ["gg"], [okey])
+            act(T.g1[:, 16:24:2], before_r, ["zc", "s16"], ["g13"], 1.0, T.zc[:, 0:1])
 
-    def layer(lv):
+        def side(i, view):
+            return lambda: tt(view, ones_in, rest, A.is_ge, ["s32", "kap", "lk", "g0z"], ["g0%d" % i])
+
+        ones = [] if first else [
+            lambda: tt(T.g1[:, 16:24:2], T.g1[:, 2:16:4], T.kap[:], A.subtract, ["g12", "kap"], ["g13"])]
+        return [lambda: tt(T.g1[:, 1:16:2], T.stf[:, 0:8], ab, A.subtract, ["stf", "stfr", "s16"], ["g10"]),
+                lambda: tt(T.g1[:, 17:24:2], place, before_l, A.subtract, ["stf", "stfr", "s16"], ["g11"]),
+                side(0, T.g0[:, 1:16:4]), side(1, T.g0[:, 3:16:4]), side(2, T.g0[:, 17:24:2])] + ones + [
+                lambda: scan(T.gg[:], T.g0[:], T.g1[:], 0.0, A.mult, A.max,
+                             ["g0%d" % i for i in range(3)] + ["g1%d" % i for i in range(4)], ["gg"]),
+                lambda: cp(out[:, 0:12], T.gg[:, 1:24:2], ["gg"], [okey])]
+
+    def layer(lv, idle=None, spare=None):
         t, ln = T["t%d" % lv], "l%d" % lv
         for h in range(2):
             for b in (2, 0, 3, 1):
@@ -316,22 +324,28 @@ def rank_program(g, core, T, topo):
         for h in range(2):
             for b in (2, 0, 3, 1):
                 view, k = t[:, 512 * h + b:512 * h + 512:4], 4 * h + b
-                if b < 2:
+                if b == 1 or (b == 0 and (h or lv == 1)):
                     ts(view, bank(k, 128), 0.015625, None, A.mult, None, ["bank%d" % k], ["t%d%d%d" % (lv, h, b)])
+                    if spare and h and b == 0:
+                        spare()
                 else:
                     act(view, bank(k, 128), ["bank%d" % k], ["t%d%d%d" % (lv, h, b)], 0.015625)
             quant("t%d" % lv, 128 * h, 128 * h + 128, t[:, 512 * h:512 * h + 512],
                   ["t%d%d%d" % (lv, h, b) for b in range(4)], ["tq%d%d" % (lv, h)])
             scores(lv, h)
+            if idle and not h:
+                idle()
 
     def query_scores():
         quant("z", 0, 128, T.zb[:], ["zb"], ["zq"])
         mm(1, [("z", 0, "qd", 0, 128)], ["zq", "qdq"])
 
-    def query_numbers():
+    def query_turns():
         turn(T.ebt[:, 0:96], T.eb[:, 0:96], ["eb"], ["ebta"])
         turn(T.ebt[:, 96:160], T.eb[:, 16:80], ["eb"], ["ebtb"])
-        scan(T.esc[:], T.kh[:], T.ebt[:], 0.0, A.mult, A.add, ["kh", "ebta", "ebtb"], ["esc"])
+
+    def query_numbers():
+        scan(T.esc[:], T.kh[:], T.ebt[:], 0.0, A.mult, A.add, ["kh", "kh0", "kh7", "ebta", "ebtb"], ["esc"])
         act(T.lk[:], T.esc[:].indirect(T.esel[:, 0:1]), ["esc", "esel"], ["lk"], -64.0, 128.0)
         send(nxt, T.kml[:], T.lk[:, 4:8], "km", ["lk"])
         act(T.stf[:, 0:8:2], T.lk[:, 0:4], ["lk"], ["stf"], -1.0, 128.0)
@@ -340,94 +354,146 @@ def rank_program(g, core, T, topo):
     for h in range(2):
         quant("t0", 128 * h, 128 * h + 128, T.t0[:, 512 * h:512 * h + 512], ["t0" + "ab"[h]], ["tq0%d" % h])
         scores(0, h)
-    for b in range(4):
-        act(T.tp0[:, 256 * b:256 * b + 256], T.t0[:, b:1024:4], ["t0a", "t0b"], ["tp0%d" % b])
-    act(T.e64[:, 3:515:4], T.idn[:], ["idn"], ["e64"])
+
+    def planes(lv, bs):
+        for b in bs:
+            act(T["tp%d" % lv][:, 256 * b:256 * b + 256], T["t%d" % lv][:, b:1024:4],
+                ["t10%d" % b, "t11%d" % b] if lv else ["t0a", "t0b"], ["tp%d%d" % (lv, b)])
+
+    planes(0, range(4))
 
     def later_constants():
         act(diag, hold, ["hold"], ["diag"], 1.0 / 512)
-        for name in ("k16", "k32"):
-            op("s", lambda: S.activation(T[name][:], tmod, ACT.Sign), ["tmod"], [name])
+        act(T.e64[:, 3:515:4], T.idn[:], ["idn"], ["e64"])
+        op("s", lambda: S.activation(T.k32[:], tmod, ACT.Sign), ["tmod"], ["k32"])
         sfill(T.g0[:], 24, 0.0, ["g0z"])
         sfill(T.k32[:, 16:128:32], 4, -1.0, ["k32"])
         cp(T.sel[:, 0:1], T.ccol[:, 0:1], ["ccol"], ["sel"])
 
-    turn(T.ccol[:], T.crow[:], ["crow%d" % i for i in range(1, 5)], ["ccol"])
-    bits(0, lambda: cp(T.esel[:, 0:1], T.ccol[:, 32:33], ["ccol"], ["esel"]),
-         lambda: quant("qd", 0, 128, T.t0[:, 768:1280], ["qb", "t0b"], ["qdq"]))
-    bits(1, lambda: held("hi", 0), lambda: held("he", 0))
-    order_and_send(0, [
-        query_scores,
-        lambda: None,
-        lambda: ts(T.eb[:, 16:80], bank(1, 64, 64), 0.0, None, A.is_gt, None, ["bank1"], ["eb"]),
-        query_numbers,
-        later_constants])
+    def query_bits():
+        ts(T.eb[:, 16:80], bank(1, 64, 64), 0.0, None, A.is_gt, None, ["bank1"], ["eb"])
 
-    F0 = ["f0%d%d" % (h, b) for h in range(2) for b in range(4)]
-    act(T.e05[:], T.e64[:], ["e64"], ["e05"], 0.0078125)
-    sfill(T.h0[:], 8, 0.0, ["h0"])
-    for b in range(2):
-        act(T.fp[:, 256 * b:256 * b + 256], T.f0[:, b:1024:4], F0, ["fp%d" % b], 0.5)
-    for b in (2, 0, 3, 1):
+    cp(T.esel[:, 0:1], T.ccol[:, 32:33], ["ccol"], ["esel"])
+    bits(0)
+    quant("qd", 0, 128, T.t0[:, 768:1280], ["qb", "t0b"], ["qdq"])
+    bits(1)
+    zeros_to(0)
+    own_bits(0)
+    query_scores()
+    zeros_to(1)
+    all_zeros()
+    own_bits(1)
+    held_bits(0)
+    held(0, 0)
+    held(0, 32)
+    order_and_send(0, [[lambda: held_bits(1), query_bits], [query_turns], [query_numbers],
+                       [later_constants, lambda: ones_to(0)], [lambda: ones_to(1)], []])
+
+    sfill(T.h0[:, 0:8], 8, 4.0, ["h0"])
+    sfill(T.h0[:, 8:9], 1, -UNIT / 2, ["hend0"])
+    sfill(T.h1[:, 8:9], 1, 4.0, ["hend1"])
+    for name in ("hb", "hz"):
+        sfill(T[name][:, 15:16], 1, 0.0, [name + "pad"])
+    for b in (2, 0, 3):
         unit("e64", b)
     cp(T.st0[:], T.stf[:, 0:8], ["stf", "stfr"], ["st0"])
-    step(T.st0, "st0", T.so0, "so0", True)
-    send(nxt, T.st1[:, 0:12], T.so0[:, 0:12], "st1", ["so0"])
+    unit("e64", 1)
+    act(T.zc[:, 0:1], n1, ["rrb"], ["zc"], -1.0, 256.0)
+    picked(T.st0, "st0")
 
-    layer(1)
-    for b in range(4):
-        act(T.tp1[:, 256 * b:256 * b + 256], T.t1[:, b:1024:4], ["t10%d" % b, "t11%d" % b], ["tp1%d" % b])
+    layer(1, None, counts)
+    later = step(T.so0, "so0", True)
+    later.append(lambda: send(nxt, T.st1[:, 0:12], T.so0[:, 0:12], "st1", ["so0"]))
+    planes(1, range(3))
     bits(0)
-    bits(1, lambda: held("hi", 0), lambda: held("he", 0))
-    order_and_send(1, [])
+    own_bits(0)
+    zeros_to(0)
+    ones_to(0)
+    bits(1)
+    own_bits(1)
+    held_bits(0)
+    zeros_to(1)
+    all_zeros()
+    planes(1, [3])
+    act(T.e05[:], T.e64[:], ["e64"], ["e05"], 0.0078125)
+    act(T.zt[:], T.jrow[:], ["jrow"], ["zt"], 0.0)
+    held(0, 0)
+    held_bits(1)
+    held(0, 32)
+    order_and_send(1, [later[0:3], later[3:5] + [lambda: ones_to(1)], later[5:6], later[6:8], [], []])
     send(prv, T.o1l[:], T.ow1[:], "o1", ["ow1"])
-    for b in range(2, 4):
-        act(T.fp[:, 256 * b:256 * b + 256], T.f0[:, b:1024:4], F0, ["fp%d" % b], 0.5)
     act(T.q64[:], qb, ["qb"], ["q64"], 64.0)
     cp(T.stf[:], T.st1[:, 0:12], ["st1"], ["stf", "stfr"])
-    unit("e05", 0)
+    act(T.zc[:, 0:1], n1, ["rrb"], ["zc"], -1.0, 256.0)
+    picked(T.st1, "st1")
     tt(T.stf[:, 8:12], T.stf[:, 8:12], T.kml[:], A.subtract, ["stf", "kml"], ["stf"])
-    unit("e05", 1)
+    counts()
     tt(T.kap[:], T.stf[:, 1:8:2], T.stf[:, 8:12], A.subtract, ["stf"], ["kap"])
-    step(T.st1, "st1", T.so1, "so1", False)
+    for call in step(T.so1, "so1", False):
+        call()
     send(nxt, T.st2[:, 0:12], T.so1[:, 0:12], "st2", ["so1"])
 
-    layer(2)
     mixed = (1, 2, 3, 5)
-    for b in range(4):
-        mm(mixed[b], [("e64", 128 * b, "t2", 0, 256), ("e64", 128 * b, "l2", 0, 256)],
-           ["e64q%d" % b, "tq20", "tq21", "lqa2", "lqb2"])
+
+    def unpack_f(bs):
+        for b in bs:
+            mm(mixed[b], [("e64", 128 * b, "l2", 0, 256)], ["e64q%d" % b, "lqa2", "lqb2"], stop=False)
 
     def mean(b):
+        if b == 3:
+            unpack_f([b])
+        mm(mixed[b], [("e64", 128 * b, "t2", 0, 256)], ["tq20", "tq21"], start=False)
         act(T.b1p[:, 256 * b:256 * b + 256], bank(mixed[b], 256), ["bank%d" % mixed[b]], ["b1p%d" % b], 0.0078125)
 
+    def half_bits(h, first=None):
+        a = 128 * h
+        hb = T.hb[:, 16 + a:144 + a]
+        ts(hb, bank(4 * h, 128), 0.0, UNIT / 2, A.is_gt, A.mult, ["bank%d" % (4 * h)], ["hb%d" % h])
+        act(T.hz[:, 16 + a:144 + a], hb, ["hb%d" % h], ["hz%d" % h], -1.0, UNIT / 2)
+        if first:
+            first()
+        scan(T.rr[:, 1 + a:129 + a], hb, hb, T.rr[:, a:a + 1], A.add, A.add,
+             ["hb%d" % h, "rr0"] + (["rra"] if h else []), ["rrb" if h else "rra"])
+
+    def mid_counts(out, key, h):
+        a = 128 * h
+        scan(out[:, a:a + 128], T[key][:, 16 + a:144 + a], T[key][:, 15 + a:143 + a],
+             out[:, 127:128] if h else -128 * UNIT, A.add, A.add,
+             [key + "0", key + "1", "y%s0" % key] if h else [key + "0", key + "pad"], ["y%s%d" % (key, h)])
+
+    layer(2, lambda: unpack_f(range(3)))
+    half_bits(0)
+    mid_counts(T.yo, "hb", 0)
+    half_bits(1, lambda: ts(T.stf[:], T.st2[:, 0:12], UNIT, -128 * UNIT, A.mult, A.add, ["st2"], ["stf", "stfr"]))
     for b in range(3):
         mean(b)
-    bits(0, None, lambda: zeros_to(0))
-    bits(1, lambda: ts(T.stf[:], T.st2[:, 0:12], 1.0, None, A.add, None, ["st2"], ["stf", "stfr"]),
-         lambda: tt(T.kap[:], T.stf[:, 1:8:2], T.stf[:, 8:12], A.subtract, ["stf"], ["kap"]))
+    tt(T.kap[:], T.stf[:, 1:8:2], T.stf[:, 8:12], A.subtract, ["stf"], ["kap"])
     picked(T.st2, "st2")
-    ts(T.zc[:], T.kap[:], n1, -257.0, A.add, A.add, ["kap", "rrb"], ["zc"])
+    mid_counts(T.arr, "hz", 0)
+    ts(T.zc[:], T.kap[:], n1, -128 * UNIT, A.add, A.add, ["kap", "rrb"], ["zc"])
     counts()
-    zeros_to(1)
-    tt(T.h0[:, 1:8:2], ones_in, T.kap[:], A.is_ge, ["s32", "kap"], ["h0"])
-    tt(T.h1[:, 1:8:2], T.stf[:, 8:12], before_l, A.subtract, ["stf", "s16"], ["h1a"])
-    tt(T.h1[:, 0:8:2], before_r, T.zc[:], A.subtract, ["zc", "s16"], ["h1b"])
-    ts(T.arr[:, 256:512], T.rr[:, 1:257], n1, 256.0, A.subtract, A.add, RR, ["arrb"])
-    scan(T.pos[:], T.h0[:], T.h1[:], 0.0, A.mult, A.max, ["h0", "h1a", "h1b"], ["pos"])
-    ts(T.nd[:, 0:4], T.h0[:, 1:8:2], -256.0, None, A.mult, None, ["h0"], ["nda"])
-    act(T.nd[:, 7:8], T.h0[:, 7:8], ["h0"], ["ndb"], -256.0, 256.0)
-    op("s", lambda: S.activation(T.junk[:], T.arr[:], ACT.Sign, bias=T.pos[:, 7:8], scale=-1.0009765625,
-                                 accum_out=T.acc[:, 0:1]), ["arra", "arrb", "pos"], ["acc"])
-    act(T.cs[:, 1023:1024], T.acc[:, 0:1], ["acc", "ndb"], ["cs3"], 0.5, T.nd[:, 7:8])
+    mid_counts(T.yo, "hb", 1)
+    tt(T.h0[:, 1:8:2], ones_in, T.kap[:], A.is_lt, ["s32", "kap"], ["h0"])
+    tt(T.h1[:, 1:8:2], before_l, T.stf[:, 8:12], A.subtract, ["stf", "s16"], ["h1a"])
+    tt(T.h1[:, 0:8:2], T.zc[:], before_r, A.subtract, ["zc", "s16"], ["h1b"])
+    mid_counts(T.arr, "hz", 1)
+    ts(T.arr[:, 257:512:2], T.yo[:, 1:256:2], n1, 256 * UNIT, A.subtract, A.add, ["yhb0", "yhb1", "rrb"], ["arrb"])
+    scan(T.pos[:, 0:9], T.h0[:, 0:9], T.h1[:, 0:9], 0.0, A.add, A.min, ["h0", "h1a", "h1b", "hend0", "hend1"], ["pos"])
+    ts(T.nd[:, 0:4], T.h0[:, 1:8:2], -UNIT, UNIT, A.mult, A.add, ["h0"], ["nda"])
+    act(T.nd[:, 7:8], T.h0[:, 7:8], ["h0"], ["ndb"], -128 * UNIT, 128 * UNIT)
+    op("s", lambda: S.activation(T.junk[:], T.arr[:, 1:512:2], ACT.Sign, bias=T.pos[:, 8:9], accum_out=T.acc[:, 0:1]),
+       ["yhz0", "yhz1", "arrb", "pos"], ["acc"])
+    act(T.cs[:, 1023:1024], T.acc[:, 0:1], ["acc", "ndb"], ["cs3"], UNIT / 2, T.nd[:, 7:8])
     mean(3)
     for c in range(3):
-        ts(T.cmp[:, 512 * c:512 * c + 512], T.arr[:], T.pos[:, 2 * c + 1:2 * c + 2], None, A.is_lt, None,
-           ["arra", "arrb", "pos"], ["cmp%d" % c])
+        ts(T.cmp[:, 256 * c:256 * c + 128], T.arr[:, 1:256:2], T.pos[:, 2 * c + 1:2 * c + 2], UNIT, A.add, A.min,
+           ["yhz0", "yhz1", "pos"], ["cmp%da" % c])
+        ts(T.cmp[:, 256 * c + 128:256 * c + 256], T.arr[:, 257:512:2], T.pos[:, 2 * c + 1:2 * c + 2], T.nd[:, c:c + 1],
+           A.add, A.min, ["arrb", "pos", "nda"], ["cmp%db" % c])
     for c in range(3):
-        scan(T.cs[:, 256 * c:256 * c + 256], T.cmp[:, 512 * c:512 * c + 256], T.cmp[:, 512 * c + 256:512 * c + 512],
-             T.nd[:, c:c + 1], A.add, A.add, ["cmp%d" % c, "nda"], ["cs%d" % c])
-    cp(T.j2[:, 0:4], T.cs[:, 255:1024:256], ["cs0", "cs1", "cs2", "cs3"], ["j2"])
+        scan(T.cs[:, 256 * c:256 * c + 256], T.cmp[:, 256 * c:256 * c + 256], T.zt[:], 0.0, A.add, A.max,
+             ["cmp%da" % c, "cmp%db" % c, "zt"], ["cs%d" % c])
+    ts(T.j2[:, 0:4], T.cs[:, 255:1024:256], -2 / UNIT, 256.0, A.mult, A.add, ["cs0", "cs1", "cs2", "cs3"], ["j2"])
     send(back2, T.j2l[:, 0:4], T.j2[:, 0:4], "j2", ["j2"])
     for b in (2, 3, 0, 1):
         (cp if b < 2 else act)(T.t2[:, 1024 + b:1280:4], T.b1p[:, 256 * b:256 * b + 256].indirect(T.j2[:, 0:4]),
@@ -436,17 +502,22 @@ def rank_program(g, core, T, topo):
     send(back2, u8(T.lb_q[:, 0:64]), u8(T.lb_q[:, 128:192]), "bq", ["b1q"])
     send(back2, T.lb_s[:, 0:64], T.lb_s[:, 128:192], "bq", ["b1q"])
 
+    act(T.orig[:], T.kb[:, obase[0]:obase[0] + 256].indirect(T.o1l[:]), ["ob0", "o1l"], ["orig"])
+    unit("e05", 0)
+    unit("e05", 1)
+    act(T.arow[:], T.orig[:].indirect(T.j2l[:, 0:4]), ["in_j2", "orig"], ["arow"])
+    tt(T.gm[:, 0:64], T.orig[:].indirect(T.j2l[:, 0:4]), T.kb[:, 768:832], A.mult, ["in_j2", "orig", "diag"], ["gm"])
     unit("e05", 2)
+    scan(T.s16[:, 0:64], T.k16[:, 0:64], T.gm[:, 0:64], 0.0, A.mult, A.add, ["k16", "gm"], ["s16"])
+    cp(T.j0[:, 0:4], T.s16[:, 15:64:16], ["s16"], ["j0"])
     unit("e05", 3)
     for b in (2, 3, 0, 1):
-        (cp if b < 2 else act)(T.x2[:, 256 * b:256 * b + 256], T.fp[:, 256 * b:256 * b + 256].indirect(T.o1l[:]),
-                               ["o1l", "fp%d" % b], ["x2%d" % b])
-    act(T.orig[:], T.kb[:, obase[0]:obase[0] + 256].indirect(T.o1l[:]), ["ob0", "o1l"], ["orig"])
+        view, picks = T.a0h[:, 64 * b:64 * b + 64], T.tp0[:, 256 * b:256 * b + 256].indirect(T.j0[:, 0:4])
+        if b < 2:
+            ts(view, picks, 0.5, None, A.mult, None, ["j0", "tp0%d" % b], ["a0h%d" % b])
+        else:
+            act(view, picks, ["j0", "tp0%d" % b], ["a0h%d" % b], 0.5)
     quant("v", 0, 128, T.vb[:], ["vb"], ["vq"])
-    for b in (2, 3, 0, 1):
-        (cp if b < 2 else act)(T.a0h[:, 64 * b:64 * b + 64], T.x2[:, 256 * b:256 * b + 256].indirect(T.j2l[:, 0:4]),
-                               ["in_j2", "x2%d" % b], ["a0h%d" % b])
-    act(T.arow[:], T.orig[:].indirect(T.j2l[:, 0:4]), ["in_j2", "orig"], ["arow"])
     op("y", lambda: g.sync.dma_start(T.ol[:], T.arow[0:128:16, :]), ["arow"], (), "out")
     for b in range(4):
         mm(b, [("e05", 128 * b, "lb", 0, 128)], ["e05q%d" % b, "b1q", "in_bq"])

@@ -4,31 +4,31 @@ X4, U8, BF, F32, U16 = "float8_e4m3fn_x4", "uint8", "bfloat16", "float32", "uint
 SCRATCH = {"ps": ("psum", [128, 4096], F32)}
 for _n, _w in (("u", 128), ("ur", 128), ("t0", 256), ("t1", 256), ("t2", 256), ("f0", 256), ("f1", 256),
                ("l1", 256), ("l2", 256), ("w", 512), ("e64", 512), ("e05", 512), ("z", 128), ("qd", 128),
-               ("v", 128), ("lb", 192), ("b", 128), ("xx", 128)):
+               ("v", 128), ("lb", 192), ("b", 128), ("xx", 128), ("xo", 64)):
     SCRATCH[_n + "_q"] = ("sbuf", [128, _w], X4)
     SCRATCH[_n + "_s"] = ("sbuf", [128, _w], U8)
-for _n, _w in (("ub", 512), ("zb", 512), ("vb", 512), ("t0", 1280), ("t1", 1280), ("t2", 1280), ("tp0", 1024),
-               ("tp1", 1024), ("f0", 1024), ("f1", 1280), ("e64", 520), ("e05", 520), ("c64", 160),
-               ("idn", 128), ("q64", 256), ("b1p", 1024), ("a0h", 256), ("xp", 256),
-               ("ones", 128), ("kb", 896), ("k16", 128), ("k32", 128), ("kh", 160),
-               ("jrow", 256), ("bit", 256), ("rr", 272), ("zr", 272), ("own", 256), ("mown", 128), ("h3", 800), ("b3", 800),
-               ("ot", 544), ("eb", 96), ("ebt", 160), ("esc", 160), ("gm", 128), ("s16", 128), ("s32", 128),
-               ("orig", 256), ("arr", 512), ("cmp", 768), ("cs", 1024), ("junk", 256), ("pos", 16), ("nd", 8),
-               ("pm", 32), ("hb", 272), ("hz", 272), ("yo", 256), ("zt", 256)):
+for _n, _w in (("ub", 512), ("zb", 512), ("vb", 512), ("t0", 1280), ("t1", 1024), ("t2", 1280), ("tp0", 1024),
+               ("tp1", 1024), ("f0", 1024), ("f1", 1024), ("bt", 512), ("qi", 384), ("e64", 520), ("e05", 520), ("c64", 160),
+               ("idn", 128), ("q64", 128), ("b1p", 1024), ("a0h", 256), ("xp", 128),
+               ("kb", 384), ("k16", 128), ("k32", 128), ("kh", 160),
+               ("jrow", 256), ("bit", 256), ("rr", 272), ("zr", 272), ("last", 128), ("drop", 128), ("dg", 32),
+               ("h5", 1344), ("b5", 1344), ("ot", 256), ("ob0", 256), ("ob1", 256), ("jfrac", 256), ("grip", 128), ("und", 32),
+               ("eb", 96), ("ebt", 160), ("esc", 160), ("gm", 128), ("s16", 128), ("s32", 128), ("orig", 256),
+               ("cmp", 768), ("cs", 768), ("junk", 256), ("pos", 16), ("pm", 32), ("hb", 272), ("hz", 272),
+               ("yo", 256), ("yz", 256), ("zt", 128), ("pp", 80)):
     SCRATCH[_n] = ("sbuf", [128, _w], BF)
-for _n, _w in (("j16", 16), ("crow", 64), ("ccol", 64), ("jm", 16), ("pp", 48), ("lk", 16),
-               ("stf", 12), ("kap", 4), ("g0", 24), ("g1", 24), ("gg", 24), ("zc", 4), ("h0", 12), ("h1", 12),
+for _n, _w in (("j16", 16), ("crow", 32), ("ccol", 32), ("undo", 16), ("jm", 16), ("lk", 16),
+               ("stf", 12), ("kap", 4), ("g0", 24), ("g1", 24), ("gg", 24), ("zc", 4), ("pk", 8),
                ("acc", 4), ("kml", 4), ("arow", 64), ("ysb", 64)):
     SCRATCH[_n] = ("sbuf", [128, _w], F32)
-for _n, _w in (("urep", 8), ("sel", 8), ("esel", 8), ("pw", 16), ("ow0", 16), ("ow1", 16), ("st0", 8), ("so0", 16),
-               ("so1", 16), ("st1", 16), ("st2", 16), ("o1l", 16), ("j2", 8), ("j2l", 8), ("j0", 8)):
+for _n, _w in (("urep", 8), ("esel", 8), ("pw", 16), ("ow0", 16), ("ow1", 16), ("st0", 8), ("so0", 16),
+               ("so1", 16), ("st1", 16), ("st2", 16), ("o1l", 16), ("j2", 8), ("j2l", 8), ("j0", 8), ("odd", 8)):
     SCRATCH[_n] = ("sbuf", [128, _w], U16)
 SEMAPHORES = ["cv", "cs", "ct", "cg", "sent", "out",
               "ld_u", "ld_xa", "ld_xb", "ld_q", "ld_z", "ld_wc", "ld_ws", "ld_v",
               "a1", "b1", "a2", "b2", "km", "st1", "st2", "o1", "j2", "bq"]
 A = AluOpType
 ACT = ActivationFunctionType
-UNIT = 1.0 / 512
 
 
 def rank_program(g, core, T, topo):
@@ -165,110 +165,106 @@ def rank_program(g, core, T, topo):
     op("y", lambda: g.sync.dma_start(T.w_s[:], T.ws[:]), (), ["ws"], "ld_ws")
     op("y", lambda: g.sync.dma_start(T.vb[:], T.v[:]), (), ["vb"], "ld_v")
 
-    tmod, hold, diag = T.kb[:, 0:128], T.kb[:, 384:512], T.kb[:, 768:896]
-    obase = (128, 512)
+    tmod, hold, diag = T.kb[:, 0:128], T.kb[:, 128:256], T.kb[:, 256:384]
     fill(T.c64[:], 64.0, ["c64"])
-    fill(T.crow[:, 32:64], 0.0, ["crow3", "crow4"])
+    fill(T.crow[:], 0.0, ["crow3", "crow4"])
     fill(T.e64[:], 0.0, ["e64"])
-    iota(T.j16[:], [[16, 16]], 0, ["j16"])
     iota(tmod, [[0, 8], [1, 16]], 0, ["tmod"])
-    iota(T.crow[:, 0:16], [[32, 8], [-256, 2]], 288, ["crow1"])
-    iota(T.crow[:, 16:32], [[32, 8], [288, 2]], 16, ["crow2"])
-    iota(T.crow[:, 32:40], [[7, 2], [32, 2], [-64, 2]], 102, ["crow3"])
-    iota(T.crow[:, 48:56], [[7, 2], [32, 2], [96, 2]], 22, ["crow4"])
-    iota(T.jrow[:], [[1, 256]], 0, ["jrow"])
+    iota(T.j16[:], [[16, 16]], 0, ["j16"])
+    iota(T.crow[:, 0:8], [[7, 2], [32, 2], [-64, 2]], 102, ["crow3"])
+    iota(T.crow[:, 16:24], [[7, 2], [32, 2], [96, 2]], 22, ["crow4"])
+    iota(T.jrow[:], [[1, 256]], 1, ["jrow"])
     op("g", lambda: g.affine_select(T.idn[:], T.c64[:, 0:128], [[-1, 128]], A.is_equal, 0.0, 0, 1), ["c64"], ["idn"])
     sfill(T.kh[:], 160, 0.5, ["kh"])
-    sfill(T.ones[:], 128, 1.0, ["ones"])
+    STEPS = []
+    for name, i, c in (("b5", 0, 0.0), ("b5", 1, -2.0), ("b5", 3, -2.0), ("b5", 4, 0.5), ("h5", 2, 0.0), ("h5", 4, 0.0)):
+        STEPS.append("%sc%d" % (name, i))
+        sfill(T[name][:, 75 + 16 * i:1344:80], 16, c, STEPS[-1:])
     sfill(T.kh[:, 0:160:16], 10, 0.0, ["kh0"], ["kh"])
     sfill(T.kh[:, 7:160:16], 10, 0.0, ["kh7"], ["kh"])
-    sfill(T.zr[:, 0:1], 1, -128.0, ["zr0"])
-    sfill(T.b3[:, 45:800:48], 16, 0.0, ["b30"])
-    sfill(T.b3[:, 61:800:48], 16, -2.0, ["b31"])
-    op("s", lambda: S.activation(T.k16[:], tmod, ACT.Sign), ["tmod"], ["k16"])
+    sfill(T.dg[:, 0:1], 1, 0.0, ["dg0"])
+    sfill(T.rr[:, 0:1], 1, 0.0, ["rr0"])
 
     def unit(name, b):
         quant(name, 128 * b, 128 * b + 128, T[name][:, 3 - b:515 - b], [name], ["%sq%d" % (name, b)])
 
     pm = T.pm[:, 0:1]
-    cp(T.urep[:], T.j16[:, 0:8], ["j16"], ["urep"])
     turn(T.pm[:], T.kb[:, 0:32], ["tmod"], ["pm"])
+    cp(T.urep[:], T.j16[:, 0:8], ["j16"], ["urep"])
     ts(hold, tmod, pm, 512.0, A.is_equal, A.mult, ["tmod", "pm"], ["hold"])
-    ts(T.jm[:], T.j16[:], pm, -128.0, A.add, A.add, ["j16", "pm"], ["jm"])
-    act(T.mown[:], hold, ["hold"], ["mown"], -2.0 ** 71, 2.0 ** 80)
+    ts(T.dg[:, 1:17], T.kb[:, 0:16], pm, None, A.is_equal, None, ["tmod", "pm"], ["dg"])
+    ts(T.jm[:], T.j16[:], pm, -256.0, A.add, A.add, ["j16", "pm"], ["jm"])
+    act(T.dg[:, 18:19], T.dg[:, 16:17], ["dg"], ["shift"], -1.0, 0.5)
 
     quant("u", 0, 128, T.ub[:], ["ub"], ["uq"])
-    turn(T.ccol[:], T.crow[:], ["crow%d" % i for i in range(1, 5)], ["ccol"])
+    tt(T.drop[:, 0:16], T.kb[:, 128:144], T.dg[:, 0:16], A.subtract, ["hold", "dg", "dg0"], ["drop16"])
+    turn(T.ccol[:], T.crow[:], ["crow3", "crow4"], ["ccol"])
     act(T.ur_s[:], T.u_s[:].indirect(T.urep[:]), ["uq", "urep"], ["urs"])
     cp(u32(T.ur_q[:]), u32(T.u_q[:]).indirect(T.urep[:]), ["uq", "urep"], ["urq"])
+    act(T.drop[:, 16:32], T.drop[:, 0:16], ["drop16"], ["drop32"])
+    act(T.last[:], tmod, ["tmod", "shift"], ["last"], 0.0, T.dg[:, 18:19])
+    act(T.drop[:, 32:64], T.drop[:, 0:32], ["drop16", "drop32"], ["drop64"])
     sfill(T.eb[:], 96, 0.0, ["eb"])
-    sfill(T.rr[:, 0:1], 1, 0.0, ["rr0"])
+    act(T.drop[:, 64:128], T.drop[:, 0:64], ["drop16", "drop32", "drop64"], ["drop"])
 
     def scores(lv, h):
         mm(4 * h, [("ur", 0, "t%d" % lv, 128 * h, 128 * h + 128)], ["urq", "urs", "tq%d%d" % (lv, h)])
 
     def bits(h):
-        ts(T.bit[:, 128 * h:128 * h + 128], bank(4 * h, 128), 0.0, None, A.is_gt, None,
-           ["bank%d" % (4 * h)], ["bit%d" % h])
-
-    def own_bits(h):
-        tt(T.own[:, 128 * h:128 * h + 128], bank(4 * h, 128), T.mown[:], A.is_gt,
-           ["bank%d" % (4 * h), "mown"], ["own%d" % h])
+        ts(T.bit[:, 128 * h:128 * h + 128], bank(4 * h, 128), 0.0, T.dg[:, 18:19], A.is_gt, A.add,
+           ["bank%d" % (4 * h), "shift"], ["bit%d" % h])
 
     def ones_to(h):
         a = 128 * h
-        scan(T.rr[:, 1 + a:129 + a], T.ones[:], T.bit[:, a:a + 128], T.rr[:, a:a + 1], A.mult, A.add,
-             ["ones", "bit%d" % h, "rr0", "rra"] if h else ["ones", "bit0", "rr0"], ["rrb" if h else "rra"])
+        scan(T.rr[:, 1 + a:129 + a], T.bit[:, a:a + 128], T.last[:], T.rr[:, a:a + 1], A.add, A.subtract,
+             ["last", "bit%d" % h, "rr0", "rra"] if h else ["last", "bit0", "rr0"], ["rrb" if h else "rra"])
 
-    def zeros_to(h):
-        a = 128 * h
-        scan(T.zr[:, 1 + a:129 + a], T.ones[:], T.bit[:, a:a + 128], T.zr[:, a:a + 1], A.add, A.subtract,
-             ["ones", "bit%d" % h, "zr0", "zra"] if h else ["ones", "bit0", "zr0"], ["zrb" if h else "zra"])
-
-    def held(h, s):
-        scan(T.h3[:, 384 * h + s:384 * h + s + 384:3], hold, T.zr[:, 128 * h:128 * h + 128], 0.0, A.add, A.min,
-             ["hold", "zr0", "zra"] + (["zrb"] if h else []), ["h3%d%d" % (h, s)])
+    def held(h):
+        scan(T.h5[:, 640 * h:640 * h + 640:5], hold, T.rr[:, 128 * h:128 * h + 128], 0.0, A.add, A.min,
+             ["hold", "rr0", "rra"] + (["rrb"] if h else []), ["h5%d" % h])
 
     def held_bits(h):
-        scan(T.b3[:, 384 * h + 32:384 * h + 416:3], T.k16[:], T.own[:, 128 * h:128 * h + 128], 0.0, A.mult, A.add,
-             ["k16", "own%d" % h], ["b3%d2" % h])
+        scan(T.b5[:, 640 * h + 32:640 * h + 672:5], T.drop[:], T.bit[:, 128 * h:128 * h + 128], 0.0, A.add, A.min,
+             ["drop", "bit%d" % h], ["b5%d" % h])
 
-    def all_zeros():
-        act(T.h3[:, 61:800:48], T.jm[:], ["jm", "zrb"], ["jz"], 1.0, T.zr[:, 256:257])
+    def less_zeros():
+        for s in (91, 123):
+            act(T.h5[:, s:1344:80], T.jm[:], ["jm", "rrb"], ["jz%d" % s], 1.0, T.rr[:, 256:257])
 
     RR = ["rr0", "rra", "rrb"]
     n1 = T.rr[:, 256:257]
 
     def order_and_send(lv, spare):
-        o, ow, tp, f = obase[lv], T["ow%d" % lv], T["tp%d" % lv], T["f%d" % lv]
+        ob, ow, tp, f = T["ob%d" % lv], T["ow%d" % lv], T["tp%d" % lv], T["f%d" % lv]
         obk, owk = "ob%d" % lv, "ow%d" % lv
-        pads = (["tmod", "hold"], ["hold", "diag"])[lv]
 
         def gap():
             for call in spare.pop(0):
                 call()
 
-        held(1, 0)
-        held(1, 32)
+        held(1)
         gap()
-        scan(T.pp[:], T.b3[:, 45:800:16], T.h3[:, 45:800:16], 0.0, A.mult, A.add,
-             ["b30", "b31", "b302", "b312", "jz", "h300", "h3032", "h310", "h3132"], ["pp"])
+        scan(T.pp[:], T.b5[:, 75:1344:16], T.h5[:, 75:1344:16], 0.0, A.mult, A.add,
+             STEPS + ["b50", "b51", "jz91", "jz123", "h50", "h51"], ["pp"])
         gap()
-        ts(T.pw[:], T.pp[:, 2:48:3], 128.0, None, A.add, None, ["pp"], ["pw"])
+        ts(T.pw[:], T.pp[:, 4:80:5], n1, 256.0, A.subtract, A.add, ["pp", "rrb"], ["pw"])
         gap()
-        cp(T.kb[:, o:o + 256].indirect(T.pw[:]), T.jrow[:], ["pw", "jrow"], [obk])
+        cp(ob[:].indirect(T.pw[:]), T.jfrac[:], ["pw", "jfrac"], [obk])
         gap()
-        turn(T.ot[:, 0:288], T.kb[:, o - 16:o + 272], [obk] + pads, ["ota"])
-        turn(T.ot[:, 288:544], T.kb[:, o:o + 256], [obk], ["otb"])
+        for h in range(2):
+            scan(T.ot[:, 128 * h:128 * h + 128], T.grip[:], ob[:, 128 * h:128 * h + 128], 0.0, A.mult, A.max,
+                 ["grip", obk], ["ot%d" % h])
         gap()
-        cp(ow[:], T.ot[:].indirect(T.sel[:, 0:1]), ["ota", "otb", "sel"], [owk])
+        for h in range(2):
+            ts(ow[:, 8 * h:8 * h + 8], T.ot[:, 128 * h + 15:128 * h + 128:16], T.undo[:, 15:16], -1.0, A.mult, A.add,
+               ["ot%d" % h, "undo"], [owk + str(h)])
         gap()
         fq, fs, lq, ls = T["f%d_q" % lv], T["f%d_s" % lv], T["l%d_q" % (lv + 1)], T["l%d_s" % (lv + 1)]
 
         def gather(h, b):
             (cp if b < 2 else act)(f[:, 512 * h + b:512 * h + 512:4],
                                    tp[:, 256 * b:256 * b + 256].indirect(ow[:, 8 * h:8 * h + 8]),
-                                   [owk, "tp%d%d" % (lv, b)], ["f%d%d%d" % (lv, h, b)])
+                                   [owk + str(h), "tp%d%d" % (lv, b)], ["f%d%d%d" % (lv, h, b)])
 
         def pack(h):
             a, sem = 128 * h, "%s%d" % ("ab"[h], lv + 1)
@@ -291,8 +287,8 @@ def rank_program(g, core, T, topo):
         tt(T.gm[:], T.rr[:, 0:257].indirect(lst[:, 0:8]), diag, A.mult, RR + [key, "diag"], ["gm"])
 
     def counts():
-        scan(T.s32[:], T.k32[:], T.gm[:], 0.0, A.mult, A.add, ["k32", "gm"], ["s32"])
         scan(T.s16[:], T.k16[:], T.gm[:], 0.0, A.mult, A.add, ["k16", "gm"], ["s16"])
+        scan(T.s32[:], T.k32[:], T.gm[:], 0.0, A.mult, A.add, ["k32", "gm"], ["s32"])
 
     ab, before_l, before_r, ones_in = T.s16[:, 15:128:16], T.s16[:, 15:128:32], T.s16[:, 31:128:32], T.s32[:, 31:128:32]
 
@@ -315,19 +311,18 @@ def rank_program(g, core, T, topo):
                              ["g0%d" % i for i in range(3)] + ["g1%d" % i for i in range(4)], ["gg"]),
                 lambda: cp(out[:, 0:12], T.gg[:, 1:24:2], ["gg"], [okey])]
 
-    def layer(lv, idle=None, spare=None):
+    def layer(lv, idle=None):
         t, ln = T["t%d" % lv], "l%d" % lv
+        turns = ((2, 0, 3, 1), (2, 3, 0, 1))
         for h in range(2):
-            for b in (2, 0, 3, 1):
+            for b in turns[h]:
                 mm(4 * h + b, [("w", 128 * b, ln, 128 * h, 128 * h + 128), ("e64", 128 * b, ln, 128 * h, 128 * h + 128)],
                    ["wq", "ws", "e64q%d" % b, "lq%s%d" % ("ab"[h], lv)])
         for h in range(2):
-            for b in (2, 0, 3, 1):
+            for b in turns[h]:
                 view, k = t[:, 512 * h + b:512 * h + 512:4], 4 * h + b
                 if b == 1 or (b == 0 and (h or lv == 1)):
                     ts(view, bank(k, 128), 0.015625, None, A.mult, None, ["bank%d" % k], ["t%d%d%d" % (lv, h, b)])
-                    if spare and h and b == 0:
-                        spare()
                 else:
                     act(view, bank(k, 128), ["bank%d" % k], ["t%d%d%d" % (lv, h, b)], 0.015625)
             quant("t%d" % lv, 128 * h, 128 * h + 128, t[:, 512 * h:512 * h + 512],
@@ -348,8 +343,6 @@ def rank_program(g, core, T, topo):
         scan(T.esc[:], T.kh[:], T.ebt[:], 0.0, A.mult, A.add, ["kh", "kh0", "kh7", "ebta", "ebtb"], ["esc"])
         act(T.lk[:], T.esc[:].indirect(T.esel[:, 0:1]), ["esc", "esel"], ["lk"], -64.0, 128.0)
         send(nxt, T.kml[:], T.lk[:, 4:8], "km", ["lk"])
-        act(T.stf[:, 0:8:2], T.lk[:, 0:4], ["lk"], ["stf"], -1.0, 128.0)
-        act(T.stf[:, 1:8:2], T.lk[:, 0:4], ["lk"], ["stfr"], -1.0, 256.0)
 
     for h in range(2):
         quant("t0", 128 * h, 128 * h + 128, T.t0[:, 512 * h:512 * h + 512], ["t0" + "ab"[h]], ["tq0%d" % h])
@@ -360,38 +353,42 @@ def rank_program(g, core, T, topo):
             act(T["tp%d" % lv][:, 256 * b:256 * b + 256], T["t%d" % lv][:, b:1024:4],
                 ["t10%d" % b, "t11%d" % b] if lv else ["t0a", "t0b"], ["tp%d%d" % (lv, b)])
 
-    planes(0, range(4))
+    planes(0, [2, 3])
 
     def later_constants():
-        act(diag, hold, ["hold"], ["diag"], 1.0 / 512)
-        act(T.e64[:, 3:515:4], T.idn[:], ["idn"], ["e64"])
-        op("s", lambda: S.activation(T.k32[:], tmod, ACT.Sign), ["tmod"], ["k32"])
-        sfill(T.g0[:], 24, 0.0, ["g0z"])
-        sfill(T.k32[:, 16:128:32], 4, -1.0, ["k32"])
-        cp(T.sel[:, 0:1], T.ccol[:, 0:1], ["ccol"], ["sel"])
+        planes(0, [0, 1])
+        scan(T.undo[:], T.und[:, 0:16], T.und[:, 16:32], 0.0, A.mult, A.add, ["und0", "und1"], ["undo"])
 
     def query_bits():
         ts(T.eb[:, 16:80], bank(1, 64, 64), 0.0, None, A.is_gt, None, ["bank1"], ["eb"])
 
-    cp(T.esel[:, 0:1], T.ccol[:, 32:33], ["ccol"], ["esel"])
-    bits(0)
+    cp(T.esel[:, 0:1], T.ccol[:, 0:1], ["ccol"], ["esel"])
     quant("qd", 0, 128, T.t0[:, 768:1280], ["qb", "t0b"], ["qdq"])
+    bits(0)
     bits(1)
-    zeros_to(0)
-    own_bits(0)
+    ones_to(0)
     query_scores()
-    zeros_to(1)
-    all_zeros()
-    own_bits(1)
     held_bits(0)
-    held(0, 0)
-    held(0, 32)
-    order_and_send(0, [[lambda: held_bits(1), query_bits], [query_turns], [query_numbers],
-                       [later_constants, lambda: ones_to(0)], [lambda: ones_to(1)], []])
+    ones_to(1)
+    less_zeros()
+    act(T.jfrac[:], T.jrow[:], ["jrow"], ["jfrac"], 1.0 / 256)
+    act(T.grip[:], hold, ["hold"], ["grip"], -0.5, 256.0)
+    act(T.und[:, 0:16], T.kb[:, 128:144], ["hold"], ["und0"], -1.0 / 512 / 256, 1.0 / 256)
+    act(T.und[:, 16:32], T.kb[:, 128:144], ["hold"], ["und1"], 0.5)
+    act(T.e64[:, 3:515:4], T.idn[:], ["idn"], ["e64"])
+    held_bits(1)
+    held(0)
+    order_and_send(0, [[query_bits], [query_turns], [query_numbers], [later_constants], [], []])
 
-    sfill(T.h0[:, 0:8], 8, 4.0, ["h0"])
-    sfill(T.h0[:, 8:9], 1, -UNIT / 2, ["hend0"])
-    sfill(T.h1[:, 8:9], 1, 4.0, ["hend1"])
+    act(T.stf[:, 0:8:2], T.lk[:, 0:4], ["lk"], ["stf"], -1.0, 128.0)
+    act(T.stf[:, 1:8:2], T.lk[:, 0:4], ["lk"], ["stfr"], -1.0, 256.0)
+    act(diag, hold, ["hold"], ["diag"], 1.0 / 512)
+    op("s", lambda: S.activation(T.k32[:], tmod, ACT.Sign), ["tmod"], ["k32"])
+    op("s", lambda: S.activation(T.k16[:], tmod, ACT.Sign), ["tmod"], ["k16"])
+    sfill(T.k32[:, 16:128:32], 4, -1.0, ["k32"])
+    sfill(T.g0[:], 24, 0.0, ["g0z"])
+    sfill(T.zr[:, 0:1], 1, -128.0, ["zr0"])
+    sfill(T.zt[:], 128, 0.0, ["zt"])
     for name in ("hb", "hz"):
         sfill(T[name][:, 15:16], 1, 0.0, [name + "pad"])
     for b in (2, 0, 3):
@@ -400,31 +397,36 @@ def rank_program(g, core, T, topo):
     unit("e64", 1)
     act(T.zc[:, 0:1], n1, ["rrb"], ["zc"], -1.0, 256.0)
     picked(T.st0, "st0")
+    fill(T.bt[:, 0:256], 0.0, ["btz0"])
+    counts()
+    fill(T.bt[:, 256:512], 0.0, ["btz"])
 
-    layer(1, None, counts)
+    layer(1)
     later = step(T.so0, "so0", True)
     later.append(lambda: send(nxt, T.st1[:, 0:12], T.so0[:, 0:12], "st1", ["so0"]))
     planes(1, range(3))
     bits(0)
-    own_bits(0)
-    zeros_to(0)
+    for call in later[0:3]:
+        call()
     ones_to(0)
     bits(1)
-    own_bits(1)
     held_bits(0)
-    zeros_to(1)
-    all_zeros()
+    held(0)
+    ones_to(1)
+    less_zeros()
     planes(1, [3])
     act(T.e05[:], T.e64[:], ["e64"], ["e05"], 0.0078125)
-    act(T.zt[:], T.jrow[:], ["jrow"], ["zt"], 0.0)
-    held(0, 0)
     held_bits(1)
-    held(0, 32)
-    order_and_send(1, [later[0:3], later[3:5] + [lambda: ones_to(1)], later[5:6], later[6:8], [], []])
-    send(prv, T.o1l[:], T.ow1[:], "o1", ["ow1"])
-    act(T.q64[:], qb, ["qb"], ["q64"], 64.0)
-    cp(T.stf[:], T.st1[:, 0:12], ["st1"], ["stf", "stfr"])
+    order_and_send(1, [later[3:5], later[5:6], later[6:8], [lambda: quant("v", 0, 128, T.vb[:], ["vb"], ["vq"])],
+                       [lambda: ts(T.odd[:, 0:4], T.jm[:, 0:4], 2.0, 513.0, A.mult, A.add, ["jm"], ["odd"])], []])
+    send(prv, T.o1l[:], T.ow1[:], "o1", ["ow10", "ow11"])
     act(T.zc[:, 0:1], n1, ["rrb"], ["zc"], -1.0, 256.0)
+    for b in range(2):
+        act(T.q64[:, 64 * b:64 * b + 64], T.t0[:, 1024 + b:1280:4], ["qb"], ["q64%d" % b], 64.0)
+    sfill(T.qi[:, 128:384:2], 128, 0.015625, ["qi"])
+    for b in range(2, 4):
+        act(T.qi[:, 128 * b - 127:128 * b:2], T.t0[:, 1024 + b:1280:4], ["qb"], ["qi%d" % b])
+    cp(T.stf[:], T.st1[:, 0:12], ["st1"], ["stf", "stfr"])
     picked(T.st1, "st1")
     tt(T.stf[:, 8:12], T.stf[:, 8:12], T.kml[:], A.subtract, ["stf", "kml"], ["stf"])
     counts()
@@ -440,7 +442,7 @@ def rank_program(g, core, T, topo):
             mm(mixed[b], [("e64", 128 * b, "l2", 0, 256)], ["e64q%d" % b, "lqa2", "lqb2"], stop=False)
 
     def mean(b):
-        if b == 3:
+        if b >= 2:
             unpack_f([b])
         mm(mixed[b], [("e64", 128 * b, "t2", 0, 256)], ["tq20", "tq21"], start=False)
         act(T.b1p[:, 256 * b:256 * b + 256], bank(mixed[b], 256), ["bank%d" % mixed[b]], ["b1p%d" % b], 0.0078125)
@@ -448,68 +450,89 @@ def rank_program(g, core, T, topo):
     def half_bits(h, first=None):
         a = 128 * h
         hb = T.hb[:, 16 + a:144 + a]
-        ts(hb, bank(4 * h, 128), 0.0, UNIT / 2, A.is_gt, A.mult, ["bank%d" % (4 * h)], ["hb%d" % h])
-        act(T.hz[:, 16 + a:144 + a], hb, ["hb%d" % h], ["hz%d" % h], -1.0, UNIT / 2)
+        ts(hb, bank(4 * h, 128), 0.0, 0.5, A.is_gt, A.mult, ["bank%d" % (4 * h)], ["hb%d" % h])
         if first:
             first()
-        scan(T.rr[:, 1 + a:129 + a], hb, hb, T.rr[:, a:a + 1], A.add, A.add,
-             ["hb%d" % h, "rr0"] + (["rra"] if h else []), ["rrb" if h else "rra"])
+        scan(T.zr[:, 1 + a:129 + a], hb, hb, T.zr[:, a:a + 1], A.add, A.add,
+             ["hb%d" % h, "zr0"] + (["zra"] if h else []), ["zrb" if h else "zra"])
+        ts(T.hz[:, 16 + a:144 + a], hb, -1.0, 0.5, A.mult, A.add, ["hb%d" % h], ["hz%d" % h])
+
+    def intervals():
+        ts(T.pk[:, 0:6:2], T.st2[:, 8:11], -256.0, None, A.add, None, ["st2"], ["pk"])
+        ts(T.pk[:, 6:7], T.st2[:, 11:12], -255.5, None, A.add, None, ["st2"], ["pk3"])
 
     def mid_counts(out, key, h):
         a = 128 * h
         scan(out[:, a:a + 128], T[key][:, 16 + a:144 + a], T[key][:, 15 + a:143 + a],
-             out[:, 127:128] if h else -128 * UNIT, A.add, A.add,
+             out[:, 127:128] if h else -128.0, A.add, A.add,
              [key + "0", key + "1", "y%s0" % key] if h else [key + "0", key + "pad"], ["y%s%d" % (key, h)])
 
-    layer(2, lambda: unpack_f(range(3)))
+    layer(2, lambda: unpack_f(range(2)))
     half_bits(0)
-    mid_counts(T.yo, "hb", 0)
-    half_bits(1, lambda: ts(T.stf[:], T.st2[:, 0:12], UNIT, -128 * UNIT, A.mult, A.add, ["st2"], ["stf", "stfr"]))
+    half_bits(1, intervals)
     for b in range(3):
         mean(b)
-    tt(T.kap[:], T.stf[:, 1:8:2], T.stf[:, 8:12], A.subtract, ["stf"], ["kap"])
-    picked(T.st2, "st2")
-    mid_counts(T.arr, "hz", 0)
-    ts(T.zc[:], T.kap[:], n1, -128 * UNIT, A.add, A.add, ["kap", "rrb"], ["zc"])
+    ts(T.stf[:, 0:8], T.st2[:, 0:8], -256.0, None, A.add, None, ["st2"], ["stf", "stfr"])
+    mid_counts(T.yo, "hb", 0)
+    tt(T.gm[:], T.zr[:, 0:257].indirect(T.st2[:, 0:8]), diag, A.mult, ["zr0", "zra", "zrb", "st2", "diag"], ["gm"])
+    tt(T.pk[:, 1:8:2], T.stf[:, 1:8:2], T.pk[:, 0:8:2], A.subtract, ["stf", "pk", "pk3"], ["kap"])
+    mid_counts(T.yz, "hz", 0)
     counts()
+    mid_counts(T.yz, "hz", 1)
     mid_counts(T.yo, "hb", 1)
-    tt(T.h0[:, 1:8:2], ones_in, T.kap[:], A.is_lt, ["s32", "kap"], ["h0"])
-    tt(T.h1[:, 1:8:2], before_l, T.stf[:, 8:12], A.subtract, ["stf", "s16"], ["h1a"])
-    tt(T.h1[:, 0:8:2], T.zc[:], before_r, A.subtract, ["zc", "s16"], ["h1b"])
-    mid_counts(T.arr, "hz", 1)
-    ts(T.arr[:, 257:512:2], T.yo[:, 1:256:2], n1, 256 * UNIT, A.subtract, A.add, ["yhb0", "yhb1", "rrb"], ["arrb"])
-    scan(T.pos[:, 0:9], T.h0[:, 0:9], T.h1[:, 0:9], 0.0, A.add, A.min, ["h0", "h1a", "h1b", "hend0", "hend1"], ["pos"])
-    ts(T.nd[:, 0:4], T.h0[:, 1:8:2], -UNIT, UNIT, A.mult, A.add, ["h0"], ["nda"])
-    act(T.nd[:, 7:8], T.h0[:, 7:8], ["h0"], ["ndb"], -128 * UNIT, 128 * UNIT)
-    op("s", lambda: S.activation(T.junk[:], T.arr[:, 1:512:2], ACT.Sign, bias=T.pos[:, 8:9], accum_out=T.acc[:, 0:1]),
-       ["yhz0", "yhz1", "arrb", "pos"], ["acc"])
-    act(T.cs[:, 1023:1024], T.acc[:, 0:1], ["acc", "ndb"], ["cs3"], UNIT / 2, T.nd[:, 7:8])
+    tt(T.pos[:, 0:8], T.pk[:], ab, A.subtract, ["kap", "pk", "pk3", "s16"], ["pos"])
+    tt(T.pos[:, 8:12], ones_in, T.pk[:, 1:8:2], A.is_ge, ["s32", "kap"], ["side"])
+    mids = (T.yz[:, 1:256:2], T.yo[:, 1:256:2])
+    midk = (["yhz0", "yhz1"], ["yhb0", "yhb1"])
+
+    def signs(bit):
+        op("s", lambda: S.activation(T.junk[:, 128 * bit:128 * bit + 128], mids[bit], ACT.Sign, scale=2.0 * bit - 1,
+                                     bias=T.pos[:, 6 + bit:7 + bit], accum_out=T.acc[:, bit:bit + 1]),
+           midk[bit] + ["pos"], ["acc%d" % bit])
+
+    def above(c, bit):
+        a = 256 * c + 128 * bit
+        ts(T.cmp[:, a:a + 128], mids[bit], T.pos[:, 2 * c + bit:2 * c + bit + 1], T.pos[:, 8 + c:9 + c] if bit else 1.0,
+           A.add if bit else A.subtract, A.min, midk[bit] + ["pos", "side"][:1 + bit], ["cmp%d%d" % (c, bit)])
+
+    def summed(c, bit):
+        a = 256 * c + 128 * bit
+        scan(T.cs[:, a:a + 128], T.cmp[:, a:a + 128], T.cs[:, a - 128:a] if bit else T.zt[:], 0.0, A.add, A.max,
+             ["cmp%d%d" % (c, bit), "cs%d0" % c if bit else "zt"], ["cs%d%d" % (c, bit)])
+
+    signs(1)
+    act(T.zc[:, 0:1], T.pos[:, 11:12], ["side"], ["zc"], -1.0)
+    act(T.zc[:, 1:2], T.pos[:, 11:12], ["side"], ["zc1"], -128.0, 128.0)
+    signs(0)
+    act(T.acc[:, 2:3], T.acc[:, 1:2], ["acc1", "zc", "zc1"], ["acc2"], T.zc[:, 0:1], T.zc[:, 1:2])
     mean(3)
     for c in range(3):
-        ts(T.cmp[:, 256 * c:256 * c + 128], T.arr[:, 1:256:2], T.pos[:, 2 * c + 1:2 * c + 2], UNIT, A.add, A.min,
-           ["yhz0", "yhz1", "pos"], ["cmp%da" % c])
-        ts(T.cmp[:, 256 * c + 128:256 * c + 256], T.arr[:, 257:512:2], T.pos[:, 2 * c + 1:2 * c + 2], T.nd[:, c:c + 1],
-           A.add, A.min, ["arrb", "pos", "nda"], ["cmp%db" % c])
+        above(c, 0)
+    above(0, 1)
+    above(1, 1)
     for c in range(3):
-        scan(T.cs[:, 256 * c:256 * c + 256], T.cmp[:, 256 * c:256 * c + 256], T.zt[:], 0.0, A.add, A.max,
-             ["cmp%da" % c, "cmp%db" % c, "zt"], ["cs%d" % c])
-    ts(T.j2[:, 0:4], T.cs[:, 255:1024:256], -2 / UNIT, 256.0, A.mult, A.add, ["cs0", "cs1", "cs2", "cs3"], ["j2"])
-    send(back2, T.j2l[:, 0:4], T.j2[:, 0:4], "j2", ["j2"])
+        summed(c, 0)
+    above(2, 1)
+    for c in range(3):
+        summed(c, 1)
+    ts(T.j2[:, 3:4], T.acc[:, 0:1], T.acc[:, 2:3], 128.0, A.min, A.add, ["acc0", "acc2"], ["j23"])
+    ts(T.j2[:, 0:3], T.cs[:, 255:768:256], -2.0, 256.0, A.mult, A.add, ["cs01", "cs11", "cs21"], ["j2"])
+    send(back2, T.j2l[:, 0:4], T.j2[:, 0:4], "j2", ["j2", "j23"])
     for b in (2, 3, 0, 1):
         (cp if b < 2 else act)(T.t2[:, 1024 + b:1280:4], T.b1p[:, 256 * b:256 * b + 256].indirect(T.j2[:, 0:4]),
-                               ["j2", "b1p%d" % b], ["b1%d" % b])
+                               ["j2", "j23", "b1p%d" % b], ["b1%d" % b])
     quant("lb", 64, 192, T.t2[:, 768:1280], ["tq21"] + ["b1%d" % b for b in range(4)], ["b1q"])
     send(back2, u8(T.lb_q[:, 0:64]), u8(T.lb_q[:, 128:192]), "bq", ["b1q"])
     send(back2, T.lb_s[:, 0:64], T.lb_s[:, 128:192], "bq", ["b1q"])
 
-    act(T.orig[:], T.kb[:, obase[0]:obase[0] + 256].indirect(T.o1l[:]), ["ob0", "o1l"], ["orig"])
+    act(T.orig[:], T.ob0[:].indirect(T.o1l[:]), ["ob0", "o1l"], ["orig"])
     unit("e05", 0)
     unit("e05", 1)
-    act(T.arow[:], T.orig[:].indirect(T.j2l[:, 0:4]), ["in_j2", "orig"], ["arow"])
-    tt(T.gm[:, 0:64], T.orig[:].indirect(T.j2l[:, 0:4]), T.kb[:, 768:832], A.mult, ["in_j2", "orig", "diag"], ["gm"])
+    act(T.arow[:], T.orig[:].indirect(T.j2l[:, 0:4]), ["in_j2", "orig"], ["arow"], 256.0, -1.0)
+    tt(T.gm[:, 0:64], T.orig[:].indirect(T.j2l[:, 0:4]), T.kb[:, 256:320], A.mult, ["in_j2", "orig", "diag"], ["gm"])
     unit("e05", 2)
     scan(T.s16[:, 0:64], T.k16[:, 0:64], T.gm[:, 0:64], 0.0, A.mult, A.add, ["k16", "gm"], ["s16"])
-    cp(T.j0[:, 0:4], T.s16[:, 15:64:16], ["s16"], ["j0"])
+    ts(T.j0[:, 0:4], T.s16[:, 15:64:16], 256.0, -1.0, A.mult, A.add, ["s16"], ["j0"])
     unit("e05", 3)
     for b in (2, 3, 0, 1):
         view, picks = T.a0h[:, 64 * b:64 * b + 64], T.tp0[:, 256 * b:256 * b + 256].indirect(T.j0[:, 0:4])
@@ -517,27 +540,31 @@ def rank_program(g, core, T, topo):
             ts(view, picks, 0.5, None, A.mult, None, ["j0", "tp0%d" % b], ["a0h%d" % b])
         else:
             act(view, picks, ["j0", "tp0%d" % b], ["a0h%d" % b], 0.5)
-    quant("v", 0, 128, T.vb[:], ["vb"], ["vq"])
     op("y", lambda: g.sync.dma_start(T.ol[:], T.arow[0:128:16, :]), ["arow"], (), "out")
     for b in range(4):
         mm(b, [("e05", 128 * b, "lb", 0, 128)], ["e05q%d" % b, "b1q", "in_bq"])
     for b in range(4):
-        tt(T.t1[:, 1024 + b:1280:4], bank(b, 64), T.a0h[:, 64 * b:64 * b + 64], A.add,
-           ["bank%d" % b, "a0h%d" % b], ["bt%d" % b])
-    quant("b", 0, 128, T.t1[:, 768:1280], ["tq11"] + ["bt%d" % b for b in range(4)], ["bq"])
-    for b in (0, 2, 1, 3):
+        tt(T.bt[:, 4 + b:512:8], bank(b, 64), T.a0h[:, 64 * b:64 * b + 64], A.add,
+           ["bank%d" % b, "a0h%d" % b, "btz0", "btz"], ["bt%d" % b])
+    quant("b", 0, 128, T.bt[:], ["btz"] + ["bt%d" % b for b in range(4)], ["bq"])
+    for b in range(4):
         mm(4 + b, [("w", 128 * b, "b", 0, 128)], ["wq", "ws", "bq"])
-    for b in (0, 2, 1, 3):
-        tt(T.xp[:, b:256:4], bank(4 + b, 64, 64), T.q64[:, b:256:4], A.add, ["bank%d" % (4 + b), "q64"], ["xp%d" % b])
     for b in range(2):
-        ts(T.f1[:, 1024 + b:1280:2], T.xp[:, b:256:2], 0.015625, None, A.mult, None,
-           ["xp%d" % b, "xp%d" % (b + 2)], ["xt%d" % b])
-    quant("xx", 0, 128, T.f1[:, 768:1280], ["fq11", "xt0", "xt1"], ["xq"])
+        xp = T.xp[:, 64 * b:64 * b + 64]
+        tt(xp, T.ps[:, 512 * (4 + b) + 1:512 * (4 + b) + 128:2], T.q64[:, 64 * b:64 * b + 64], A.add,
+           ["bank%d" % (4 + b), "q64%d" % b], ["xp%d" % b])
+        act(T.f1[:, 4 + b:512:8], xp, ["xp%d" % b, "fq10"], ["xt%d" % b], 0.015625)
+    for b in range(2, 4):
+        scan(T.f1[:, b:512:4], bank(4 + b, 128), T.qi[:, 128 * b - 128:128 * b], 0.0, A.mult, A.add,
+             ["bank%d" % (4 + b), "qi", "qi%d" % b, "fq10"], ["xt%d" % b])
+    quant("xx", 0, 128, T.f1[:, 0:512], ["xt%d" % b for b in range(4)], ["xq"])
     mm(0, [("v", 0, "xx", 0, 128)], ["vq", "xq"])
-    op("y", lambda: g.sync.dma_start(T.oc[:], u8(T.xx_q[:, 64:128])), ["xq"], (), "out")
+    cp(u32(T.xo_q[:]), u32(T.xx_q[:]).indirect(T.odd[:, 0:4]), ["xq", "odd"], ["xoq"])
+    act(T.xo_s[:], T.xx_s[:].indirect(T.odd[:, 0:4]), ["xq", "odd"], ["xos"])
+    op("y", lambda: g.sync.dma_start(T.oc[:], u8(T.xo_q[:])), ["xoq"], (), "out")
     for k in range(4):
-        op("s", lambda: S.dma_start(T.osc[4 * k:4 * k + 4, :], T.xx_s[32 * k:32 * k + 4, 64:128]), ["xq"], (), "out")
-    cp(T.ysb[:], bank(0, 64, 64), ["bank0"], ["ysb"])
+        op("s", lambda: S.dma_start(T.osc[4 * k:4 * k + 4, :], T.xo_s[32 * k:32 * k + 4, :]), ["xos"], (), "out")
+    cp(T.ysb[:], T.ps[:, 1:128:2], ["bank0"], ["ysb"])
     op("y", lambda: g.sync.dma_start(T.y[:], T.ysb[:]), ["ysb"], (), "out")
     for sem in ("cg", "sent", "ct", "cs", "cv", "out"):
         g.wait_ge(T.sem[sem], total[sem])

from concourse.mybir import dt, AluOpType, ActivationFunctionType

X4, U8, BF, F32, U16 = "float8_e4m3fn_x4", "uint8", "bfloat16", "float32", "uint16"
SCRATCH = {"ps": ("psum", [128, 4096], F32)}
for _n, _w in (("u", 128), ("ur", 128), ("t0", 256), ("t1", 256), ("t2", 256), ("f0", 256), ("f1", 256),
               ("l1", 256), ("l2", 256), ("w", 512), ("e64", 512), ("e05", 512), ("z", 128), ("qd", 128),
               ("v", 128), ("lb", 192), ("b", 128), ("xx", 128), ("xo", 64)):
    SCRATCH[_n + "_q"] = ("sbuf", [128, _w], X4)
    SCRATCH[_n + "_s"] = ("sbuf", [128, _w], U8)
for _n, _w in (("ub", 512), ("zb", 512), ("vb", 512), ("t0", 1280), ("t1", 1024), ("t2", 1280), ("tp0", 1024),
               ("tp1", 1024), ("f0", 1024), ("f1", 1024), ("bt", 512), ("qi", 384), ("e64", 520), ("e05", 520), ("c64", 160),
               ("idn", 128), ("q64", 128), ("b1p", 1024), ("a0h", 256), ("xp", 128),
               ("kb", 384), ("k16", 128), ("k32", 128), ("kh", 160),
               ("jrow", 256), ("bit", 256), ("rr", 272), ("zr", 272), ("last", 128), ("drop", 128), ("dg", 32),
               ("h5", 1344), ("b5", 1344), ("ot", 256), ("ob0", 256), ("ob1", 256), ("jfrac", 256), ("grip", 128), ("und", 32),
               ("eb", 96), ("ebt", 160), ("esc", 160), ("gm", 128), ("s16", 128), ("s32", 128), ("orig", 256),
               ("cmp", 768), ("cs", 768), ("junk", 256), ("pos", 16), ("pm", 32), ("hb", 272), ("hz", 272),
               ("yo", 256), ("yz", 256), ("zt", 128), ("pp", 80)):
    SCRATCH[_n] = ("sbuf", [128, _w], BF)
for _n, _w in (("j16", 16), ("crow", 32), ("ccol", 32), ("undo", 16), ("jm", 16), ("lk", 16),
               ("stf", 12), ("kap", 4), ("g0", 24), ("g1", 24), ("gg", 24), ("zc", 4), ("pk", 8),
               ("acc", 4), ("kml", 4), ("arow", 64), ("ysb", 64)):
    SCRATCH[_n] = ("sbuf", [128, _w], F32)
for _n, _w in (("urep", 8), ("esel", 8), ("pw", 16), ("ow0", 16), ("ow1", 16), ("st0", 8), ("so0", 16),
               ("so1", 16), ("st1", 16), ("st2", 16), ("o1l", 16), ("j2", 8), ("j2l", 8), ("j0", 8), ("odd", 8)):
    SCRATCH[_n] = ("sbuf", [128, _w], U16)
SEMAPHORES = ["cv", "cs", "ct", "cg", "sent", "out",
              "ld_u", "ld_xa", "ld_xb", "ld_q", "ld_z", "ld_wc", "ld_ws", "ld_v",
              "a1", "b1", "a2", "b2", "km", "st1", "st2", "o1", "j2", "bq"]
A = AluOpType
ACT = ActivationFunctionType


def rank_program(g, core, T, topo):
    rank = T.rank_of(core)
    if rank is None:
        return
    cores = list(T.cores)
    n = len(cores)
    nxt, prv = cores[(rank + 1) % n], cores[(rank - 1) % n]
    back2, fwd2 = cores[(rank - 2) % n], cores[(rank + 2) % n]
    V, S, P = g.vector, g.scalar, g.tensor
    queues = {"v": V, "s": S, "t": P, "g": g, "y": g.sync}
    counter = {"v": "cv", "s": "cs", "t": "ct", "g": "cg"}
    seen = {k: {} for k in queues}
    total = {}
    writer, readers = {}, {}

    def need(q, tok):
        sem, val, clock = tok[0], tok[1], tok[2]
        if seen[q].get(sem, 0) >= val:
            return
        queues[q].wait_ge(T.sem[sem], val)
        seen[q][sem] = val
        for k in clock:
            if seen[q].get(k, 0) < clock[k]:
                seen[q][k] = clock[k]

    def before(q, r, w):
        toks = [writer[k] for k in list(r) + list(w) if k in writer]
        for k in w:
            toks += readers.get(k, [])
        for k in r:
            if k.startswith("bank"):
                toks += [t for t in readers.get(k, []) if t[3] != q]
        for t in sorted(toks, key=lambda t: -t[1]):
            need(q, t)

    def after(tok, r, w):
        for k in r:
            readers.setdefault(k, []).append(tok)
        for k in w:
            writer[k] = tok
            readers[k] = []

    def op(q, call, r=(), w=(), sem=None):
        before(q, r, w)
        name, inc = (counter[q], 1) if sem is None else (sem, 16)
        call().then_inc(T.sem[name], inc)
        total[name] = total.get(name, 0) + inc
        after((name, total[name], dict(seen[q]), q), r, w)

    def arrives(sem, src, key, writes=1):
        total[sem] = writes * len(topo.engines(src, core))
        writer[key] = (sem, total[sem], {}, "r")

    def send(dst, out, src, sem, r):
        before("g", r, ())
        rid, pid, _ = topo.addr(dst)
        g.remote_dma(out, src, T.sem[sem], T.sem.sent, pid, rid, topo.mask(core, dst))
        total["sent"] = total.get("sent", 0) + len(topo.engines(core, dst))

    def ts(out, in0, s1, s2, o0, o1, r, w):
        if o1 is None:
            op("v", lambda: V.tensor_scalar(out, in0, s1, None, o0), r, w)
        else:
            op("v", lambda: V.tensor_scalar(out, in0, s1, s2, o0, o1), r, w)

    def tt(out, a, b, o, r, w):
        op("v", lambda: V.tensor_tensor(out, a, b, o), r, w)

    def cp(out, a, r, w):
        op("v", lambda: V.tensor_copy(out, a), r, w)

    def scan(out, a, b, init, o0, o1, r, w):
        op("v", lambda: V.tensor_tensor_scan(out, a, b, init, o0, o1), r, w)

    def turn(out, a, r, w):
        op("v", lambda: V.transpose(out, a), r, w)

    def fill(ap, c, w):
        op("v", lambda: V.memset(ap, c), (), w)

    def act(out, a, r, w, scale=1.0, bias=None):
        if bias is not None:
            op("s", lambda: S.activation(out, a, ACT.Identity, bias=bias, scale=scale), r, w)
        elif scale == 1.0:
            op("s", lambda: S.activation(out, a, ACT.Copy), r, w)
        else:
            op("s", lambda: S.activation(out, a, ACT.Copy, scale=scale), r, w)

    def sfill(ap, m, c, w, r=()):
        act(ap, T.c64[:, 0:m], ["c64"] + list(r), w, c / 64.0)

    def quant(name, a, b, src, r, w):
        op("v", lambda: V.quantize_mx(T[name + "_q"][:, a:b], T[name + "_s"][:, a:b], src), r, w)

    def bank(k, m, a=0):
        return T.ps[:, 512 * k + a:512 * k + a + m]

    def mm(k, terms, r, start=True, stop=True):
        before("t", r, ["bank%d" % k] if start else [])
        for i, (ln, la, rn, ra, rb) in enumerate(terms):
            ins = P.matmul_mx(bank(k, rb - ra), T[ln + "_q"][:, la:la + 128], T[ln + "_s"][:, la:la + 128],
                              T[rn + "_q"][:, ra:rb], T[rn + "_s"][:, ra:rb],
                              start and i == 0, stop and i == len(terms) - 1)
        if not stop:
            return
        ins.then_inc(T.sem.ct, 1)
        total["ct"] = total.get("ct", 0) + 1
        after(("ct", total["ct"], dict(seen["t"]), "t"), r, ["bank%d" % k])

    def iota(out, pattern, base, w):
        op("g", lambda: g.iota(out, pattern, base, 0, allow_small_or_imprecise_dtypes=True), (), w)

    u8 = lambda v: v.bitcast(dt.uint8)
    u32 = lambda v: v.bitcast(dt.uint32)

    for lv in (1, 2):
        arrives("a%d" % lv, prv, "lqa%d" % lv, 2)
        arrives("b%d" % lv, prv, "lqb%d" % lv, 2 if topo.chip(prv) == topo.chip(core) else 1)
    for s, k in (("km", "kml"), ("st1", "st1"), ("st2", "st2")):
        arrives(s, prv, k)
    arrives("o1", nxt, "o1l")
    arrives("j2", fwd2, "in_j2")
    arrives("bq", fwd2, "in_bq", 2)

    qb = T.t0[:, 1024:1280]
    op("y", lambda: g.sync.dma_start(T.ub[:], T.u[:]), (), ["ub"], "ld_u")
    op("y", lambda: g.sync.dma_start(T.t0[:, 0:512], T.x[:, 0:512]), (), ["t0a"], "ld_xa")
    op("y", lambda: g.sync.dma_start(T.t0[:, 512:1024], T.x[:, 512:1024]), (), ["t0b"], "ld_xb")
    op("y", lambda: g.sync.dma_start(qb, T.q[:]), (), ["qb"], "ld_q")
    op("y", lambda: g.sync.dma_start(T.zb[:], T.z[:]), (), ["zb"], "ld_z")
    op("y", lambda: g.sync.dma_start(u8(T.w_q[:]), T.wc[:]), ["t0b"], ["wq"], "ld_wc")
    op("y", lambda: g.sync.dma_start(T.w_s[:], T.ws[:]), (), ["ws"], "ld_ws")
    op("y", lambda: g.sync.dma_start(T.vb[:], T.v[:]), (), ["vb"], "ld_v")

    tmod, hold, diag = T.kb[:, 0:128], T.kb[:, 128:256], T.kb[:, 256:384]
    fill(T.c64[:], 64.0, ["c64"])
    fill(T.crow[:], 0.0, ["crow3", "crow4"])
    fill(T.e64[:], 0.0, ["e64"])
    iota(tmod, [[0, 8], [1, 16]], 0, ["tmod"])
    iota(T.j16[:], [[16, 16]], 0, ["j16"])
    iota(T.crow[:, 0:8], [[7, 2], [32, 2], [-64, 2]], 102, ["crow3"])
    iota(T.crow[:, 16:24], [[7, 2], [32, 2], [96, 2]], 22, ["crow4"])
    iota(T.jrow[:], [[1, 256]], 1, ["jrow"])
    op("g", lambda: g.affine_select(T.idn[:], T.c64[:, 0:128], [[-1, 128]], A.is_equal, 0.0, 0, 1), ["c64"], ["idn"])
    sfill(T.kh[:], 160, 0.5, ["kh"])
    STEPS = []
    for name, i, c in (("b5", 0, 0.0), ("b5", 1, -2.0), ("b5", 3, -2.0), ("b5", 4, 0.5), ("h5", 2, 0.0), ("h5", 4, 0.0)):
        STEPS.append("%sc%d" % (name, i))
        sfill(T[name][:, 75 + 16 * i:1344:80], 16, c, STEPS[-1:])
    sfill(T.kh[:, 0:160:16], 10, 0.0, ["kh0"], ["kh"])
    sfill(T.kh[:, 7:160:16], 10, 0.0, ["kh7"], ["kh"])
    sfill(T.dg[:, 0:1], 1, 0.0, ["dg0"])
    sfill(T.rr[:, 0:1], 1, 0.0, ["rr0"])

    def unit(name, b):
        quant(name, 128 * b, 128 * b + 128, T[name][:, 3 - b:515 - b], [name], ["%sq%d" % (name, b)])

    pm = T.pm[:, 0:1]
    turn(T.pm[:], T.kb[:, 0:32], ["tmod"], ["pm"])
    cp(T.urep[:], T.j16[:, 0:8], ["j16"], ["urep"])
    ts(hold, tmod, pm, 512.0, A.is_equal, A.mult, ["tmod", "pm"], ["hold"])
    ts(T.dg[:, 1:17], T.kb[:, 0:16], pm, None, A.is_equal, None, ["tmod", "pm"], ["dg"])
    ts(T.jm[:], T.j16[:], pm, -256.0, A.add, A.add, ["j16", "pm"], ["jm"])
    act(T.dg[:, 18:19], T.dg[:, 16:17], ["dg"], ["shift"], -1.0, 0.5)

    quant("u", 0, 128, T.ub[:], ["ub"], ["uq"])
    tt(T.drop[:, 0:16], T.kb[:, 128:144], T.dg[:, 0:16], A.subtract, ["hold", "dg", "dg0"], ["drop16"])
    turn(T.ccol[:], T.crow[:], ["crow3", "crow4"], ["ccol"])
    act(T.ur_s[:], T.u_s[:].indirect(T.urep[:]), ["uq", "urep"], ["urs"])
    cp(u32(T.ur_q[:]), u32(T.u_q[:]).indirect(T.urep[:]), ["uq", "urep"], ["urq"])
    act(T.drop[:, 16:32], T.drop[:, 0:16], ["drop16"], ["drop32"])
    act(T.last[:], tmod, ["tmod", "shift"], ["last"], 0.0, T.dg[:, 18:19])
    act(T.drop[:, 32:64], T.drop[:, 0:32], ["drop16", "drop32"], ["drop64"])
    sfill(T.eb[:], 96, 0.0, ["eb"])
    act(T.drop[:, 64:128], T.drop[:, 0:64], ["drop16", "drop32", "drop64"], ["drop"])

    def scores(lv, h):
        mm(4 * h, [("ur", 0, "t%d" % lv, 128 * h, 128 * h + 128)], ["urq", "urs", "tq%d%d" % (lv, h)])

    def bits(h):
        ts(T.bit[:, 128 * h:128 * h + 128], bank(4 * h, 128), 0.0, T.dg[:, 18:19], A.is_gt, A.add,
           ["bank%d" % (4 * h), "shift"], ["bit%d" % h])

    def ones_to(h):
        a = 128 * h
        scan(T.rr[:, 1 + a:129 + a], T.bit[:, a:a + 128], T.last[:], T.rr[:, a:a + 1], A.add, A.subtract,
             ["last", "bit%d" % h, "rr0", "rra"] if h else ["last", "bit0", "rr0"], ["rrb" if h else "rra"])

    def held(h):
        scan(T.h5[:, 640 * h:640 * h + 640:5], hold, T.rr[:, 128 * h:128 * h + 128], 0.0, A.add, A.min,
             ["hold", "rr0", "rra"] + (["rrb"] if h else []), ["h5%d" % h])

    def held_bits(h):
        scan(T.b5[:, 640 * h + 32:640 * h + 672:5], T.drop[:], T.bit[:, 128 * h:128 * h + 128], 0.0, A.add, A.min,
             ["drop", "bit%d" % h], ["b5%d" % h])

    def less_zeros():
        for s in (91, 123):
            act(T.h5[:, s:1344:80], T.jm[:], ["jm", "rrb"], ["jz%d" % s], 1.0, T.rr[:, 256:257])

    RR = ["rr0", "rra", "rrb"]
    n1 = T.rr[:, 256:257]

    def order_and_send(lv, spare):
        ob, ow, tp, f = T["ob%d" % lv], T["ow%d" % lv], T["tp%d" % lv], T["f%d" % lv]
        obk, owk = "ob%d" % lv, "ow%d" % lv

        def gap():
            for call in spare.pop(0):
                call()

        held(1)
        gap()
        scan(T.pp[:], T.b5[:, 75:1344:16], T.h5[:, 75:1344:16], 0.0, A.mult, A.add,
             STEPS + ["b50", "b51", "jz91", "jz123", "h50", "h51"], ["pp"])
        gap()
        ts(T.pw[:], T.pp[:, 4:80:5], n1, 256.0, A.subtract, A.add, ["pp", "rrb"], ["pw"])
        gap()
        cp(ob[:].indirect(T.pw[:]), T.jfrac[:], ["pw", "jfrac"], [obk])
        gap()
        for h in range(2):
            scan(T.ot[:, 128 * h:128 * h + 128], T.grip[:], ob[:, 128 * h:128 * h + 128], 0.0, A.mult, A.max,
                 ["grip", obk], ["ot%d" % h])
        gap()
        for h in range(2):
            ts(ow[:, 8 * h:8 * h + 8], T.ot[:, 128 * h + 15:128 * h + 128:16], T.undo[:, 15:16], -1.0, A.mult, A.add,
               ["ot%d" % h, "undo"], [owk + str(h)])
        gap()
        fq, fs, lq, ls = T["f%d_q" % lv], T["f%d_s" % lv], T["l%d_q" % (lv + 1)], T["l%d_s" % (lv + 1)]

        def gather(h, b):
            (cp if b < 2 else act)(f[:, 512 * h + b:512 * h + 512:4],
                                   tp[:, 256 * b:256 * b + 256].indirect(ow[:, 8 * h:8 * h + 8]),
                                   [owk + str(h), "tp%d%d" % (lv, b)], ["f%d%d%d" % (lv, h, b)])

        def pack(h):
            a, sem = 128 * h, "%s%d" % ("ab"[h], lv + 1)
            quant("f%d" % lv, a, a + 128, f[:, 4 * a:4 * a + 512],
                  ["f%d%d%d" % (lv, h, b) for b in range(4)], ["fq%d%d" % (lv, h)])
            near = topo.chip(core) == topo.chip(nxt)
            if h and not near:
                send(nxt, ls[:], fs[:], "a%d" % (lv + 1), ["fq%d0" % lv, "fq%d1" % lv])
            send(nxt, u8(lq[:, a:a + 128]), u8(fq[:, a:a + 128]), sem, ["fq%d%d" % (lv, h)])
            if near:
                send(nxt, ls[:, a:a + 128], fs[:, a:a + 128], sem, ["fq%d%d" % (lv, h)])

        for h, b in ((0, 2), (0, 3), (1, 2), (1, 3), (0, 0), (0, 1), (1, 0)):
            gather(h, b)
        pack(0)
        gather(1, 1)
        pack(1)

    def picked(lst, key):
        tt(T.gm[:], T.rr[:, 0:257].indirect(lst[:, 0:8]), diag, A.mult, RR + [key, "diag"], ["gm"])

    def counts():
        scan(T.s16[:], T.k16[:], T.gm[:], 0.0, A.mult, A.add, ["k16", "gm"], ["s16"])
        scan(T.s32[:], T.k32[:], T.gm[:], 0.0, A.mult, A.add, ["k32", "gm"], ["s32"])

    ab, before_l, before_r, ones_in = T.s16[:, 15:128:16], T.s16[:, 15:128:32], T.s16[:, 31:128:32], T.s32[:, 31:128:32]

    def step(out, okey, first):
        rest = T.lk[:, 4:8] if first else T.kap[:]
        place = T.stf[:, 1:8:2] if first else T.stf[:, 8:12]
        act(T.g1[:, 0:16:2], ab, ["zc", "s16"], ["g12"], 1.0, T.zc[:, 0:1])
        if first:
            act(T.g1[:, 16:24:2], before_r, ["zc", "s16"], ["g13"], 1.0, T.zc[:, 0:1])

        def side(i, view):
            return lambda: tt(view, ones_in, rest, A.is_ge, ["s32", "kap", "lk", "g0z"], ["g0%d" % i])

        ones = [] if first else [
            lambda: tt(T.g1[:, 16:24:2], T.g1[:, 2:16:4], T.kap[:], A.subtract, ["g12", "kap"], ["g13"])]
        return [lambda: tt(T.g1[:, 1:16:2], T.stf[:, 0:8], ab, A.subtract, ["stf", "stfr", "s16"], ["g10"]),
                lambda: tt(T.g1[:, 17:24:2], place, before_l, A.subtract, ["stf", "stfr", "s16"], ["g11"]),
                side(0, T.g0[:, 1:16:4]), side(1, T.g0[:, 3:16:4]), side(2, T.g0[:, 17:24:2])] + ones + [
                lambda: scan(T.gg[:], T.g0[:], T.g1[:], 0.0, A.mult, A.max,
                             ["g0%d" % i for i in range(3)] + ["g1%d" % i for i in range(4)], ["gg"]),
                lambda: cp(out[:, 0:12], T.gg[:, 1:24:2], ["gg"], [okey])]

    def layer(lv, idle=None):
        t, ln = T["t%d" % lv], "l%d" % lv
        turns = ((2, 0, 3, 1), (2, 3, 0, 1))
        for h in range(2):
            for b in turns[h]:
                mm(4 * h + b, [("w", 128 * b, ln, 128 * h, 128 * h + 128), ("e64", 128 * b, ln, 128 * h, 128 * h + 128)],
                   ["wq", "ws", "e64q%d" % b, "lq%s%d" % ("ab"[h], lv)])
        for h in range(2):
            for b in turns[h]:
                view, k = t[:, 512 * h + b:512 * h + 512:4], 4 * h + b
                if b == 1 or (b == 0 and (h or lv == 1)):
                    ts(view, bank(k, 128), 0.015625, None, A.mult, None, ["bank%d" % k], ["t%d%d%d" % (lv, h, b)])
                else:
                    act(view, bank(k, 128), ["bank%d" % k], ["t%d%d%d" % (lv, h, b)], 0.015625)
            quant("t%d" % lv, 128 * h, 128 * h + 128, t[:, 512 * h:512 * h + 512],
                  ["t%d%d%d" % (lv, h, b) for b in range(4)], ["tq%d%d" % (lv, h)])
            scores(lv, h)
            if idle and not h:
                idle()

    def query_scores():
        quant("z", 0, 128, T.zb[:], ["zb"], ["zq"])
        mm(1, [("z", 0, "qd", 0, 128)], ["zq", "qdq"])

    def query_turns():
        turn(T.ebt[:, 0:96], T.eb[:, 0:96], ["eb"], ["ebta"])
        turn(T.ebt[:, 96:160], T.eb[:, 16:80], ["eb"], ["ebtb"])

    def query_numbers():
        scan(T.esc[:], T.kh[:], T.ebt[:], 0.0, A.mult, A.add, ["kh", "kh0", "kh7", "ebta", "ebtb"], ["esc"])
        act(T.lk[:], T.esc[:].indirect(T.esel[:, 0:1]), ["esc", "esel"], ["lk"], -64.0, 128.0)
        send(nxt, T.kml[:], T.lk[:, 4:8], "km", ["lk"])

    for h in range(2):
        quant("t0", 128 * h, 128 * h + 128, T.t0[:, 512 * h:512 * h + 512], ["t0" + "ab"[h]], ["tq0%d" % h])
        scores(0, h)

    def planes(lv, bs):
        for b in bs:
            act(T["tp%d" % lv][:, 256 * b:256 * b + 256], T["t%d" % lv][:, b:1024:4],
                ["t10%d" % b, "t11%d" % b] if lv else ["t0a", "t0b"], ["tp%d%d" % (lv, b)])

    planes(0, [2, 3])

    def later_constants():
        planes(0, [0, 1])
        scan(T.undo[:], T.und[:, 0:16], T.und[:, 16:32], 0.0, A.mult, A.add, ["und0", "und1"], ["undo"])

    def query_bits():
        ts(T.eb[:, 16:80], bank(1, 64, 64), 0.0, None, A.is_gt, None, ["bank1"], ["eb"])

    cp(T.esel[:, 0:1], T.ccol[:, 0:1], ["ccol"], ["esel"])
    quant("qd", 0, 128, T.t0[:, 768:1280], ["qb", "t0b"], ["qdq"])
    bits(0)
    bits(1)
    ones_to(0)
    query_scores()
    held_bits(0)
    ones_to(1)
    less_zeros()
    act(T.jfrac[:], T.jrow[:], ["jrow"], ["jfrac"], 1.0 / 256)
    act(T.grip[:], hold, ["hold"], ["grip"], -0.5, 256.0)
    act(T.und[:, 0:16], T.kb[:, 128:144], ["hold"], ["und0"], -1.0 / 512 / 256, 1.0 / 256)
    act(T.und[:, 16:32], T.kb[:, 128:144], ["hold"], ["und1"], 0.5)
    act(T.e64[:, 3:515:4], T.idn[:], ["idn"], ["e64"])
    held_bits(1)
    held(0)
    order_and_send(0, [[query_bits], [query_turns], [query_numbers], [later_constants], [], []])

    act(T.stf[:, 0:8:2], T.lk[:, 0:4], ["lk"], ["stf"], -1.0, 128.0)
    act(T.stf[:, 1:8:2], T.lk[:, 0:4], ["lk"], ["stfr"], -1.0, 256.0)
    act(diag, hold, ["hold"], ["diag"], 1.0 / 512)
    op("s", lambda: S.activation(T.k32[:], tmod, ACT.Sign), ["tmod"], ["k32"])
    op("s", lambda: S.activation(T.k16[:], tmod, ACT.Sign), ["tmod"], ["k16"])
    sfill(T.k32[:, 16:128:32], 4, -1.0, ["k32"])
    sfill(T.g0[:], 24, 0.0, ["g0z"])
    sfill(T.zr[:, 0:1], 1, -128.0, ["zr0"])
    sfill(T.zt[:], 128, 0.0, ["zt"])
    for name in ("hb", "hz"):
        sfill(T[name][:, 15:16], 1, 0.0, [name + "pad"])
    for b in (2, 0, 3):
        unit("e64", b)
    cp(T.st0[:], T.stf[:, 0:8], ["stf", "stfr"], ["st0"])
    unit("e64", 1)
    act(T.zc[:, 0:1], n1, ["rrb"], ["zc"], -1.0, 256.0)
    picked(T.st0, "st0")
    fill(T.bt[:, 0:256], 0.0, ["btz0"])
    counts()
    fill(T.bt[:, 256:512], 0.0, ["btz"])

    layer(1)
    later = step(T.so0, "so0", True)
    later.append(lambda: send(nxt, T.st1[:, 0:12], T.so0[:, 0:12], "st1", ["so0"]))
    planes(1, range(3))
    bits(0)
    for call in later[0:3]:
        call()
    ones_to(0)
    bits(1)
    held_bits(0)
    held(0)
    ones_to(1)
    less_zeros()
    planes(1, [3])
    act(T.e05[:], T.e64[:], ["e64"], ["e05"], 0.0078125)
    held_bits(1)
    order_and_send(1, [later[3:5], later[5:6], later[6:8], [lambda: quant("v", 0, 128, T.vb[:], ["vb"], ["vq"])],
                       [lambda: ts(T.odd[:, 0:4], T.jm[:, 0:4], 2.0, 513.0, A.mult, A.add, ["jm"], ["odd"])], []])
    send(prv, T.o1l[:], T.ow1[:], "o1", ["ow10", "ow11"])
    act(T.zc[:, 0:1], n1, ["rrb"], ["zc"], -1.0, 256.0)
    for b in range(2):
        act(T.q64[:, 64 * b:64 * b + 64], T.t0[:, 1024 + b:1280:4], ["qb"], ["q64%d" % b], 64.0)
    sfill(T.qi[:, 128:384:2], 128, 0.015625, ["qi"])
    for b in range(2, 4):
        act(T.qi[:, 128 * b - 127:128 * b:2], T.t0[:, 1024 + b:1280:4], ["qb"], ["qi%d" % b])
    cp(T.stf[:], T.st1[:, 0:12], ["st1"], ["stf", "stfr"])
    picked(T.st1, "st1")
    tt(T.stf[:, 8:12], T.stf[:, 8:12], T.kml[:], A.subtract, ["stf", "kml"], ["stf"])
    counts()
    tt(T.kap[:], T.stf[:, 1:8:2], T.stf[:, 8:12], A.subtract, ["stf"], ["kap"])
    for call in step(T.so1, "so1", False):
        call()
    send(nxt, T.st2[:, 0:12], T.so1[:, 0:12], "st2", ["so1"])

    mixed = (1, 2, 3, 5)

    def unpack_f(bs):
        for b in bs:
            mm(mixed[b], [("e64", 128 * b, "l2", 0, 256)], ["e64q%d" % b, "lqa2", "lqb2"], stop=False)

    def mean(b):
        if b >= 2:
            unpack_f([b])
        mm(mixed[b], [("e64", 128 * b, "t2", 0, 256)], ["tq20", "tq21"], start=False)
        act(T.b1p[:, 256 * b:256 * b + 256], bank(mixed[b], 256), ["bank%d" % mixed[b]], ["b1p%d" % b], 0.0078125)

    def half_bits(h, first=None):
        a = 128 * h
        hb = T.hb[:, 16 + a:144 + a]
        ts(hb, bank(4 * h, 128), 0.0, 0.5, A.is_gt, A.mult, ["bank%d" % (4 * h)], ["hb%d" % h])
        if first:
            first()
        scan(T.zr[:, 1 + a:129 + a], hb, hb, T.zr[:, a:a + 1], A.add, A.add,
             ["hb%d" % h, "zr0"] + (["zra"] if h else []), ["zrb" if h else "zra"])
        ts(T.hz[:, 16 + a:144 + a], hb, -1.0, 0.5, A.mult, A.add, ["hb%d" % h], ["hz%d" % h])

    def intervals():
        ts(T.pk[:, 0:6:2], T.st2[:, 8:11], -256.0, None, A.add, None, ["st2"], ["pk"])
        ts(T.pk[:, 6:7], T.st2[:, 11:12], -255.5, None, A.add, None, ["st2"], ["pk3"])

    def mid_counts(out, key, h):
        a = 128 * h
        scan(out[:, a:a + 128], T[key][:, 16 + a:144 + a], T[key][:, 15 + a:143 + a],
             out[:, 127:128] if h else -128.0, A.add, A.add,
             [key + "0", key + "1", "y%s0" % key] if h else [key + "0", key + "pad"], ["y%s%d" % (key, h)])

    layer(2, lambda: unpack_f(range(2)))
    half_bits(0)
    half_bits(1, intervals)
    for b in range(3):
        mean(b)
    ts(T.stf[:, 0:8], T.st2[:, 0:8], -256.0, None, A.add, None, ["st2"], ["stf", "stfr"])
    mid_counts(T.yo, "hb", 0)
    tt(T.gm[:], T.zr[:, 0:257].indirect(T.st2[:, 0:8]), diag, A.mult, ["zr0", "zra", "zrb", "st2", "diag"], ["gm"])
    tt(T.pk[:, 1:8:2], T.stf[:, 1:8:2], T.pk[:, 0:8:2], A.subtract, ["stf", "pk", "pk3"], ["kap"])
    mid_counts(T.yz, "hz", 0)
    counts()
    mid_counts(T.yz, "hz", 1)
    mid_counts(T.yo, "hb", 1)
    tt(T.pos[:, 0:8], T.pk[:], ab, A.subtract, ["kap", "pk", "pk3", "s16"], ["pos"])
    tt(T.pos[:, 8:12], ones_in, T.pk[:, 1:8:2], A.is_ge, ["s32", "kap"], ["side"])
    mids = (T.yz[:, 1:256:2], T.yo[:, 1:256:2])
    midk = (["yhz0", "yhz1"], ["yhb0", "yhb1"])

    def signs(bit):
        op("s", lambda: S.activation(T.junk[:, 128 * bit:128 * bit + 128], mids[bit], ACT.Sign, scale=2.0 * bit - 1,
                                     bias=T.pos[:, 6 + bit:7 + bit], accum_out=T.acc[:, bit:bit + 1]),
           midk[bit] + ["pos"], ["acc%d" % bit])

    def above(c, bit):
        a = 256 * c + 128 * bit
        ts(T.cmp[:, a:a + 128], mids[bit], T.pos[:, 2 * c + bit:2 * c + bit + 1], T.pos[:, 8 + c:9 + c] if bit else 1.0,
           A.add if bit else A.subtract, A.min, midk[bit] + ["pos", "side"][:1 + bit], ["cmp%d%d" % (c, bit)])

    def summed(c, bit):
        a = 256 * c + 128 * bit
        scan(T.cs[:, a:a + 128], T.cmp[:, a:a + 128], T.cs[:, a - 128:a] if bit else T.zt[:], 0.0, A.add, A.max,
             ["cmp%d%d" % (c, bit), "cs%d0" % c if bit else "zt"], ["cs%d%d" % (c, bit)])

    signs(1)
    act(T.zc[:, 0:1], T.pos[:, 11:12], ["side"], ["zc"], -1.0)
    act(T.zc[:, 1:2], T.pos[:, 11:12], ["side"], ["zc1"], -128.0, 128.0)
    signs(0)
    act(T.acc[:, 2:3], T.acc[:, 1:2], ["acc1", "zc", "zc1"], ["acc2"], T.zc[:, 0:1], T.zc[:, 1:2])
    mean(3)
    for c in range(3):
        above(c, 0)
    above(0, 1)
    above(1, 1)
    for c in range(3):
        summed(c, 0)
    above(2, 1)
    for c in range(3):
        summed(c, 1)
    ts(T.j2[:, 3:4], T.acc[:, 0:1], T.acc[:, 2:3], 128.0, A.min, A.add, ["acc0", "acc2"], ["j23"])
    ts(T.j2[:, 0:3], T.cs[:, 255:768:256], -2.0, 256.0, A.mult, A.add, ["cs01", "cs11", "cs21"], ["j2"])
    send(back2, T.j2l[:, 0:4], T.j2[:, 0:4], "j2", ["j2", "j23"])
    for b in (2, 3, 0, 1):
        (cp if b < 2 else act)(T.t2[:, 1024 + b:1280:4], T.b1p[:, 256 * b:256 * b + 256].indirect(T.j2[:, 0:4]),
                               ["j2", "j23", "b1p%d" % b], ["b1%d" % b])
    quant("lb", 64, 192, T.t2[:, 768:1280], ["tq21"] + ["b1%d" % b for b in range(4)], ["b1q"])
    send(back2, u8(T.lb_q[:, 0:64]), u8(T.lb_q[:, 128:192]), "bq", ["b1q"])
    send(back2, T.lb_s[:, 0:64], T.lb_s[:, 128:192], "bq", ["b1q"])

    act(T.orig[:], T.ob0[:].indirect(T.o1l[:]), ["ob0", "o1l"], ["orig"])
    unit("e05", 0)
    unit("e05", 1)
    act(T.arow[:], T.orig[:].indirect(T.j2l[:, 0:4]), ["in_j2", "orig"], ["arow"], 256.0, -1.0)
    tt(T.gm[:, 0:64], T.orig[:].indirect(T.j2l[:, 0:4]), T.kb[:, 256:320], A.mult, ["in_j2", "orig", "diag"], ["gm"])
    unit("e05", 2)
    scan(T.s16[:, 0:64], T.k16[:, 0:64], T.gm[:, 0:64], 0.0, A.mult, A.add, ["k16", "gm"], ["s16"])
    ts(T.j0[:, 0:4], T.s16[:, 15:64:16], 256.0, -1.0, A.mult, A.add, ["s16"], ["j0"])
    unit("e05", 3)
    for b in (2, 3, 0, 1):
        view, picks = T.a0h[:, 64 * b:64 * b + 64], T.tp0[:, 256 * b:256 * b + 256].indirect(T.j0[:, 0:4])
        if b < 2:
            ts(view, picks, 0.5, None, A.mult, None, ["j0", "tp0%d" % b], ["a0h%d" % b])
        else:
            act(view, picks, ["j0", "tp0%d" % b], ["a0h%d" % b], 0.5)
    op("y", lambda: g.sync.dma_start(T.ol[:], T.arow[0:128:16, :]), ["arow"], (), "out")
    for b in range(4):
        mm(b, [("e05", 128 * b, "lb", 0, 128)], ["e05q%d" % b, "b1q", "in_bq"])
    for b in range(4):
        tt(T.bt[:, 4 + b:512:8], bank(b, 64), T.a0h[:, 64 * b:64 * b + 64], A.add,
           ["bank%d" % b, "a0h%d" % b, "btz0", "btz"], ["bt%d" % b])
    quant("b", 0, 128, T.bt[:], ["btz"] + ["bt%d" % b for b in range(4)], ["bq"])
    for b in range(4):
        mm(4 + b, [("w", 128 * b, "b", 0, 128)], ["wq", "ws", "bq"])
    for b in range(2):
        xp = T.xp[:, 64 * b:64 * b + 64]
        tt(xp, T.ps[:, 512 * (4 + b) + 1:512 * (4 + b) + 128:2], T.q64[:, 64 * b:64 * b + 64], A.add,
           ["bank%d" % (4 + b), "q64%d" % b], ["xp%d" % b])
        act(T.f1[:, 4 + b:512:8], xp, ["xp%d" % b, "fq10"], ["xt%d" % b], 0.015625)
    for b in range(2, 4):
        scan(T.f1[:, b:512:4], bank(4 + b, 128), T.qi[:, 128 * b - 128:128 * b], 0.0, A.mult, A.add,
             ["bank%d" % (4 + b), "qi", "qi%d" % b, "fq10"], ["xt%d" % b])
    quant("xx", 0, 128, T.f1[:, 0:512], ["xt%d" % b for b in range(4)], ["xq"])
    mm(0, [("v", 0, "xx", 0, 128)], ["vq", "xq"])
    cp(u32(T.xo_q[:]), u32(T.xx_q[:]).indirect(T.odd[:, 0:4]), ["xq", "odd"], ["xoq"])
    act(T.xo_s[:], T.xx_s[:].indirect(T.odd[:, 0:4]), ["xq", "odd"], ["xos"])
    op("y", lambda: g.sync.dma_start(T.oc[:], u8(T.xo_q[:])), ["xoq"], (), "out")
    for k in range(4):
        op("s", lambda: S.dma_start(T.osc[4 * k:4 * k + 4, :], T.xo_s[32 * k:32 * k + 4, :]), ["xos"], (), "out")
    cp(T.ysb[:], T.ps[:, 1:128:2], ["bank0"], ["ysb"])
    op("y", lambda: g.sync.dma_start(T.y[:], T.ysb[:]), ["ysb"], (), "out")
    for sem in ("cg", "sent", "ct", "cs", "cv", "out"):
        g.wait_ge(T.sem[sem], total[sem])
